import numpy as np
import ml_dtypes


def mxq(x, axis, fmt="e4m3"):
    dtype, down = {"e4m3": (ml_dtypes.float8_e4m3fn, 7), "e5m2": (ml_dtypes.float8_e5m2, 14)}[fmt]
    v = np.moveaxis(np.asarray(x, np.float32).astype(ml_dtypes.bfloat16).astype(np.float64), axis, -1)
    blocks = v.reshape(v.shape[:-1] + (-1, 32))
    amax = np.abs(blocks).max(-1, keepdims=True)
    byte = np.maximum(np.where(amax > 0, np.frexp(amax)[1] - 1 + 127, 0) - down, 1)
    scale = np.exp2(byte - 127.0)
    codes = (blocks / scale).astype(np.float32).astype(dtype).astype(np.float64)
    return np.moveaxis((codes * scale).reshape(v.shape), -1, axis)


WIDE = False


def mx_kscale(k):
    if not WIDE:
        return np.ones(k)
    levels = np.array([24, -24, 12, -12, 0])
    if k % 512:
        return np.exp2(np.random.permutation(np.resize(levels, k // 32))).repeat(32)
    a = np.empty((k // 512, 16))
    for p in range(k // 512):
        a[p, :8] = np.random.permutation(np.resize(levels, 8))
        for g in range(8):
            far = levels[np.abs(levels - a[p, g]) >= 10]
            a[p, g + 8] = far[np.random.randint(len(far))]
    return np.exp2(a.ravel()).repeat(32)


def f64(x):
    return np.asarray(x).astype(np.float64)


def striped(idx):
    return np.tile(idx.reshape(-1, 16).T, (8, 1)).astype(np.uint16)


def unstriped(offs):
    return offs[:16].T.reshape(-1).astype(np.int64)


def striped8(idx):
    return np.concatenate([v.reshape(-1, 16).T for v in idx]).astype(np.uint16)


def unstriped8(offs):
    return np.stack([offs[16 * g:16 * g + 16].T.reshape(-1) for g in range(8)]).astype(np.int64)


E2M1 = np.array([0.0, 0.5, 1.0, 1.5, 2.0, 3.0, 4.0, 6.0, -0.0, -0.5, -1.0, -1.5, -2.0, -3.0, -4.0, -6.0])


def pack_weight(w, fmt):
    k, n = w.shape
    w = f64(np.asarray(w, np.float32).astype(ml_dtypes.bfloat16)).reshape(k // 32, 32, n)
    amax = np.abs(w).max(1)
    if fmt == "e4m3":
        byte = np.frexp(amax)[1] - 1 + 127 - 7
    else:
        mant, ex = np.frexp(amax / 6.0)
        byte = np.where(mant > 0.5, ex, ex - 1) + 127
    byte = np.clip(np.where(amax > 0, byte, 1), 1, 254)
    scaled = (w * np.exp2(127.0 - byte)[:, None, :]).reshape(k, n).astype(np.float32)
    by_word = np.ascontiguousarray(scaled.reshape(k // 512, 128, 4, n).transpose(0, 1, 3, 2))
    if fmt == "e4m3":
        words = by_word.astype(ml_dtypes.float8_e4m3fn).view(np.uint8)
    else:
        c = by_word.astype(ml_dtypes.float4_e2m1fn).view(np.uint8) & 0xF
        words = (c[..., 0::2] | (c[..., 1::2] << 4)).reshape(k // 512, 128, 2 * n)
    return np.ascontiguousarray(words), np.ascontiguousarray(byte.astype(np.uint8).reshape(k // 512, 16, n))


def unpack_weight(words, scales, fmt):
    g, _, n = scales.shape
    words = np.ascontiguousarray(words).reshape(g, 128, n, -1)
    if fmt == "e4m3":
        vals = words.view(ml_dtypes.float8_e4m3fn).astype(np.float64)
    else:
        nib = np.empty((g, 128, n, 4), np.uint8)
        nib[..., 0::2] = words & 0xF
        nib[..., 1::2] = words >> 4
        vals = E2M1[nib]
    vals = vals * np.repeat(np.exp2(scales.astype(np.float64) - 127.0), 8, axis=1)[..., None]
    return vals.transpose(0, 1, 3, 2).reshape(g * 512, n)


def pack_table4(v):
    words, scales = pack_weight(v, "e2m1")
    g, t = words.shape[0] // 2, v.shape[1]
    return np.ascontiguousarray(words.reshape(g, 2, 128, t, 2).transpose(0, 2, 3, 1, 4).reshape(g, 128, t, 4)), scales


def unpack_table4(words, scales):
    g, _, t, _ = words.shape
    return unpack_weight(words.reshape(g, 128, t, 2, 2).transpose(0, 3, 1, 2, 4).reshape(2 * g, 128, 2 * t), scales, "e2m1")


def silu(f):
    return f / (1.0 + np.exp(-np.maximum(f, -700.0)))


K, L, R, N, T, J = 512, 1024, 512, 512, 2048, 1024


def setup_inputs():
    n = np.random.standard_normal
    s = mx_kscale(K)[:, None]
    s2 = mx_kscale(L)[:, None]
    u = mx_kscale(R)[:, None]
    p_tab = pack_table4(n((L, T)) * s2)
    p_wa = pack_weight(n((K, R)) / np.sqrt(K) / s, "e2m1")
    p_wb = pack_weight(n((L, R)) / np.sqrt(L) / s2 * u.T, "e2m1")
    return {
        "tab_words": p_tab[0],
        "tab_scales": p_tab[1],
        "xT": (n((K, T)) * s).astype(np.float32),
        "wgt2": np.repeat(np.random.uniform(0.5, 2.0, (8, J)), 16, axis=0).astype(np.float32),
        "wa_words": p_wa[0],
        "wa_scales": p_wa[1],
        "wb_words": p_wb[0],
        "wb_scales": p_wb[1],
        "wd": (n((R, N)) / np.sqrt(R) / u).astype(np.float32),
        "offs": striped(np.random.permutation(T)[:J]),
        "offs2": striped8(np.stack([np.random.permutation(T)[:J] for _ in range(8)])),
    }


def reference(tab_words, tab_scales, xT, wgt2, wa_words, wa_scales, wb_words, wb_scales, wd, offs, offs2):
    idx = unstriped(offs)
    idx2 = unstriped8(offs2)
    tab_ = unpack_table4(tab_words, tab_scales)[:, idx]
    rows = np.arange(K)
    xg = f64(wgt2)[rows // 4 % 128] * f64(xT)[rows[:, None], idx2[rows % 512 // 64]]
    xT_ = mxq(xg, 0, "e4m3")
    wa_ = unpack_weight(wa_words, wa_scales, "e2m1")
    wb_ = unpack_weight(wb_words, wb_scales, "e2m1")
    ya = wa_.T @ xT_
    yb = wb_.T @ tab_
    h = silu(ya) * yb
    h_ = mxq(h, 0, "e4m3")
    wd_ = mxq(f64(wd), 0, "e4m3")
    y = wd_.T @ h_
    return y

@@ -1,0 +1,243 @@
+from contextlib import ExitStack
+
+import concourse.mybir as mybir
+
+K, L, R, N, T, J = 512, 1024, 512, 512, 2048, 1024
+FLOPS = 2 * J * (K * R + L * R + R * N)
+
+F32 = mybir.dt.float32
+BF16 = mybir.dt.bfloat16
+I32 = mybir.dt.int32
+U32 = mybir.dt.uint32
+U16 = mybir.dt.uint16
+U8 = mybir.dt.uint8
+FP8X4 = mybir.dt.float8_e4m3fn_x4
+FP4X4 = mybir.dt.float4_e2m1fn_x4
+MULT = mybir.AluOpType.mult
+SILU = mybir.ActivationFunctionType.Silu
+
+P = 128
+PACK = 4
+GROUP = 16
+XC = 256
+TC = 512
+HC = 128
+SPANS = ((0, 512), (512, 768), (768, 1024))
+EARLY = 4
+
+
+def tile_list_htabg_glu_none_kernel(
+    tc, tab_words, tab_scales, xT, wgt2, wa_words, wa_scales, wb_words, wb_scales, wd, offs, offs2, out
+):
+    nc = tc.nc
+    with ExitStack() as ctx:
+        keep = ctx.enter_context(tc.tile_pool(name="keep", bufs=1))
+        ring = ctx.enter_context(tc.tile_pool(name="ring", bufs=3))
+        psum_a = ctx.enter_context(tc.psum_pool(name="psum_a", bufs=2))
+        psum_b = ctx.enter_context(tc.psum_pool(name="psum_b", bufs=4))
+        psum_y = ctx.enter_context(tc.psum_pool(name="psum_y", bufs=2))
+
+        lst = keep.tile([P, J // GROUP], U16, name="lst")
+        lst2 = keep.tile([P, J // GROUP], U16, name="lst2")
+        tab_s = keep.tile([P, T], U8, name="tab_s", align_bytes=64)
+        tab_w = keep.tile([P, T], I32, name="tab_w", align_bytes=64)
+        wgt = [keep.tile([P, b - a], F32, name="wgt%d" % a, align_bytes=64) for a, b in SPANS]
+        got_x = [keep.tile([P, PACK, b - a], F32, name="got_x%d" % a, align_bytes=64) for a, b in SPANS]
+        x_pl = [keep.tile([P, T], F32, name="x_pl%d" % i, align_bytes=64) for i in range(PACK)]
+        wd_raw = keep.tile([P, PACK, N], F32, name="wd_raw", align_bytes=64)
+        w_raw = [keep.tile([P, n, 2 * R], U8, name="w_raw%d" % n, align_bytes=64) for n in (1, 2)]
+        ws_raw = [keep.tile([P, n, R], U8, name="ws_raw%d" % n, align_bytes=64) for n in (1, 2)]
+        w_cod = [keep.tile([P, n, 2 * R], U8, name="w_cod%d" % n, align_bytes=64) for n in (1, 2)]
+        w_scl = [keep.tile([P, n, R], U8, name="w_scl%d" % n, align_bytes=64) for n in (1, 2)]
+        got_s = keep.tile([P, J], U8, name="got_s", align_bytes=64)
+        v_scl = [keep.tile([P, J], U8, name="v_scl%d" % a, align_bytes=64) for a in range(2)]
+        warm = keep.tile([P, 8], F32, name="warm")
+        warm_out = keep.tile([P, 8], F32, name="warm_out")
+
+        nc.vector.memset(ws_raw[1][:].rearrange("p a r -> p (a r)").bitcast(I32), 0)
+        nc.vector.memset(ws_raw[0][:].rearrange("p a r -> p (a r)").bitcast(I32), 0)
+        nc.vector.memset(warm[:], 0.0)
+        for q in range(4):
+            nc.vector.memset(tab_s[32 * q : 32 * q + 24, :].bitcast(I32), 0)
+        for a in range(2):
+            nc.vector.memset(v_scl[a][96:128, :].bitcast(I32), 0)
+        nc.scalar.activation(warm_out[:], warm[:], SILU)
+
+        x_rows = xT.rearrange("(p i) t -> i p t", i=PACK)
+        wd_rows = wd.rearrange("(b t q) n -> t b q n", t=PACK, q=8)
+        nc.sync.dma_start(lst[:], offs)
+        for q in range(4):
+            nc.sync.dma_start(
+                tab_s[32 * q + 24 : 32 * q + 32, :].bitcast(I32), tab_scales[:, 4 * q : 4 * q + 4, :].bitcast(I32)
+            )
+        nc.sync.dma_start(tab_w[:], tab_words[0].rearrange("p t b -> p (t b)").bitcast(I32))
+        nc.sync.dma_start(w_raw[1][:].bitcast(I32), wb_words.rearrange("a p c -> p a c").bitcast(I32))
+        for q in range(4):
+            nc.sync.dma_start(
+                ws_raw[1][32 * q : 32 * q + 4, :, :].bitcast(I32),
+                wb_scales[:, 4 * q : 4 * q + 4, :].rearrange("a q r -> q a r").bitcast(I32),
+            )
+        nc.sync.dma_start(lst2[:], offs2)
+        nc.sync.dma_start(wgt[0][:], wgt2[:, SPANS[0][0] : SPANS[0][1]])
+        for i in range(2):
+            nc.sync.dma_start(x_pl[i][:], x_rows[i])
+        nc.sync.dma_start(w_raw[0][:, 0, :].bitcast(I32), wa_words[0].bitcast(I32))
+        for q in range(4):
+            nc.sync.dma_start(
+                ws_raw[0][32 * q : 32 * q + 4, 0, :].bitcast(I32), wa_scales[0, 4 * q : 4 * q + 4, :].bitcast(I32)
+            )
+        for i in range(2, PACK):
+            nc.sync.dma_start(x_pl[i][:], x_rows[i])
+        for u in (1, 2):
+            for t in (2 * u - 2, 2 * u - 1):
+                nc.sync.dma_start(wd_raw[:, t, :], wd_rows[t])
+            nc.sync.dma_start(wgt[u][:], wgt2[:, SPANS[u][0] : SPANS[u][1]])
+
+        x_bf = [keep.tile([P, XC * PACK], BF16, name="x_bf%d" % c, align_bytes=64) for c in range(J // XC)]
+        x_cod = [keep.tile([P, XC], U32, name="x_cod%d" % c, align_bytes=64) for c in range(J // XC)]
+        x_scl = [keep.tile([P, XC], U8, name="x_scl%d" % c, align_bytes=64) for c in range(J // XC)]
+        got_w = [keep.tile([P, TC], U32, name="got_w%d" % c, align_bytes=64) for c in range(J // TC)]
+        v_cod = [keep.tile([P, 4 * TC], U8, name="v_cod%d" % c, align_bytes=64) for c in range(J // TC)]
+        gate = [keep.tile([P, HC * PACK], F32, name="gate%d" % s, align_bytes=64) for s in range(J // HC)]
+        lin = [keep.tile([P, HC * PACK], F32, name="lin%d" % s, align_bytes=64) for s in range(EARLY)]
+        wd_bf = keep.tile([P, N * PACK], BF16, name="wd_bf", align_bytes=64)
+        wd_cod = keep.tile([P, N], U32, name="wd_cod", align_bytes=64)
+        wd_scl = keep.tile([P, N], U8, name="wd_scl", align_bytes=64)
+        out_rows = out.rearrange("(m p) j -> p m j", p=P)
+
+        nc.vector.tensor_copy(got_s[:], tab_s[:].indirect(lst[:]))
+        for a in range(2):
+            nc.gpsimd.dma_start(v_scl[a][0:100, :].bitcast(I32), got_s[24 + 4 * a : 124 + 4 * a, :].bitcast(I32))
+        for c in range(J // TC):
+            entries = lst[:, c * TC // GROUP : (c + 1) * TC // GROUP]
+            nc.vector.tensor_copy(got_w[c][:], tab_w[:].bitcast(U32).indirect(entries))
+        for c in range(J // TC):
+            nc.vector.tensor_copy(
+                v_cod[c][:].bitcast(U16).rearrange("p (d j) -> p d j", d=2),
+                got_w[c][:].bitcast(U16).rearrange("p (j d) -> p d j", d=2),
+            )
+
+        def order_columns(n):
+            nc.vector.tensor_copy(
+                w_cod[n][:].bitcast(I32).rearrange("p a (t b w) -> p a t b w", t=PACK, w=4),
+                w_raw[n][:].bitcast(I32).rearrange("p a (b t w) -> p a t b w", t=PACK, w=4),
+            )
+            nc.vector.tensor_copy(
+                w_scl[n][:].bitcast(I32).rearrange("p a (t b w) -> p a t b w", t=PACK, w=2),
+                ws_raw[n][:].bitcast(I32).rearrange("p a (b t w) -> p a t b w", t=PACK, w=2),
+            )
+
+        order_columns(1)
+        order_columns(0)
+        yb = {}
+
+        def table_product(s):
+            j0 = s * HC
+            vc, vo = divmod(j0, TC)
+            bank = psum_b.tile([P, PACK, HC], F32, name="bank")
+            for t in range(PACK):
+                for a in range(2):
+                    nc.tensor.matmul_mx(
+                        out=bank[:, t, :],
+                        lhsT=w_cod[1][:, a, 2 * P * t : 2 * P * (t + 1)].bitcast(FP4X4),
+                        lhsT_scale=w_scl[1][:, a, P * t : P * (t + 1)],
+                        rhs=v_cod[vc][:, 2 * (a * TC + vo) : 2 * (a * TC + vo + HC)].bitcast(FP4X4),
+                        rhs_scale=v_scl[a][:, j0 : j0 + HC],
+                        start=(a == 0),
+                        stop=(a == 1),
+                    )
+            yb[s] = bank[:].rearrange("p t j -> p j t")
+            if s < EARLY:
+                staged = lin[s][:].rearrange("p (j t) -> p j t", t=PACK)
+                nc.scalar.copy(staged, yb[s])
+                yb[s] = staged
+
+        for s in range(J // HC):
+            table_product(s)
+
+        def gather_x(u, i, j0, j1):
+            a = SPANS[u][0]
+            entries = lst2[:, j0 // GROUP : j1 // GROUP]
+            nc.vector.tensor_tensor(
+                got_x[u][:, i, j0 - a : j1 - a], x_pl[i][:].indirect(entries), wgt[u][:, j0 - a : j1 - a], MULT
+            )
+
+        def round_x(u, c):
+            a = c * XC - SPANS[u][0]
+            nc.scalar.copy(
+                x_bf[c][:].rearrange("p (c i t) -> p c t i", i=2, t=PACK),
+                got_x[u][:, :, a : a + XC].rearrange("p t (c i) -> p c t i", i=2),
+            )
+
+        def head_product(c):
+            nc.vector.quantize_mx(out=x_cod[c][:].bitcast(FP8X4), scales=x_scl[c][:], in_=x_bf[c][:])
+            for xo in range(0, XC, HC):
+                s = (c * XC + xo) // HC
+                ya = psum_a.tile([P, PACK, HC], F32, name="ya")
+                for t in range(PACK):
+                    nc.tensor.matmul_mx(
+                        out=ya[:, t, :],
+                        lhsT=w_cod[0][:, 0, 2 * P * t : 2 * P * (t + 1)].bitcast(FP4X4),
+                        lhsT_scale=w_scl[0][:, 0, P * t : P * (t + 1)],
+                        rhs=x_cod[c][:, xo : xo + HC].bitcast(FP8X4),
+                        rhs_scale=x_scl[c][:, xo : xo + HC],
+                        start=True,
+                        stop=True,
+                    )
+                nc.scalar.activation(
+                    gate[s][:].rearrange("p (j t) -> p j t", t=PACK), ya[:].rearrange("p t j -> p j t"), SILU
+                )
+
+        h_bf = {}
+
+        def join(s):
+            h_bf[s] = ring.tile([P, HC * PACK], BF16, name="h_bf", align_bytes=64)
+            nc.vector.tensor_tensor(
+                h_bf[s][:].rearrange("p (j t) -> p j t", t=PACK),
+                yb[s],
+                gate[s][:].rearrange("p (j t) -> p j t", t=PACK),
+                MULT,
+            )
+
+        def second_layer(s):
+            h_cod = ring.tile([P, HC], U32, name="h_cod", align_bytes=64)
+            h_scl = ring.tile([P, HC], U8, name="h_scl", align_bytes=64)
+            nc.vector.quantize_mx(out=h_cod[:].bitcast(FP8X4), scales=h_scl[:], in_=h_bf[s][:])
+            y = psum_y.tile([P, N // P, HC], F32, name="y")
+            for m in range(N // P):
+                nc.tensor.matmul_mx(
+                    out=y[:, m, :],
+                    lhsT=wd_cod[:, P * m : P * (m + 1)].bitcast(FP8X4),
+                    lhsT_scale=wd_scl[:, P * m : P * (m + 1)],
+                    rhs=h_cod[:].bitcast(FP8X4),
+                    rhs_scale=h_scl[:],
+                    start=True,
+                    stop=True,
+                )
+            y_sb = ring.tile([P, N // P, HC], F32, name="y_sb", align_bytes=64)
+            nc.scalar.copy(y_sb[:], y[:])
+            nc.sync.dma_start(out_rows[:, :, s * HC : (s + 1) * HC], y_sb[:])
+
+        for i in range(PACK - 1):
+            gather_x(0, i, 0, 2 * XC)
+        for c in range(2):
+            gather_x(0, PACK - 1, c * XC, (c + 1) * XC)
+            round_x(0, c)
+        head_product(0)
+        head_product(1)
+        for c in (2, 3):
+            for i in range(PACK):
+                gather_x(c - 1, i, c * XC, (c + 1) * XC)
+            round_x(c - 1, c)
+            head_product(c)
+            if c == 2:
+                nc.scalar.copy(
+                    wd_bf[:].rearrange("p (c i t) -> p c t i", i=2, t=PACK),
+                    wd_raw[:].rearrange("p t (c i) -> p c t i", i=2),
+                )
+                nc.vector.quantize_mx(out=wd_cod[:].bitcast(FP8X4), scales=wd_scl[:], in_=wd_bf[:])
+        join(0)
+        for s in range(1, J // HC):
+            join(s)
+            second_layer(s - 1)
+        second_layer(J // HC - 1)

@@ -22,8 +22,7 @@ GROUP = 16
 XC = 256
 TC = 512
 HC = 128
-SPANS = ((0, 512), (512, 768), (768, 1024))
-EARLY = 4
+GROUPS = ((0, 1), (2, 3), (4, 5), (6,), (7,))
 
 
 def tile_list_htabg_glu_none_kernel(
@@ -32,17 +31,16 @@ def tile_list_htabg_glu_none_kernel(
     nc = tc.nc
     with ExitStack() as ctx:
         keep = ctx.enter_context(tc.tile_pool(name="keep", bufs=1))
-        ring = ctx.enter_context(tc.tile_pool(name="ring", bufs=3))
         psum_a = ctx.enter_context(tc.psum_pool(name="psum_a", bufs=2))
-        psum_b = ctx.enter_context(tc.psum_pool(name="psum_b", bufs=4))
-        psum_y = ctx.enter_context(tc.psum_pool(name="psum_y", bufs=2))
+        psum_b = ctx.enter_context(tc.psum_pool(name="psum_b", bufs=3))
+        psum_y = ctx.enter_context(tc.psum_pool(name="psum_y", bufs=3))
 
         lst = keep.tile([P, J // GROUP], U16, name="lst")
         lst2 = keep.tile([P, J // GROUP], U16, name="lst2")
         tab_s = keep.tile([P, T], U8, name="tab_s", align_bytes=64)
         tab_w = keep.tile([P, T], I32, name="tab_w", align_bytes=64)
-        wgt = [keep.tile([P, b - a], F32, name="wgt%d" % a, align_bytes=64) for a, b in SPANS]
-        got_x = [keep.tile([P, PACK, b - a], F32, name="got_x%d" % a, align_bytes=64) for a, b in SPANS]
+        wgt = keep.tile([P, J], F32, name="wgt", align_bytes=64)
+        got_x = keep.tile([P, PACK, J], F32, name="got_x", align_bytes=64)
         x_pl = [keep.tile([P, T], F32, name="x_pl%d" % i, align_bytes=64) for i in range(PACK)]
         wd_raw = keep.tile([P, PACK, N], F32, name="wd_raw", align_bytes=64)
         w_raw = [keep.tile([P, n, 2 * R], U8, name="w_raw%d" % n, align_bytes=64) for n in (1, 2)]
@@ -70,15 +68,8 @@ def tile_list_htabg_glu_none_kernel(
             nc.sync.dma_start(
                 tab_s[32 * q + 24 : 32 * q + 32, :].bitcast(I32), tab_scales[:, 4 * q : 4 * q + 4, :].bitcast(I32)
             )
-        nc.sync.dma_start(tab_w[:], tab_words[0].rearrange("p t b -> p (t b)").bitcast(I32))
-        nc.sync.dma_start(w_raw[1][:].bitcast(I32), wb_words.rearrange("a p c -> p a c").bitcast(I32))
-        for q in range(4):
-            nc.sync.dma_start(
-                ws_raw[1][32 * q : 32 * q + 4, :, :].bitcast(I32),
-                wb_scales[:, 4 * q : 4 * q + 4, :].rearrange("a q r -> q a r").bitcast(I32),
-            )
         nc.sync.dma_start(lst2[:], offs2)
-        nc.sync.dma_start(wgt[0][:], wgt2[:, SPANS[0][0] : SPANS[0][1]])
+        nc.sync.dma_start(wgt[:], wgt2)
         for i in range(2):
             nc.sync.dma_start(x_pl[i][:], x_rows[i])
         nc.sync.dma_start(w_raw[0][:, 0, :].bitcast(I32), wa_words[0].bitcast(I32))
@@ -88,10 +79,15 @@ def tile_list_htabg_glu_none_kernel(
             )
         for i in range(2, PACK):
             nc.sync.dma_start(x_pl[i][:], x_rows[i])
-        for u in (1, 2):
-            for t in (2 * u - 2, 2 * u - 1):
-                nc.sync.dma_start(wd_raw[:, t, :], wd_rows[t])
-            nc.sync.dma_start(wgt[u][:], wgt2[:, SPANS[u][0] : SPANS[u][1]])
+        nc.sync.dma_start(w_raw[1][:].bitcast(I32), wb_words.rearrange("a p c -> p a c").bitcast(I32))
+        for q in range(4):
+            nc.sync.dma_start(
+                ws_raw[1][32 * q : 32 * q + 4, :, :].bitcast(I32),
+                wb_scales[:, 4 * q : 4 * q + 4, :].rearrange("a q r -> q a r").bitcast(I32),
+            )
+        nc.sync.dma_start(tab_w[:], tab_words[0].rearrange("p t b -> p (t b)").bitcast(I32))
+        for t in range(PACK):
+            nc.sync.dma_start(wd_raw[:, t, :], wd_rows[t])
 
         x_bf = [keep.tile([P, XC * PACK], BF16, name="x_bf%d" % c, align_bytes=64) for c in range(J // XC)]
         x_cod = [keep.tile([P, XC], U32, name="x_cod%d" % c, align_bytes=64) for c in range(J // XC)]
@@ -99,23 +95,10 @@ def tile_list_htabg_glu_none_kernel(
         got_w = [keep.tile([P, TC], U32, name="got_w%d" % c, align_bytes=64) for c in range(J // TC)]
         v_cod = [keep.tile([P, 4 * TC], U8, name="v_cod%d" % c, align_bytes=64) for c in range(J // TC)]
         gate = [keep.tile([P, HC * PACK], F32, name="gate%d" % s, align_bytes=64) for s in range(J // HC)]
-        lin = [keep.tile([P, HC * PACK], F32, name="lin%d" % s, align_bytes=64) for s in range(EARLY)]
         wd_bf = keep.tile([P, N * PACK], BF16, name="wd_bf", align_bytes=64)
         wd_cod = keep.tile([P, N], U32, name="wd_cod", align_bytes=64)
         wd_scl = keep.tile([P, N], U8, name="wd_scl", align_bytes=64)
         out_rows = out.rearrange("(m p) j -> p m j", p=P)
-
-        nc.vector.tensor_copy(got_s[:], tab_s[:].indirect(lst[:]))
-        for a in range(2):
-            nc.gpsimd.dma_start(v_scl[a][0:100, :].bitcast(I32), got_s[24 + 4 * a : 124 + 4 * a, :].bitcast(I32))
-        for c in range(J // TC):
-            entries = lst[:, c * TC // GROUP : (c + 1) * TC // GROUP]
-            nc.vector.tensor_copy(got_w[c][:], tab_w[:].bitcast(U32).indirect(entries))
-        for c in range(J // TC):
-            nc.vector.tensor_copy(
-                v_cod[c][:].bitcast(U16).rearrange("p (d j) -> p d j", d=2),
-                got_w[c][:].bitcast(U16).rearrange("p (j d) -> p d j", d=2),
-            )
 
         def order_columns(n):
             nc.vector.tensor_copy(
@@ -127,49 +110,27 @@ def tile_list_htabg_glu_none_kernel(
                 ws_raw[n][:].bitcast(I32).rearrange("p a (b t w) -> p a t b w", t=PACK, w=2),
             )
 
-        order_columns(1)
-        order_columns(0)
-        yb = {}
-
-        def table_product(s):
-            j0 = s * HC
-            vc, vo = divmod(j0, TC)
-            bank = psum_b.tile([P, PACK, HC], F32, name="bank")
-            for t in range(PACK):
-                for a in range(2):
-                    nc.tensor.matmul_mx(
-                        out=bank[:, t, :],
-                        lhsT=w_cod[1][:, a, 2 * P * t : 2 * P * (t + 1)].bitcast(FP4X4),
-                        lhsT_scale=w_scl[1][:, a, P * t : P * (t + 1)],
-                        rhs=v_cod[vc][:, 2 * (a * TC + vo) : 2 * (a * TC + vo + HC)].bitcast(FP4X4),
-                        rhs_scale=v_scl[a][:, j0 : j0 + HC],
-                        start=(a == 0),
-                        stop=(a == 1),
-                    )
-            yb[s] = bank[:].rearrange("p t j -> p j t")
-            if s < EARLY:
-                staged = lin[s][:].rearrange("p (j t) -> p j t", t=PACK)
-                nc.scalar.copy(staged, yb[s])
-                yb[s] = staged
-
-        for s in range(J // HC):
-            table_product(s)
-
-        def gather_x(u, i, j0, j1):
-            a = SPANS[u][0]
+        def gather_x(i, j0, j1):
             entries = lst2[:, j0 // GROUP : j1 // GROUP]
-            nc.vector.tensor_tensor(
-                got_x[u][:, i, j0 - a : j1 - a], x_pl[i][:].indirect(entries), wgt[u][:, j0 - a : j1 - a], MULT
-            )
+            nc.vector.tensor_tensor(got_x[:, i, j0:j1], x_pl[i][:].indirect(entries), wgt[:, j0:j1], MULT)
 
-        def round_x(u, c):
-            a = c * XC - SPANS[u][0]
+        nc.vector.tensor_copy(got_s[:], tab_s[:].indirect(lst[:]))
+        for a in range(2):
+            nc.gpsimd.dma_start(v_scl[a][0:100, :].bitcast(I32), got_s[24 + 4 * a : 124 + 4 * a, :].bitcast(I32))
+        for i in range(PACK - 1):
+            gather_x(i, 0, J)
+        order_columns(0)
+        for c in range(J // XC):
+            gather_x(PACK - 1, c * XC, (c + 1) * XC)
             nc.scalar.copy(
                 x_bf[c][:].rearrange("p (c i t) -> p c t i", i=2, t=PACK),
-                got_x[u][:, :, a : a + XC].rearrange("p t (c i) -> p c t i", i=2),
+                got_x[:, :, c * XC : (c + 1) * XC].rearrange("p t (c i) -> p c t i", i=2),
             )
-
-        def head_product(c):
+        nc.scalar.copy(
+            wd_bf[:].rearrange("p (c i t) -> p c t i", i=2, t=PACK),
+            wd_raw[:].rearrange("p t (c i) -> p c t i", i=2),
+        )
+        for c in range(J // XC):
             nc.vector.quantize_mx(out=x_cod[c][:].bitcast(FP8X4), scales=x_scl[c][:], in_=x_bf[c][:])
             for xo in range(0, XC, HC):
                 s = (c * XC + xo) // HC
@@ -188,56 +149,67 @@ def tile_list_htabg_glu_none_kernel(
                     gate[s][:].rearrange("p (j t) -> p j t", t=PACK), ya[:].rearrange("p t j -> p j t"), SILU
                 )
 
-        h_bf = {}
+        for c in range(J // TC):
+            entries = lst[:, c * TC // GROUP : (c + 1) * TC // GROUP]
+            nc.vector.tensor_copy(got_w[c][:], tab_w[:].bitcast(U32).indirect(entries))
+        order_columns(1)
+        for c in range(J // TC):
+            nc.vector.tensor_copy(
+                v_cod[c][:].bitcast(U16).rearrange("p (d j) -> p d j", d=2),
+                got_w[c][:].bitcast(U16).rearrange("p (j d) -> p d j", d=2),
+            )
+        nc.vector.quantize_mx(out=wd_cod[:].bitcast(FP8X4), scales=wd_scl[:], in_=wd_bf[:])
 
-        def join(s):
-            h_bf[s] = ring.tile([P, HC * PACK], BF16, name="h_bf", align_bytes=64)
+        def join(s, h_cols):
+            j0 = s * HC
+            vc, vo = divmod(j0, TC)
+            yb = psum_b.tile([P, PACK, HC], F32, name="yb")
+            for t in range(PACK):
+                for a in range(2):
+                    nc.tensor.matmul_mx(
+                        out=yb[:, t, :],
+                        lhsT=w_cod[1][:, a, 2 * P * t : 2 * P * (t + 1)].bitcast(FP4X4),
+                        lhsT_scale=w_scl[1][:, a, P * t : P * (t + 1)],
+                        rhs=v_cod[vc][:, 2 * (a * TC + vo) : 2 * (a * TC + vo + HC)].bitcast(FP4X4),
+                        rhs_scale=v_scl[a][:, j0 : j0 + HC],
+                        start=(a == 0),
+                        stop=(a == 1),
+                    )
             nc.vector.tensor_tensor(
-                h_bf[s][:].rearrange("p (j t) -> p j t", t=PACK),
-                yb[s],
+                h_cols.rearrange("p (j t) -> p j t", t=PACK),
+                yb[:].rearrange("p t j -> p j t"),
                 gate[s][:].rearrange("p (j t) -> p j t", t=PACK),
                 MULT,
             )
 
-        def second_layer(s):
-            h_cod = ring.tile([P, HC], U32, name="h_cod", align_bytes=64)
-            h_scl = ring.tile([P, HC], U8, name="h_scl", align_bytes=64)
-            nc.vector.quantize_mx(out=h_cod[:].bitcast(FP8X4), scales=h_scl[:], in_=h_bf[s][:])
-            y = psum_y.tile([P, N // P, HC], F32, name="y")
-            for m in range(N // P):
-                nc.tensor.matmul_mx(
-                    out=y[:, m, :],
-                    lhsT=wd_cod[:, P * m : P * (m + 1)].bitcast(FP8X4),
-                    lhsT_scale=wd_scl[:, P * m : P * (m + 1)],
-                    rhs=h_cod[:].bitcast(FP8X4),
-                    rhs_scale=h_scl[:],
-                    start=True,
-                    stop=True,
-                )
-            y_sb = ring.tile([P, N // P, HC], F32, name="y_sb", align_bytes=64)
-            nc.scalar.copy(y_sb[:], y[:])
-            nc.sync.dma_start(out_rows[:, :, s * HC : (s + 1) * HC], y_sb[:])
+        def first_layer(group):
+            h_bf = keep.tile([P, len(group) * HC * PACK], BF16, name="h_bf%d" % group[0], align_bytes=64)
+            for u, s in enumerate(group):
+                join(s, h_bf[:, u * HC * PACK : (u + 1) * HC * PACK])
+            return h_bf
 
-        for i in range(PACK - 1):
-            gather_x(0, i, 0, 2 * XC)
-        for c in range(2):
-            gather_x(0, PACK - 1, c * XC, (c + 1) * XC)
-            round_x(0, c)
-        head_product(0)
-        head_product(1)
-        for c in (2, 3):
-            for i in range(PACK):
-                gather_x(c - 1, i, c * XC, (c + 1) * XC)
-            round_x(c - 1, c)
-            head_product(c)
-            if c == 2:
-                nc.scalar.copy(
-                    wd_bf[:].rearrange("p (c i t) -> p c t i", i=2, t=PACK),
-                    wd_raw[:].rearrange("p t (c i) -> p c t i", i=2),
-                )
-                nc.vector.quantize_mx(out=wd_cod[:].bitcast(FP8X4), scales=wd_scl[:], in_=wd_bf[:])
-        join(0)
-        for s in range(1, J // HC):
-            join(s)
-            second_layer(s - 1)
-        second_layer(J // HC - 1)
+        def second_layer(group, h_bf):
+            h_cod = keep.tile([P, len(group) * HC], U32, name="h_cod%d" % group[0], align_bytes=64)
+            h_scl = keep.tile([P, len(group) * HC], U8, name="h_scl%d" % group[0], align_bytes=64)
+            nc.vector.quantize_mx(out=h_cod[:].bitcast(FP8X4), scales=h_scl[:], in_=h_bf[:])
+            for u, s in enumerate(group):
+                y = psum_y.tile([P, N // P, HC], F32, name="y")
+                for m in range(N // P):
+                    nc.tensor.matmul_mx(
+                        out=y[:, m, :],
+                        lhsT=wd_cod[:, P * m : P * (m + 1)].bitcast(FP8X4),
+                        lhsT_scale=wd_scl[:, P * m : P * (m + 1)],
+                        rhs=h_cod[:, u * HC : (u + 1) * HC].bitcast(FP8X4),
+                        rhs_scale=h_scl[:, u * HC : (u + 1) * HC],
+                        start=True,
+                        stop=True,
+                    )
+                y_sb = keep.tile([P, N // P, HC], F32, name="y_sb%d" % s, align_bytes=64)
+                nc.scalar.copy(y_sb[:], y[:])
+                nc.sync.dma_start(out_rows[:, :, s * HC : (s + 1) * HC], y_sb[:])
+
+        made = [first_layer(GROUPS[0])]
+        for g in range(1, len(GROUPS)):
+            made.append(first_layer(GROUPS[g]))
+            second_layer(GROUPS[g - 1], made[g - 1])
+        second_layer(GROUPS[-1], made[-1])

@@ -22,6 +22,7 @@ GROUP = 16
 XC = 256
 TC = 512
 HC = 128
+WC = 256
 GROUPS = ((0, 1), (2, 3), (4, 5), (6,), (7,))
 
 
@@ -31,76 +32,76 @@ def tile_list_htabg_glu_none_kernel(
     nc = tc.nc
     with ExitStack() as ctx:
         keep = ctx.enter_context(tc.tile_pool(name="keep", bufs=1))
-        psum_a = ctx.enter_context(tc.psum_pool(name="psum_a", bufs=2))
-        psum_b = ctx.enter_context(tc.psum_pool(name="psum_b", bufs=3))
-        psum_y = ctx.enter_context(tc.psum_pool(name="psum_y", bufs=3))
+        psum_a = ctx.enter_context(tc.psum_pool(name="psum_a", bufs=4))
+        psum_b = ctx.enter_context(tc.psum_pool(name="psum_b", bufs=4))
 
         lst = keep.tile([P, J // GROUP], U16, name="lst")
         lst2 = keep.tile([P, J // GROUP], U16, name="lst2")
         tab_s = keep.tile([P, T], U8, name="tab_s", align_bytes=64)
         tab_w = keep.tile([P, T], I32, name="tab_w", align_bytes=64)
-        wgt = keep.tile([P, J], F32, name="wgt", align_bytes=64)
-        got_x = keep.tile([P, PACK, J], F32, name="got_x", align_bytes=64)
-        x_pl = [keep.tile([P, T], F32, name="x_pl%d" % i, align_bytes=64) for i in range(PACK)]
+        wgt = keep.tile([P, J], F32, name="wgt", tag="wgt", align_bytes=64)
+        got_x = {}
+        x_pl = [keep.tile([P, T], F32, name="x_pl%d" % i, tag="x_pl%d" % i, align_bytes=64) for i in range(PACK)]
         wd_raw = keep.tile([P, PACK, N], F32, name="wd_raw", align_bytes=64)
-        w_raw = [keep.tile([P, n, 2 * R], U8, name="w_raw%d" % n, align_bytes=64) for n in (1, 2)]
-        ws_raw = [keep.tile([P, n, R], U8, name="ws_raw%d" % n, align_bytes=64) for n in (1, 2)]
-        w_cod = [keep.tile([P, n, 2 * R], U8, name="w_cod%d" % n, align_bytes=64) for n in (1, 2)]
-        w_scl = [keep.tile([P, n, R], U8, name="w_scl%d" % n, align_bytes=64) for n in (1, 2)]
+        w_raw = [keep.tile([P, n, 2 * R], U8, name="w_raw%d" % n, tag="w_raw%d" % n, align_bytes=64) for n in (1, 2)]
+        ws_raw = [keep.tile([P, n, R], U8, name="ws_raw%d" % n, tag="ws_raw%d" % n, align_bytes=64) for n in (1, 2)]
+        w_cod, w_scl, got_w, v_cod, wd_bf, wd_cod, wd_scl = {}, {}, {}, {}, {}, {}, {}
         got_s = keep.tile([P, J], U8, name="got_s", align_bytes=64)
         v_scl = [keep.tile([P, J], U8, name="v_scl%d" % a, align_bytes=64) for a in range(2)]
         warm = keep.tile([P, 8], F32, name="warm")
         warm_out = keep.tile([P, 8], F32, name="warm_out")
 
-        nc.vector.memset(ws_raw[1][:].rearrange("p a r -> p (a r)").bitcast(I32), 0)
         nc.vector.memset(ws_raw[0][:].rearrange("p a r -> p (a r)").bitcast(I32), 0)
+        nc.vector.memset(ws_raw[1][:].rearrange("p a r -> p (a r)").bitcast(I32), 0)
         nc.vector.memset(warm[:], 0.0)
-        for q in range(4):
-            nc.vector.memset(tab_s[32 * q : 32 * q + 24, :].bitcast(I32), 0)
+        nc.vector.memset(tab_s[32:64, :].bitcast(I32), 0)
+        nc.vector.memset(tab_s[64:128, :].bitcast(I32), 0)
         for a in range(2):
-            nc.vector.memset(v_scl[a][96:128, :].bitcast(I32), 0)
+            nc.vector.memset(v_scl[a][:].bitcast(I32), 0)
         nc.scalar.activation(warm_out[:], warm[:], SILU)
 
         x_rows = xT.rearrange("(p i) t -> i p t", i=PACK)
         wd_rows = wd.rearrange("(b t q) n -> t b q n", t=PACK, q=8)
+        def load_scale_rows(n, scales, quadrants):
+            for q in quadrants:
+                nc.sync.dma_start(
+                    ws_raw[n][32 * q : 32 * q + 4, :, :].bitcast(I32),
+                    scales[:, 4 * q : 4 * q + 4, :].rearrange("a q r -> q a r").bitcast(I32),
+                )
+
+        def move_scale_rows(moves):
+            for a, q in [divmod(move, 4) for move in moves]:
+                row = 16 * a + 4 * q
+                nc.sync.dma_start(v_scl[a][32 * q : 32 * q + 4, :].bitcast(I32), got_s[row : row + 4, :].bitcast(I32))
+
         nc.sync.dma_start(lst[:], offs)
-        for q in range(4):
-            nc.sync.dma_start(
-                tab_s[32 * q + 24 : 32 * q + 32, :].bitcast(I32), tab_scales[:, 4 * q : 4 * q + 4, :].bitcast(I32)
-            )
-        nc.sync.dma_start(lst2[:], offs2)
-        nc.sync.dma_start(wgt[:], wgt2)
-        for i in range(2):
-            nc.sync.dma_start(x_pl[i][:], x_rows[i])
-        nc.sync.dma_start(w_raw[0][:, 0, :].bitcast(I32), wa_words[0].bitcast(I32))
-        for q in range(4):
-            nc.sync.dma_start(
-                ws_raw[0][32 * q : 32 * q + 4, 0, :].bitcast(I32), wa_scales[0, 4 * q : 4 * q + 4, :].bitcast(I32)
-            )
-        for i in range(2, PACK):
-            nc.sync.dma_start(x_pl[i][:], x_rows[i])
-        nc.sync.dma_start(w_raw[1][:].bitcast(I32), wb_words.rearrange("a p c -> p a c").bitcast(I32))
-        for q in range(4):
-            nc.sync.dma_start(
-                ws_raw[1][32 * q : 32 * q + 4, :, :].bitcast(I32),
-                wb_scales[:, 4 * q : 4 * q + 4, :].rearrange("a q r -> q a r").bitcast(I32),
-            )
+        nc.sync.dma_start(tab_s[0:32, :].bitcast(I32), tab_scales.rearrange("a q t -> (a q) t").bitcast(I32))
         nc.sync.dma_start(tab_w[:], tab_words[0].rearrange("p t b -> p (t b)").bitcast(I32))
+        nc.sync.dma_start(lst2[:], offs2)
+        nc.sync.dma_start(x_pl[0][:], x_rows[0])
+        nc.sync.dma_start(wgt[:], wgt2)
+        nc.vector.tensor_copy(got_s[:], tab_s[:].indirect(lst[:]))
+        load_scale_rows(1, wb_scales, range(4))
+        nc.sync.dma_start(w_raw[1][:].bitcast(I32), wb_words.rearrange("a p c -> p a c").bitcast(I32))
+        load_scale_rows(0, wa_scales, range(1))
+        nc.sync.dma_start(x_pl[1][:], x_rows[1])
+        move_scale_rows(range(6))
+        nc.sync.dma_start(x_pl[2][:], x_rows[2])
+        move_scale_rows(range(6, 8))
+        load_scale_rows(0, wa_scales, range(1, 4))
+        nc.sync.dma_start(w_raw[0][:, 0, :].bitcast(I32), wa_words[0].bitcast(I32))
+        nc.sync.dma_start(x_pl[3][:], x_rows[3])
         for t in range(PACK):
             nc.sync.dma_start(wd_raw[:, t, :], wd_rows[t])
 
-        x_bf = [keep.tile([P, XC * PACK], BF16, name="x_bf%d" % c, align_bytes=64) for c in range(J // XC)]
-        x_cod = [keep.tile([P, XC], U32, name="x_cod%d" % c, align_bytes=64) for c in range(J // XC)]
-        x_scl = [keep.tile([P, XC], U8, name="x_scl%d" % c, align_bytes=64) for c in range(J // XC)]
-        got_w = [keep.tile([P, TC], U32, name="got_w%d" % c, align_bytes=64) for c in range(J // TC)]
-        v_cod = [keep.tile([P, 4 * TC], U8, name="v_cod%d" % c, align_bytes=64) for c in range(J // TC)]
+        x_bf = [keep.tile([P, XC * PACK], BF16, name="x_bf%d" % c, tag="x_bf%d" % c, align_bytes=64) for c in range(J // XC)]
+        x_cod, x_scl = {}, {}
         gate = [keep.tile([P, HC * PACK], F32, name="gate%d" % s, align_bytes=64) for s in range(J // HC)]
-        wd_bf = keep.tile([P, N * PACK], BF16, name="wd_bf", align_bytes=64)
-        wd_cod = keep.tile([P, N], U32, name="wd_cod", align_bytes=64)
-        wd_scl = keep.tile([P, N], U8, name="wd_scl", align_bytes=64)
         out_rows = out.rearrange("(m p) j -> p m j", p=P)
 
-        def order_columns(n):
+        def order_columns(n, cod_tag, scl_tag):
+            w_cod[n] = keep.tile([P, n + 1, 2 * R], U8, name="w_cod%d" % n, tag=cod_tag, align_bytes=64)
+            w_scl[n] = keep.tile([P, n + 1, R], U8, name="w_scl%d" % n, tag=scl_tag, align_bytes=64)
             nc.vector.tensor_copy(
                 w_cod[n][:].bitcast(I32).rearrange("p a (t b w) -> p a t b w", t=PACK, w=4),
                 w_raw[n][:].bitcast(I32).rearrange("p a (b t w) -> p a t b w", t=PACK, w=4),
@@ -112,29 +113,26 @@ def tile_list_htabg_glu_none_kernel(
 
         def gather_x(i, j0, j1):
             entries = lst2[:, j0 // GROUP : j1 // GROUP]
-            nc.vector.tensor_tensor(got_x[:, i, j0:j1], x_pl[i][:].indirect(entries), wgt[:, j0:j1], MULT)
+            half, o0 = divmod(j0, TC)
+            got = got_x[i // 2, half][:, i % 2, o0 : o0 + j1 - j0]
+            nc.vector.tensor_tensor(got, x_pl[i][:].indirect(entries), wgt[:, j0:j1], MULT)
 
-        nc.vector.tensor_copy(got_s[:], tab_s[:].indirect(lst[:]))
-        for a in range(2):
-            nc.gpsimd.dma_start(v_scl[a][0:100, :].bitcast(I32), got_s[24 + 4 * a : 124 + 4 * a, :].bitcast(I32))
-        for i in range(PACK - 1):
-            gather_x(i, 0, J)
-        order_columns(0)
-        for c in range(J // XC):
-            gather_x(PACK - 1, c * XC, (c + 1) * XC)
+        def round_pair(c, u):
+            half, o0 = divmod(c * XC, TC)
             nc.scalar.copy(
-                x_bf[c][:].rearrange("p (c i t) -> p c t i", i=2, t=PACK),
-                got_x[:, :, c * XC : (c + 1) * XC].rearrange("p t (c i) -> p c t i", i=2),
+                x_bf[c][:].rearrange("p (c i t) -> p c t i", i=2, t=PACK)[:, :, 2 * u : 2 * u + 2, :],
+                got_x[u, half][:, :, o0 : o0 + XC].rearrange("p t (c i) -> p c t i", i=2),
             )
-        nc.scalar.copy(
-            wd_bf[:].rearrange("p (c i t) -> p c t i", i=2, t=PACK),
-            wd_raw[:].rearrange("p t (c i) -> p c t i", i=2),
-        )
-        for c in range(J // XC):
+
+        def quantize_x(c):
+            x_cod[c] = keep.tile([P, XC], U32, name="x_cod%d" % c, align_bytes=64)
+            x_scl[c] = keep.tile([P, XC], U8, name="x_scl%d" % c, align_bytes=64)
             nc.vector.quantize_mx(out=x_cod[c][:].bitcast(FP8X4), scales=x_scl[c][:], in_=x_bf[c][:])
+
+        def gates(c):
             for xo in range(0, XC, HC):
                 s = (c * XC + xo) // HC
-                ya = psum_a.tile([P, PACK, HC], F32, name="ya")
+                ya = psum_a.tile([P, PACK, HC], F32, name="ya", tag="acc")
                 for t in range(PACK):
                     nc.tensor.matmul_mx(
                         out=ya[:, t, :],
@@ -149,16 +147,29 @@ def tile_list_htabg_glu_none_kernel(
                     gate[s][:].rearrange("p (j t) -> p j t", t=PACK), ya[:].rearrange("p t j -> p j t"), SILU
                 )
 
-        for c in range(J // TC):
+        def gather_words(c):
+            got_w[c] = keep.tile([P, TC], U32, name="got_w%d" % c, align_bytes=64)
             entries = lst[:, c * TC // GROUP : (c + 1) * TC // GROUP]
             nc.vector.tensor_copy(got_w[c][:], tab_w[:].bitcast(U32).indirect(entries))
-        order_columns(1)
-        for c in range(J // TC):
+
+        def round_wd(u, tag):
+            wd_bf[u] = keep.tile([P, WC * PACK], BF16, name="wd_bf%d" % u, tag=tag, align_bytes=64)
+            nc.scalar.copy(
+                wd_bf[u][:].rearrange("p (c i t) -> p c t i", i=2, t=PACK),
+                wd_raw[:, :, u * WC : (u + 1) * WC].rearrange("p t (c i) -> p c t i", i=2),
+            )
+
+        def quantize_wd(u):
+            wd_cod[u] = keep.tile([P, WC], U32, name="wd_cod%d" % u, align_bytes=64)
+            wd_scl[u] = keep.tile([P, WC], U8, name="wd_scl%d" % u, align_bytes=64)
+            nc.vector.quantize_mx(out=wd_cod[u][:].bitcast(FP8X4), scales=wd_scl[u][:], in_=wd_bf[u][:])
+
+        def part_words(c, tag):
+            v_cod[c] = keep.tile([P, 4 * TC], U8, name="v_cod%d" % c, tag=tag, align_bytes=64)
             nc.vector.tensor_copy(
                 v_cod[c][:].bitcast(U16).rearrange("p (d j) -> p d j", d=2),
                 got_w[c][:].bitcast(U16).rearrange("p (j d) -> p d j", d=2),
             )
-        nc.vector.quantize_mx(out=wd_cod[:].bitcast(FP8X4), scales=wd_scl[:], in_=wd_bf[:])
 
         def join(s, h_cols):
             j0 = s * HC
@@ -188,28 +199,80 @@ def tile_list_htabg_glu_none_kernel(
                 join(s, h_bf[:, u * HC * PACK : (u + 1) * HC * PACK])
             return h_bf
 
-        def second_layer(group, h_bf):
-            h_cod = keep.tile([P, len(group) * HC], U32, name="h_cod%d" % group[0], align_bytes=64)
-            h_scl = keep.tile([P, len(group) * HC], U8, name="h_scl%d" % group[0], align_bytes=64)
+        def quantize_h(group, h_bf):
+            width = len(group) * HC
+            h_cod = keep.tile([P, width], U32, name="h_cod%d" % group[0], align_bytes=64)
+            h_scl = keep.tile([P, width], U8, name="h_scl%d" % group[0], align_bytes=64)
             nc.vector.quantize_mx(out=h_cod[:].bitcast(FP8X4), scales=h_scl[:], in_=h_bf[:])
-            for u, s in enumerate(group):
-                y = psum_y.tile([P, N // P, HC], F32, name="y")
-                for m in range(N // P):
+            return h_cod, h_scl
+
+        def second_layer(group, h_cod, h_scl):
+            width = len(group) * HC
+            j0 = group[0] * HC
+            per_bank = PACK * HC // width
+            for m0 in range(0, N // P, per_bank):
+                y = psum_a.tile([P, per_bank, width], F32, name="y", tag="acc")
+                for m in range(m0, m0 + per_bank):
                     nc.tensor.matmul_mx(
-                        out=y[:, m, :],
-                        lhsT=wd_cod[:, P * m : P * (m + 1)].bitcast(FP8X4),
-                        lhsT_scale=wd_scl[:, P * m : P * (m + 1)],
-                        rhs=h_cod[:, u * HC : (u + 1) * HC].bitcast(FP8X4),
-                        rhs_scale=h_scl[:, u * HC : (u + 1) * HC],
+                        out=y[:, m - m0, :],
+                        lhsT=wd_cod[m // 2][:, P * (m % 2) : P * (m % 2 + 1)].bitcast(FP8X4),
+                        lhsT_scale=wd_scl[m // 2][:, P * (m % 2) : P * (m % 2 + 1)],
+                        rhs=h_cod[:].bitcast(FP8X4),
+                        rhs_scale=h_scl[:],
                         start=True,
                         stop=True,
                     )
-                y_sb = keep.tile([P, N // P, HC], F32, name="y_sb%d" % s, align_bytes=64)
-                nc.scalar.copy(y_sb[:], y[:])
-                nc.sync.dma_start(out_rows[:, :, s * HC : (s + 1) * HC], y_sb[:])
+                y_sb = keep.tile([P, per_bank, width], F32, name="y_sb%d_%d" % (group[0], m0), align_bytes=64)
+                if group == GROUPS[-1]:
+                    nc.vector.tensor_copy(y_sb[:], y[:])
+                else:
+                    nc.scalar.copy(y_sb[:], y[:])
+                nc.sync.dma_start(out_rows[:, m0 : m0 + per_bank, j0 : j0 + width], y_sb[:])
 
-        made = [first_layer(GROUPS[0])]
-        for g in range(1, len(GROUPS)):
-            made.append(first_layer(GROUPS[g]))
-            second_layer(GROUPS[g - 1], made[g - 1])
-        second_layer(GROUPS[-1], made[-1])
+        def new_got(pair, half, tag):
+            got_x[pair, half] = keep.tile([P, 2, TC], F32, name="got_x%d%d" % (pair, half), tag=tag, align_bytes=64)
+
+        for c in range(J // TC):
+            gather_words(c)
+        for c in range(J // TC):
+            part_words(c, "v_cod%d" % c)
+        for half in range(2):
+            new_got(0, half, "got_x0%d" % half)
+            gather_x(0, half * TC, (half + 1) * TC)
+        for half in range(2):
+            gather_x(1, half * TC, (half + 1) * TC)
+            round_pair(2 * half, 0)
+            round_pair(2 * half + 1, 0)
+        order_columns(1, "w_cod1", "w_scl1")
+        new_got(1, 0, "got_x10")
+        gather_x(2, 0, TC)
+        order_columns(0, "w_cod0", "w_scl0")
+        for c in range(2):
+            gather_x(3, c * XC, (c + 1) * XC)
+            round_pair(c, 1)
+        quantize_x(0)
+        gates(0)
+        round_wd(0, "wd_bf0")
+        new_got(1, 1, "x_bf0")
+        gather_x(2, TC, J)
+        quantize_x(1)
+        for c in range(2, 4):
+            gather_x(3, c * XC, (c + 1) * XC)
+            round_pair(c, 1)
+        gates(1)
+        round_wd(1, "wd_bf1")
+        h_bf = first_layer(GROUPS[0])
+        quantize_wd(0)
+        quantize_x(2)
+        made = quantize_h(GROUPS[0], h_bf)
+        quantize_x(3)
+        gates(2)
+        h_bf = first_layer(GROUPS[1])
+        quantize_wd(1)
+        second_layer(GROUPS[0], *made)
+        gates(3)
+        for g in range(2, len(GROUPS)):
+            ahead = first_layer(GROUPS[g])
+            second_layer(GROUPS[g - 1], *quantize_h(GROUPS[g - 1], h_bf))
+            h_bf = ahead
+        second_layer(GROUPS[-1], *quantize_h(GROUPS[-1], h_bf))

@@ -39,7 +39,7 @@ def tile_list_htabg_glu_none_kernel(
         lst2 = keep.tile([P, J // GROUP], U16, name="lst2")
         tab_s = keep.tile([P, T], U8, name="tab_s", align_bytes=64)
         tab_w = keep.tile([P, T], I32, name="tab_w", align_bytes=64)
-        wgt = keep.tile([P, J], F32, name="wgt", tag="wgt", align_bytes=64)
+        wgt = [keep.tile([P, TC], F32, name="wgt%d" % half, align_bytes=64) for half in range(2)]
         got_x = {}
         x_pl = [keep.tile([P, T], F32, name="x_pl%d" % i, tag="x_pl%d" % i, align_bytes=64) for i in range(PACK)]
         wd_raw = keep.tile([P, PACK, N], F32, name="wd_raw", align_bytes=64)
@@ -72,30 +72,27 @@ def tile_list_htabg_glu_none_kernel(
         def move_scale_rows(moves):
             for a, q in [divmod(move, 4) for move in moves]:
                 row = 16 * a + 4 * q
-                nc.sync.dma_start(v_scl[a][32 * q : 32 * q + 4, :].bitcast(I32), got_s[row : row + 4, :].bitcast(I32))
+                nc.gpsimd.dma_start(v_scl[a][32 * q : 32 * q + 4, :].bitcast(I32), got_s[row : row + 4, :].bitcast(I32))
 
         nc.sync.dma_start(lst[:], offs)
         nc.sync.dma_start(tab_s[0:32, :].bitcast(I32), tab_scales.rearrange("a q t -> (a q) t").bitcast(I32))
-        nc.sync.dma_start(tab_w[:], tab_words[0].rearrange("p t b -> p (t b)").bitcast(I32))
         nc.sync.dma_start(lst2[:], offs2)
         nc.sync.dma_start(x_pl[0][:], x_rows[0])
-        nc.sync.dma_start(wgt[:], wgt2)
-        nc.vector.tensor_copy(got_s[:], tab_s[:].indirect(lst[:]))
-        load_scale_rows(1, wb_scales, range(4))
-        nc.sync.dma_start(w_raw[1][:].bitcast(I32), wb_words.rearrange("a p c -> p a c").bitcast(I32))
-        load_scale_rows(0, wa_scales, range(1))
-        nc.sync.dma_start(x_pl[1][:], x_rows[1])
-        move_scale_rows(range(6))
-        nc.sync.dma_start(x_pl[2][:], x_rows[2])
-        move_scale_rows(range(6, 8))
-        load_scale_rows(0, wa_scales, range(1, 4))
+        for half in range(2):
+            nc.sync.dma_start(wgt[half][:], wgt2[:, half * TC : (half + 1) * TC])
+        for i in range(1, 3):
+            nc.sync.dma_start(x_pl[i][:], x_rows[i])
+        load_scale_rows(0, wa_scales, range(4))
         nc.sync.dma_start(w_raw[0][:, 0, :].bitcast(I32), wa_words[0].bitcast(I32))
         nc.sync.dma_start(x_pl[3][:], x_rows[3])
+        nc.sync.dma_start(w_raw[1][:].bitcast(I32), wb_words.rearrange("a p c -> p a c").bitcast(I32))
+        load_scale_rows(1, wb_scales, range(4))
+        nc.sync.dma_start(tab_w[:], tab_words[0].rearrange("p t b -> p (t b)").bitcast(I32))
         for t in range(PACK):
             nc.sync.dma_start(wd_raw[:, t, :], wd_rows[t])
 
         x_bf = [keep.tile([P, XC * PACK], BF16, name="x_bf%d" % c, tag="x_bf%d" % c, align_bytes=64) for c in range(J // XC)]
-        x_cod, x_scl = {}, {}
+        x_cod, x_scl, h_bf = {}, {}, {}
         gate = [keep.tile([P, HC * PACK], F32, name="gate%d" % s, align_bytes=64) for s in range(J // HC)]
         out_rows = out.rearrange("(m p) j -> p m j", p=P)
 
@@ -115,7 +112,7 @@ def tile_list_htabg_glu_none_kernel(
             entries = lst2[:, j0 // GROUP : j1 // GROUP]
             half, o0 = divmod(j0, TC)
             got = got_x[i // 2, half][:, i % 2, o0 : o0 + j1 - j0]
-            nc.vector.tensor_tensor(got, x_pl[i][:].indirect(entries), wgt[:, j0:j1], MULT)
+            nc.vector.tensor_tensor(got, x_pl[i][:].indirect(entries), wgt[half][:, o0 : o0 + j1 - j0], MULT)
 
         def round_pair(c, u):
             half, o0 = divmod(c * XC, TC)
@@ -148,7 +145,7 @@ def tile_list_htabg_glu_none_kernel(
                 )
 
         def gather_words(c):
-            got_w[c] = keep.tile([P, TC], U32, name="got_w%d" % c, align_bytes=64)
+            got_w[c] = keep.tile([P, TC], U32, name="got_w%d" % c, tag="got_w", align_bytes=64)
             entries = lst[:, c * TC // GROUP : (c + 1) * TC // GROUP]
             nc.vector.tensor_copy(got_w[c][:], tab_w[:].bitcast(U32).indirect(entries))
 
@@ -171,7 +168,11 @@ def tile_list_htabg_glu_none_kernel(
                 got_w[c][:].bitcast(U16).rearrange("p (j d) -> p d j", d=2),
             )
 
-        def join(s, h_cols):
+        def join(s):
+            group = [g for g in GROUPS if s in g][0]
+            if s == group[0]:
+                h_bf[group] = keep.tile([P, len(group) * HC * PACK], BF16, name="h_bf%d" % s, align_bytes=64)
+            h_cols = h_bf[group][:, (s - group[0]) * HC * PACK : (s - group[0] + 1) * HC * PACK]
             j0 = s * HC
             vc, vo = divmod(j0, TC)
             yb = psum_b.tile([P, PACK, HC], F32, name="yb")
@@ -193,17 +194,11 @@ def tile_list_htabg_glu_none_kernel(
                 MULT,
             )
 
-        def first_layer(group):
-            h_bf = keep.tile([P, len(group) * HC * PACK], BF16, name="h_bf%d" % group[0], align_bytes=64)
-            for u, s in enumerate(group):
-                join(s, h_bf[:, u * HC * PACK : (u + 1) * HC * PACK])
-            return h_bf
-
-        def quantize_h(group, h_bf):
+        def quantize_h(group):
             width = len(group) * HC
             h_cod = keep.tile([P, width], U32, name="h_cod%d" % group[0], align_bytes=64)
             h_scl = keep.tile([P, width], U8, name="h_scl%d" % group[0], align_bytes=64)
-            nc.vector.quantize_mx(out=h_cod[:].bitcast(FP8X4), scales=h_scl[:], in_=h_bf[:])
+            nc.vector.quantize_mx(out=h_cod[:].bitcast(FP8X4), scales=h_scl[:], in_=h_bf[group][:])
             return h_cod, h_scl
 
         def second_layer(group, h_cod, h_scl):
@@ -223,56 +218,49 @@ def tile_list_htabg_glu_none_kernel(
                         stop=True,
                     )
                 y_sb = keep.tile([P, per_bank, width], F32, name="y_sb%d_%d" % (group[0], m0), align_bytes=64)
-                if group == GROUPS[-1]:
-                    nc.vector.tensor_copy(y_sb[:], y[:])
-                else:
-                    nc.scalar.copy(y_sb[:], y[:])
+                nc.scalar.copy(y_sb[:], y[:])
                 nc.sync.dma_start(out_rows[:, m0 : m0 + per_bank, j0 : j0 + width], y_sb[:])
 
         def new_got(pair, half, tag):
             got_x[pair, half] = keep.tile([P, 2, TC], F32, name="got_x%d%d" % (pair, half), tag=tag, align_bytes=64)
 
-        for c in range(J // TC):
-            gather_words(c)
-        for c in range(J // TC):
-            part_words(c, "v_cod%d" % c)
+        nc.vector.tensor_copy(got_s[:], tab_s[:].indirect(lst[:]))
+        move_scale_rows(range(8))
+        for pair in range(2):
+            for half in range(2):
+                new_got(pair, half, "got_x%d%d" % (pair, half))
         for half in range(2):
-            new_got(0, half, "got_x0%d" % half)
             gather_x(0, half * TC, (half + 1) * TC)
         for half in range(2):
             gather_x(1, half * TC, (half + 1) * TC)
             round_pair(2 * half, 0)
             round_pair(2 * half + 1, 0)
-        order_columns(1, "w_cod1", "w_scl1")
-        new_got(1, 0, "got_x10")
-        gather_x(2, 0, TC)
+        for half in range(2):
+            gather_x(2, half * TC, (half + 1) * TC)
         order_columns(0, "w_cod0", "w_scl0")
+        for c in range(J // XC):
+            gather_x(3, c * XC, (c + 1) * XC)
+            round_pair(c, 1)
         for c in range(2):
-            gather_x(3, c * XC, (c + 1) * XC)
-            round_pair(c, 1)
-        quantize_x(0)
-        gates(0)
-        round_wd(0, "wd_bf0")
-        new_got(1, 1, "x_bf0")
-        gather_x(2, TC, J)
-        quantize_x(1)
+            quantize_x(c)
+            gates(c)
+        order_columns(1, "w_cod1", "w_scl1")
+        gather_words(0)
         for c in range(2, 4):
-            gather_x(3, c * XC, (c + 1) * XC)
-            round_pair(c, 1)
-        gates(1)
-        round_wd(1, "wd_bf1")
-        h_bf = first_layer(GROUPS[0])
-        quantize_wd(0)
-        quantize_x(2)
-        made = quantize_h(GROUPS[0], h_bf)
-        quantize_x(3)
-        gates(2)
-        h_bf = first_layer(GROUPS[1])
-        quantize_wd(1)
-        second_layer(GROUPS[0], *made)
-        gates(3)
-        for g in range(2, len(GROUPS)):
-            ahead = first_layer(GROUPS[g])
-            second_layer(GROUPS[g - 1], *quantize_h(GROUPS[g - 1], h_bf))
-            h_bf = ahead
-        second_layer(GROUPS[-1], *quantize_h(GROUPS[-1], h_bf))
+            quantize_x(c)
+            gates(c)
+            round_wd(c - 2, "wd_bf%d" % (c - 2))
+        part_words(0, "v_cod0")
+        gather_words(1)
+        part_words(1, "v_cod1")
+        for s in GROUPS[0]:
+            join(s)
+        for u in range(N // WC):
+            quantize_wd(u)
+        second_layer(GROUPS[0], *quantize_h(GROUPS[0]))
+        for s in range(len(GROUPS[0]), J // HC):
+            join(s)
+            for group in GROUPS[1:]:
+                if group[-1] == s - 1:
+                    second_layer(group, *quantize_h(group))
+        second_layer(GROUPS[-1], *quantize_h(GROUPS[-1]))

@@ -80,13 +80,13 @@ def tile_list_htabg_glu_none_kernel(
         nc.sync.dma_start(x_pl[0][:], x_rows[0])
         for half in range(2):
             nc.sync.dma_start(wgt[half][:], wgt2[:, half * TC : (half + 1) * TC])
-        for i in range(1, 3):
-            nc.sync.dma_start(x_pl[i][:], x_rows[i])
+        nc.sync.dma_start(x_pl[1][:], x_rows[1])
+        load_scale_rows(1, wb_scales, range(4))
+        nc.sync.dma_start(x_pl[2][:], x_rows[2])
         load_scale_rows(0, wa_scales, range(4))
         nc.sync.dma_start(w_raw[0][:, 0, :].bitcast(I32), wa_words[0].bitcast(I32))
-        nc.sync.dma_start(x_pl[3][:], x_rows[3])
         nc.sync.dma_start(w_raw[1][:].bitcast(I32), wb_words.rearrange("a p c -> p a c").bitcast(I32))
-        load_scale_rows(1, wb_scales, range(4))
+        nc.sync.dma_start(x_pl[3][:], x_rows[3])
         nc.sync.dma_start(tab_w[:], tab_words[0].rearrange("p t b -> p (t b)").bitcast(I32))
         for t in range(PACK):
             nc.sync.dma_start(wd_raw[:, t, :], wd_rows[t])
@@ -204,7 +204,7 @@ def tile_list_htabg_glu_none_kernel(
         def second_layer(group, h_cod, h_scl):
             width = len(group) * HC
             j0 = group[0] * HC
-            per_bank = PACK * HC // width
+            per_bank = 2 if group == GROUPS[-1] else PACK * HC // width
             for m0 in range(0, N // P, per_bank):
                 y = psum_a.tile([P, per_bank, width], F32, name="y", tag="acc")
                 for m in range(m0, m0 + per_bank):
@@ -218,7 +218,10 @@ def tile_list_htabg_glu_none_kernel(
                         stop=True,
                     )
                 y_sb = keep.tile([P, per_bank, width], F32, name="y_sb%d_%d" % (group[0], m0), align_bytes=64)
-                nc.scalar.copy(y_sb[:], y[:])
+                if group == GROUPS[-1] and m0 > 0:
+                    nc.vector.tensor_copy(y_sb[:], y[:])
+                else:
+                    nc.scalar.copy(y_sb[:], y[:])
                 nc.sync.dma_start(out_rows[:, m0 : m0 + per_bank, j0 : j0 + width], y_sb[:])
 
         def new_got(pair, half, tag):
@@ -238,18 +241,19 @@ def tile_list_htabg_glu_none_kernel(
         for half in range(2):
             gather_x(2, half * TC, (half + 1) * TC)
         order_columns(0, "w_cod0", "w_scl0")
+        order_columns(1, "w_cod1", "w_scl1")
         for c in range(J // XC):
             gather_x(3, c * XC, (c + 1) * XC)
             round_pair(c, 1)
         for c in range(2):
             quantize_x(c)
             gates(c)
-        order_columns(1, "w_cod1", "w_scl1")
         gather_words(0)
+        for u in range(N // WC):
+            round_wd(u, "wd_bf%d" % u)
         for c in range(2, 4):
             quantize_x(c)
             gates(c)
-            round_wd(c - 2, "wd_bf%d" % (c - 2))
         part_words(0, "v_cod0")
         gather_words(1)
         part_words(1, "v_cod1")

@@ -1,6 +1,7 @@
 from contextlib import ExitStack
 
 import concourse.mybir as mybir
+from concourse.masks import make_identity
 
 K, L, R, N, T, J = 512, 1024, 512, 512, 2048, 1024
 FLOPS = 2 * J * (K * R + L * R + R * N)
@@ -22,6 +23,7 @@ GROUP = 16
 XC = 256
 TC = 512
 HC = 128
+PASSES = 3
 WC = 256
 GROUPS = ((0, 1), (2, 3), (4, 5), (6,), (7,))
 
@@ -39,20 +41,30 @@ def tile_list_htabg_glu_none_kernel(
         lst2 = keep.tile([P, J // GROUP], U16, name="lst2")
         tab_s = keep.tile([P, T], U8, name="tab_s", align_bytes=64)
         tab_w = keep.tile([P, T], I32, name="tab_w", align_bytes=64)
-        wgt = [keep.tile([P, TC], F32, name="wgt%d" % half, align_bytes=64) for half in range(2)]
-        got_x = {}
+        wgt = keep.tile([P, J], F32, name="wgt", align_bytes=64)
+        got_x = keep.tile([P, PACK, J], F32, name="got_x", align_bytes=64)
         x_pl = [keep.tile([P, T], F32, name="x_pl%d" % i, tag="x_pl%d" % i, align_bytes=64) for i in range(PACK)]
         wd_raw = keep.tile([P, PACK, N], F32, name="wd_raw", align_bytes=64)
-        w_raw = [keep.tile([P, n, 2 * R], U8, name="w_raw%d" % n, tag="w_raw%d" % n, align_bytes=64) for n in (1, 2)]
-        ws_raw = [keep.tile([P, n, R], U8, name="ws_raw%d" % n, tag="ws_raw%d" % n, align_bytes=64) for n in (1, 2)]
-        w_cod, w_scl, got_w, v_cod, wd_bf, wd_cod, wd_scl = {}, {}, {}, {}, {}, {}, {}
+        w_raw = keep.tile([P, PASSES, 2 * R], U8, name="w_raw", align_bytes=64)
+        ws_raw = keep.tile([P, PASSES, R], U8, name="ws_raw", align_bytes=64)
+        w_cod = keep.tile([P, PASSES, 2 * R], U8, name="w_cod", align_bytes=64)
+        w_scl = keep.tile([P, PASSES, R], U8, name="w_scl", align_bytes=64)
+        wd_bf = keep.tile([P, N * PACK], BF16, name="wd_bf", align_bytes=64)
+        wd_cod = keep.tile([P, N], U32, name="wd_cod", align_bytes=64)
+        wd_scl = keep.tile([P, N], U8, name="wd_scl", align_bytes=64)
+        got_w, v_cod = {}, {}
         got_s = keep.tile([P, J], U8, name="got_s", align_bytes=64)
         v_scl = [keep.tile([P, J], U8, name="v_scl%d" % a, align_bytes=64) for a in range(2)]
         warm = keep.tile([P, 8], F32, name="warm")
         warm_out = keep.tile([P, 8], F32, name="warm_out")
 
-        nc.vector.memset(ws_raw[0][:].rearrange("p a r -> p (a r)").bitcast(I32), 0)
-        nc.vector.memset(ws_raw[1][:].rearrange("p a r -> p (a r)").bitcast(I32), 0)
+        ident = keep.tile([P, P], F32, name="ident", align_bytes=64)
+        wgt_rows = keep.tile([P, P], F32, name="wgt_rows", align_bytes=64)
+        wgt_cols = keep.tile([P, J // P, P], F32, name="wgt_cols", align_bytes=64)
+
+        make_identity(nc, ident[:])
+        nc.vector.memset(wgt_rows[64:128, :], 0.0)
+        nc.vector.memset(ws_raw[:].rearrange("p a r -> p (a r)").bitcast(I32), 0)
         nc.vector.memset(warm[:], 0.0)
         nc.vector.memset(tab_s[32:64, :].bitcast(I32), 0)
         nc.vector.memset(tab_s[64:128, :].bitcast(I32), 0)
@@ -62,10 +74,10 @@ def tile_list_htabg_glu_none_kernel(
 
         x_rows = xT.rearrange("(p i) t -> i p t", i=PACK)
         wd_rows = wd.rearrange("(b t q) n -> t b q n", t=PACK, q=8)
-        def load_scale_rows(n, scales, quadrants):
-            for q in quadrants:
+        def load_scale_rows(a0, a1, scales):
+            for q in range(4):
                 nc.sync.dma_start(
-                    ws_raw[n][32 * q : 32 * q + 4, :, :].bitcast(I32),
+                    ws_raw[32 * q : 32 * q + 4, a0:a1, :].bitcast(I32),
                     scales[:, 4 * q : 4 * q + 4, :].rearrange("a q r -> q a r").bitcast(I32),
                 )
 
@@ -74,19 +86,18 @@ def tile_list_htabg_glu_none_kernel(
                 row = 16 * a + 4 * q
                 nc.gpsimd.dma_start(v_scl[a][32 * q : 32 * q + 4, :].bitcast(I32), got_s[row : row + 4, :].bitcast(I32))
 
+        nc.sync.dma_start(wgt_rows[0:64, :], wgt2.rearrange("(g r) (c j) -> r c g j", r=GROUP, j=P)[0])
         nc.sync.dma_start(lst[:], offs)
         nc.sync.dma_start(tab_s[0:32, :].bitcast(I32), tab_scales.rearrange("a q t -> (a q) t").bitcast(I32))
         nc.sync.dma_start(lst2[:], offs2)
         nc.sync.dma_start(x_pl[0][:], x_rows[0])
-        for half in range(2):
-            nc.sync.dma_start(wgt[half][:], wgt2[:, half * TC : (half + 1) * TC])
         nc.sync.dma_start(x_pl[1][:], x_rows[1])
-        load_scale_rows(1, wb_scales, range(4))
+        load_scale_rows(1, 3, wb_scales)
         nc.sync.dma_start(x_pl[2][:], x_rows[2])
-        load_scale_rows(0, wa_scales, range(4))
-        nc.sync.dma_start(w_raw[0][:, 0, :].bitcast(I32), wa_words[0].bitcast(I32))
-        nc.sync.dma_start(w_raw[1][:].bitcast(I32), wb_words.rearrange("a p c -> p a c").bitcast(I32))
+        load_scale_rows(0, 1, wa_scales)
         nc.sync.dma_start(x_pl[3][:], x_rows[3])
+        nc.sync.dma_start(w_raw[:, 0, :].bitcast(I32), wa_words[0].bitcast(I32))
+        nc.sync.dma_start(w_raw[:, 1:3, :].bitcast(I32), wb_words.rearrange("a p c -> p a c").bitcast(I32))
         nc.sync.dma_start(tab_w[:], tab_words[0].rearrange("p t b -> p (t b)").bitcast(I32))
         for t in range(PACK):
             nc.sync.dma_start(wd_raw[:, t, :], wd_rows[t])
@@ -96,29 +107,24 @@ def tile_list_htabg_glu_none_kernel(
         gate = [keep.tile([P, HC * PACK], F32, name="gate%d" % s, align_bytes=64) for s in range(J // HC)]
         out_rows = out.rearrange("(m p) j -> p m j", p=P)
 
-        def order_columns(n, cod_tag, scl_tag):
-            w_cod[n] = keep.tile([P, n + 1, 2 * R], U8, name="w_cod%d" % n, tag=cod_tag, align_bytes=64)
-            w_scl[n] = keep.tile([P, n + 1, R], U8, name="w_scl%d" % n, tag=scl_tag, align_bytes=64)
+        def order_columns():
             nc.vector.tensor_copy(
-                w_cod[n][:].bitcast(I32).rearrange("p a (t b w) -> p a t b w", t=PACK, w=4),
-                w_raw[n][:].bitcast(I32).rearrange("p a (b t w) -> p a t b w", t=PACK, w=4),
+                w_cod[:].bitcast(I32).rearrange("p a (t b w) -> p t a b w", t=PACK, w=4),
+                w_raw[:].bitcast(I32).rearrange("p a (b t w) -> p t a b w", t=PACK, w=4),
             )
             nc.vector.tensor_copy(
-                w_scl[n][:].bitcast(I32).rearrange("p a (t b w) -> p a t b w", t=PACK, w=2),
-                ws_raw[n][:].bitcast(I32).rearrange("p a (b t w) -> p a t b w", t=PACK, w=2),
+                w_scl[:].bitcast(I32).rearrange("p a (t b w) -> p t a b w", t=PACK, w=2),
+                ws_raw[:].bitcast(I32).rearrange("p a (b t w) -> p t a b w", t=PACK, w=2),
             )
 
         def gather_x(i, j0, j1):
             entries = lst2[:, j0 // GROUP : j1 // GROUP]
-            half, o0 = divmod(j0, TC)
-            got = got_x[i // 2, half][:, i % 2, o0 : o0 + j1 - j0]
-            nc.vector.tensor_tensor(got, x_pl[i][:].indirect(entries), wgt[half][:, o0 : o0 + j1 - j0], MULT)
+            nc.vector.tensor_tensor(got_x[:, i, j0:j1], x_pl[i][:].indirect(entries), wgt[:, j0:j1], MULT)
 
-        def round_pair(c, u):
-            half, o0 = divmod(c * XC, TC)
+        def round_x(c):
             nc.scalar.copy(
-                x_bf[c][:].rearrange("p (c i t) -> p c t i", i=2, t=PACK)[:, :, 2 * u : 2 * u + 2, :],
-                got_x[u, half][:, :, o0 : o0 + XC].rearrange("p t (c i) -> p c t i", i=2),
+                x_bf[c][:].rearrange("p (c i t) -> p c t i", i=2, t=PACK),
+                got_x[:, :, c * XC : (c + 1) * XC].rearrange("p t (c i) -> p c t i", i=2),
             )
 
         def quantize_x(c):
@@ -133,8 +139,8 @@ def tile_list_htabg_glu_none_kernel(
                 for t in range(PACK):
                     nc.tensor.matmul_mx(
                         out=ya[:, t, :],
-                        lhsT=w_cod[0][:, 0, 2 * P * t : 2 * P * (t + 1)].bitcast(FP4X4),
-                        lhsT_scale=w_scl[0][:, 0, P * t : P * (t + 1)],
+                        lhsT=w_cod[:, 0, 2 * P * t : 2 * P * (t + 1)].bitcast(FP4X4),
+                        lhsT_scale=w_scl[:, 0, P * t : P * (t + 1)],
                         rhs=x_cod[c][:, xo : xo + HC].bitcast(FP8X4),
                         rhs_scale=x_scl[c][:, xo : xo + HC],
                         start=True,
@@ -149,17 +155,11 @@ def tile_list_htabg_glu_none_kernel(
             entries = lst[:, c * TC // GROUP : (c + 1) * TC // GROUP]
             nc.vector.tensor_copy(got_w[c][:], tab_w[:].bitcast(U32).indirect(entries))
 
-        def round_wd(u, tag):
-            wd_bf[u] = keep.tile([P, WC * PACK], BF16, name="wd_bf%d" % u, tag=tag, align_bytes=64)
+        def round_wd(u):
             nc.scalar.copy(
-                wd_bf[u][:].rearrange("p (c i t) -> p c t i", i=2, t=PACK),
+                wd_bf[:, u * WC * PACK : (u + 1) * WC * PACK].rearrange("p (c i t) -> p c t i", i=2, t=PACK),
                 wd_raw[:, :, u * WC : (u + 1) * WC].rearrange("p t (c i) -> p c t i", i=2),
             )
-
-        def quantize_wd(u):
-            wd_cod[u] = keep.tile([P, WC], U32, name="wd_cod%d" % u, align_bytes=64)
-            wd_scl[u] = keep.tile([P, WC], U8, name="wd_scl%d" % u, align_bytes=64)
-            nc.vector.quantize_mx(out=wd_cod[u][:].bitcast(FP8X4), scales=wd_scl[u][:], in_=wd_bf[u][:])
 
         def part_words(c, tag):
             v_cod[c] = keep.tile([P, 4 * TC], U8, name="v_cod%d" % c, tag=tag, align_bytes=64)
@@ -180,8 +180,8 @@ def tile_list_htabg_glu_none_kernel(
                 for a in range(2):
                     nc.tensor.matmul_mx(
                         out=yb[:, t, :],
-                        lhsT=w_cod[1][:, a, 2 * P * t : 2 * P * (t + 1)].bitcast(FP4X4),
-                        lhsT_scale=w_scl[1][:, a, P * t : P * (t + 1)],
+                        lhsT=w_cod[:, 1 + a, 2 * P * t : 2 * P * (t + 1)].bitcast(FP4X4),
+                        lhsT_scale=w_scl[:, 1 + a, P * t : P * (t + 1)],
                         rhs=v_cod[vc][:, 2 * (a * TC + vo) : 2 * (a * TC + vo + HC)].bitcast(FP4X4),
                         rhs_scale=v_scl[a][:, j0 : j0 + HC],
                         start=(a == 0),
@@ -210,8 +210,8 @@ def tile_list_htabg_glu_none_kernel(
                 for m in range(m0, m0 + per_bank):
                     nc.tensor.matmul_mx(
                         out=y[:, m - m0, :],
-                        lhsT=wd_cod[m // 2][:, P * (m % 2) : P * (m % 2 + 1)].bitcast(FP8X4),
-                        lhsT_scale=wd_scl[m // 2][:, P * (m % 2) : P * (m % 2 + 1)],
+                        lhsT=wd_cod[:, P * m : P * (m + 1)].bitcast(FP8X4),
+                        lhsT_scale=wd_scl[:, P * m : P * (m + 1)],
                         rhs=h_cod[:].bitcast(FP8X4),
                         rhs_scale=h_scl[:],
                         start=True,
@@ -224,33 +224,39 @@ def tile_list_htabg_glu_none_kernel(
                     nc.scalar.copy(y_sb[:], y[:])
                 nc.sync.dma_start(out_rows[:, m0 : m0 + per_bank, j0 : j0 + width], y_sb[:])
 
-        def new_got(pair, half, tag):
-            got_x[pair, half] = keep.tile([P, 2, TC], F32, name="got_x%d%d" % (pair, half), tag=tag, align_bytes=64)
+        turned = psum_a.tile([P, P], F32, name="turned", tag="acc")
+        nc.tensor.transpose(turned[:], wgt_rows[:], ident[:])
+        for half in range(2):
+            blocks = slice(half * PACK, (half + 1) * PACK)
+            nc.scalar.copy(
+                wgt_cols[:, blocks, :].rearrange("p c (g r) -> p (c g) r", r=GROUP),
+                turned[:, 32 * half : 32 * (half + 1)].unsqueeze(2).to_broadcast([P, 32, GROUP]),
+            )
+        for half in range(2):
+            spread = psum_a.tile([P, PACK, P], F32, name="spread", tag="acc")
+            for c in range(PACK):
+                nc.tensor.transpose(spread[:, c, :], wgt_cols[:, half * PACK + c, :], ident[:])
+            nc.scalar.copy(wgt[:, half * TC : (half + 1) * TC], spread[:].rearrange("p c j -> p (c j)"))
 
         nc.vector.tensor_copy(got_s[:], tab_s[:].indirect(lst[:]))
         move_scale_rows(range(8))
-        for pair in range(2):
-            for half in range(2):
-                new_got(pair, half, "got_x%d%d" % (pair, half))
         for half in range(2):
             gather_x(0, half * TC, (half + 1) * TC)
-        for half in range(2):
-            gather_x(1, half * TC, (half + 1) * TC)
-            round_pair(2 * half, 0)
-            round_pair(2 * half + 1, 0)
-        for half in range(2):
-            gather_x(2, half * TC, (half + 1) * TC)
-        order_columns(0, "w_cod0", "w_scl0")
-        order_columns(1, "w_cod1", "w_scl1")
-        for c in range(J // XC):
+        for i in range(1, PACK - 1):
+            gather_x(i, 0, J)
+        for c in range(2):
             gather_x(3, c * XC, (c + 1) * XC)
-            round_pair(c, 1)
+            round_x(c)
+        gather_x(3, TC, J)
+        for c in range(2, 4):
+            round_x(c)
+        order_columns()
         for c in range(2):
             quantize_x(c)
             gates(c)
         gather_words(0)
         for u in range(N // WC):
-            round_wd(u, "wd_bf%d" % u)
+            round_wd(u)
         for c in range(2, 4):
             quantize_x(c)
             gates(c)
@@ -259,8 +265,7 @@ def tile_list_htabg_glu_none_kernel(
         part_words(1, "v_cod1")
         for s in GROUPS[0]:
             join(s)
-        for u in range(N // WC):
-            quantize_wd(u)
+        nc.vector.quantize_mx(out=wd_cod[:].bitcast(FP8X4), scales=wd_scl[:], in_=wd_bf[:])
         second_layer(GROUPS[0], *quantize_h(GROUPS[0]))
         for s in range(len(GROUPS[0]), J // HC):
             join(s)

@@ -104,7 +104,7 @@ def tile_list_htabg_glu_none_kernel(
 
         x_bf = [keep.tile([P, XC * PACK], BF16, name="x_bf%d" % c, tag="x_bf%d" % c, align_bytes=64) for c in range(J // XC)]
         x_cod, x_scl, h_bf = {}, {}, {}
-        gate = [keep.tile([P, HC * PACK], F32, name="gate%d" % s, align_bytes=64) for s in range(J // HC)]
+        gate = [keep.tile([P, PACK * XC], F32, name="gate%d" % c, align_bytes=64)[:] for c in range(J // XC)]
         out_rows = out.rearrange("(m p) j -> p m j", p=P)
 
         def order_columns():
@@ -133,22 +133,19 @@ def tile_list_htabg_glu_none_kernel(
             nc.vector.quantize_mx(out=x_cod[c][:].bitcast(FP8X4), scales=x_scl[c][:], in_=x_bf[c][:])
 
         def gates(c):
-            for xo in range(0, XC, HC):
-                s = (c * XC + xo) // HC
-                ya = psum_a.tile([P, PACK, HC], F32, name="ya", tag="acc")
-                for t in range(PACK):
+            for t0 in range(0, PACK, 2):
+                ya = psum_a.tile([P, 2, XC], F32, name="ya", tag="acc")
+                for t in range(t0, t0 + 2):
                     nc.tensor.matmul_mx(
-                        out=ya[:, t, :],
+                        out=ya[:, t - t0, :],
                         lhsT=w_cod[:, 0, 2 * P * t : 2 * P * (t + 1)].bitcast(FP4X4),
                         lhsT_scale=w_scl[:, 0, P * t : P * (t + 1)],
-                        rhs=x_cod[c][:, xo : xo + HC].bitcast(FP8X4),
-                        rhs_scale=x_scl[c][:, xo : xo + HC],
+                        rhs=x_cod[c][:].bitcast(FP8X4),
+                        rhs_scale=x_scl[c][:],
                         start=True,
                         stop=True,
                     )
-                nc.scalar.activation(
-                    gate[s][:].rearrange("p (j t) -> p j t", t=PACK), ya[:].rearrange("p t j -> p j t"), SILU
-                )
+                nc.scalar.activation(gate[c][:, t0 * XC : (t0 + 2) * XC], ya[:].rearrange("p t j -> p (t j)"), SILU)
 
         def gather_words(c):
             got_w[c] = keep.tile([P, TC], U32, name="got_w%d" % c, tag="got_w", align_bytes=64)
@@ -175,6 +172,7 @@ def tile_list_htabg_glu_none_kernel(
             h_cols = h_bf[group][:, (s - group[0]) * HC * PACK : (s - group[0] + 1) * HC * PACK]
             j0 = s * HC
             vc, vo = divmod(j0, TC)
+            gc, go = divmod(j0, XC)
             yb = psum_b.tile([P, PACK, HC], F32, name="yb")
             for t in range(PACK):
                 for a in range(2):
@@ -188,9 +186,9 @@ def tile_list_htabg_glu_none_kernel(
                         stop=(a == 1),
                     )
             nc.vector.tensor_tensor(
-                h_cols.rearrange("p (j t) -> p j t", t=PACK),
-                yb[:].rearrange("p t j -> p j t"),
-                gate[s][:].rearrange("p (j t) -> p j t", t=PACK),
+                h_cols.rearrange("p (c i t) -> p c t i", i=2, t=PACK),
+                yb[:].rearrange("p t (c i) -> p c t i", i=2),
+                gate[gc].rearrange("p (t c i) -> p c t i", t=PACK, i=2)[:, go // 2 : (go + HC) // 2, :, :],
                 MULT,
             )
 

@@ -87,10 +87,10 @@ def tile_list_htabg_glu_none_kernel(
                 nc.gpsimd.dma_start(v_scl[a][32 * q : 32 * q + 4, :].bitcast(I32), got_s[row : row + 4, :].bitcast(I32))
 
         nc.sync.dma_start(wgt_rows[0:64, :], wgt2.rearrange("(g r) (c j) -> r c g j", r=GROUP, j=P)[0])
-        nc.sync.dma_start(lst[:], offs)
         nc.sync.dma_start(tab_s[0:32, :].bitcast(I32), tab_scales.rearrange("a q t -> (a q) t").bitcast(I32))
-        nc.sync.dma_start(lst2[:], offs2)
+        nc.sync.dma_start(lst[:], offs)
         nc.sync.dma_start(x_pl[0][:], x_rows[0])
+        nc.sync.dma_start(lst2[:], offs2)
         nc.sync.dma_start(x_pl[1][:], x_rows[1])
         load_scale_rows(1, 3, wb_scales)
         nc.sync.dma_start(x_pl[2][:], x_rows[2])
@@ -224,17 +224,16 @@ def tile_list_htabg_glu_none_kernel(
 
         turned = psum_a.tile([P, P], F32, name="turned", tag="acc")
         nc.tensor.transpose(turned[:], wgt_rows[:], ident[:])
-        for half in range(2):
-            blocks = slice(half * PACK, (half + 1) * PACK)
+        for c0, c1 in ((0, 2), (2, 4), (4, 8)):
             nc.scalar.copy(
-                wgt_cols[:, blocks, :].rearrange("p c (g r) -> p (c g) r", r=GROUP),
-                turned[:, 32 * half : 32 * (half + 1)].unsqueeze(2).to_broadcast([P, 32, GROUP]),
+                wgt_cols[:, c0:c1, :].rearrange("p c (g r) -> p (c g) r", r=GROUP),
+                turned[:, 8 * c0 : 8 * c1].unsqueeze(2).to_broadcast([P, 8 * (c1 - c0), GROUP]),
             )
-        for half in range(2):
-            spread = psum_a.tile([P, PACK, P], F32, name="spread", tag="acc")
-            for c in range(PACK):
-                nc.tensor.transpose(spread[:, c, :], wgt_cols[:, half * PACK + c, :], ident[:])
-            nc.scalar.copy(wgt[:, half * TC : (half + 1) * TC], spread[:].rearrange("p c j -> p (c j)"))
+        for c0, c1 in ((0, 2), (2, 4), (4, 8)):
+            spread = psum_a.tile([P, c1 - c0, P], F32, name="spread", tag="acc")
+            for c in range(c0, c1):
+                nc.tensor.transpose(spread[:, c - c0, :], wgt_cols[:, c, :], ident[:])
+            nc.scalar.copy(wgt[:, c0 * P : c1 * P], spread[:].rearrange("p c j -> p (c j)"))
 
         nc.vector.tensor_copy(got_s[:], tab_s[:].indirect(lst[:]))
         move_scale_rows(range(8))

@@ -20,12 +20,9 @@ SILU = mybir.ActivationFunctionType.Silu
 P = 128
 PACK = 4
 GROUP = 16
-XC = 256
-TC = 512
-HC = 128
-PASSES = 3
-WC = 256
-GROUPS = ((0, 1), (2, 3), (4, 5), (6,), (7,))
+CHUNK = 256
+HALF = 512
+STEP = 128
 
 
 def tile_list_htabg_glu_none_kernel(
@@ -34,239 +31,313 @@ def tile_list_htabg_glu_none_kernel(
     nc = tc.nc
     with ExitStack() as ctx:
         keep = ctx.enter_context(tc.tile_pool(name="keep", bufs=1))
-        psum_a = ctx.enter_context(tc.psum_pool(name="psum_a", bufs=4))
-        psum_b = ctx.enter_context(tc.psum_pool(name="psum_b", bufs=4))
+        reuse = ctx.enter_context(tc.tile_pool(name="reuse", bufs=1))
+        psum = ctx.enter_context(tc.psum_pool(name="psum", bufs=1))
+
+        def sb(name, shape, dtype):
+            return keep.tile(shape, dtype, name=name, tag=name, align_bytes=64)
+
+        def sb_at(name, shape, dtype, offset):
+            return reuse.tile(shape, dtype, name=name, tag=name, align_bytes=64, offset=offset)
+
+        def bank(number, name, shape):
+            return psum.tile(shape, F32, name=name, tag="bank%d" % number)
 
         lst = keep.tile([P, J // GROUP], U16, name="lst")
         lst2 = keep.tile([P, J // GROUP], U16, name="lst2")
-        tab_s = keep.tile([P, T], U8, name="tab_s", align_bytes=64)
-        tab_w = keep.tile([P, T], I32, name="tab_w", align_bytes=64)
-        wgt = keep.tile([P, J], F32, name="wgt", align_bytes=64)
-        got_x = keep.tile([P, PACK, J], F32, name="got_x", align_bytes=64)
-        x_pl = [keep.tile([P, T], F32, name="x_pl%d" % i, tag="x_pl%d" % i, align_bytes=64) for i in range(PACK)]
-        wd_raw = keep.tile([P, PACK, N], F32, name="wd_raw", align_bytes=64)
-        w_raw = keep.tile([P, PASSES, 2 * R], U8, name="w_raw", align_bytes=64)
-        ws_raw = keep.tile([P, PASSES, R], U8, name="ws_raw", align_bytes=64)
-        w_cod = keep.tile([P, PASSES, 2 * R], U8, name="w_cod", align_bytes=64)
-        w_scl = keep.tile([P, PASSES, R], U8, name="w_scl", align_bytes=64)
-        wd_bf = keep.tile([P, N * PACK], BF16, name="wd_bf", align_bytes=64)
-        wd_cod = keep.tile([P, N], U32, name="wd_cod", align_bytes=64)
-        wd_scl = keep.tile([P, N], U8, name="wd_scl", align_bytes=64)
-        got_w, v_cod = {}, {}
-        got_s = keep.tile([P, J], U8, name="got_s", align_bytes=64)
-        v_scl = [keep.tile([P, J], U8, name="v_scl%d" % a, align_bytes=64) for a in range(2)]
-        warm = keep.tile([P, 8], F32, name="warm")
-        warm_out = keep.tile([P, 8], F32, name="warm_out")
-
-        ident = keep.tile([P, P], F32, name="ident", align_bytes=64)
-        wgt_rows = keep.tile([P, P], F32, name="wgt_rows", align_bytes=64)
-        wgt_cols = keep.tile([P, J // P, P], F32, name="wgt_cols", align_bytes=64)
+        tab_s = sb("tab_s", [P, T], U8)
+        tab_w = sb("tab_w", [P, T], I32)
+        wgt = sb("wgt", [P, J], F32)
+        got_x = sb("got_x", [P, PACK, J], F32)
+        x_pl = [sb("x_pl%d" % i, [P, T], F32) for i in range(PACK)]
+        wd_raw = sb_at("wd_raw", [P, PACK, N], F32, 960)
+        w_raw = sb("w_raw", [P, 3, 2 * R], U8)
+        was_raw = sb("was_raw", [P, 1, R], U8)
+        wbs_raw = sb_at("wbs_raw", [P, 2, R], U8, 9216)
+        wa_scl = sb("wa_scl", [P, 1, R], U8)
+        wd_bf = sb("wd_bf", [P, N * PACK], BF16)
+        wd_scl = sb("wd_scl", [P, N], U8)
+        got_s = sb("got_s", [P, J], U8)
+        v_scl = sb("v_scl", [P, 2, J], U8)
+        warm = sb("warm", [P, 8], F32)
+        warm_out = sb("warm_out", [P, 8], F32)
+        ident = sb("ident", [P, P], F32)
+        wgt_rows = sb("wgt_rows", [P, P], F32)
+        wgt_cols = sb_at("wgt_cols", [P, J // P, P], F32, 11264)
 
         make_identity(nc, ident[:])
         nc.vector.memset(wgt_rows[64:128, :], 0.0)
-        nc.vector.memset(ws_raw[:].rearrange("p a r -> p (a r)").bitcast(I32), 0)
+        nc.vector.memset(wbs_raw[:].rearrange("p a r -> p (a r)").bitcast(I32), 0)
+        nc.vector.memset(was_raw[:].rearrange("p a r -> p (a r)").bitcast(I32), 0)
         nc.vector.memset(warm[:], 0.0)
         nc.vector.memset(tab_s[32:64, :].bitcast(I32), 0)
         nc.vector.memset(tab_s[64:128, :].bitcast(I32), 0)
-        for a in range(2):
-            nc.vector.memset(v_scl[a][:].bitcast(I32), 0)
+        nc.vector.memset(v_scl[:].rearrange("p a j -> p (a j)").bitcast(I32), 0)
         nc.scalar.activation(warm_out[:], warm[:], SILU)
 
         x_rows = xT.rearrange("(p i) t -> i p t", i=PACK)
         wd_rows = wd.rearrange("(b t q) n -> t b q n", t=PACK, q=8)
-        def load_scale_rows(a0, a1, scales):
+
+        def load_scale_rows(tile, scales):
             for q in range(4):
                 nc.sync.dma_start(
-                    ws_raw[32 * q : 32 * q + 4, a0:a1, :].bitcast(I32),
+                    tile[32 * q : 32 * q + 4, :, :].bitcast(I32),
                     scales[:, 4 * q : 4 * q + 4, :].rearrange("a q r -> q a r").bitcast(I32),
                 )
 
-        def move_scale_rows(moves):
-            for a, q in [divmod(move, 4) for move in moves]:
-                row = 16 * a + 4 * q
-                nc.gpsimd.dma_start(v_scl[a][32 * q : 32 * q + 4, :].bitcast(I32), got_s[row : row + 4, :].bitcast(I32))
+        def move_scale_rows(q0, q1):
+            for q in range(q0, q1):
+                nc.sync.dma_start(v_scl[32 * q : 32 * q + 4, :, :].bitcast(I32), got_s[8 * q : 8 * q + 8, :].bitcast(I32))
 
         nc.sync.dma_start(wgt_rows[0:64, :], wgt2.rearrange("(g r) (c j) -> r c g j", r=GROUP, j=P)[0])
-        nc.sync.dma_start(tab_s[0:32, :].bitcast(I32), tab_scales.rearrange("a q t -> (a q) t").bitcast(I32))
+        nc.sync.dma_start(tab_s[0:32, :].bitcast(I32), tab_scales.rearrange("a q t -> q a t").bitcast(I32))
         nc.sync.dma_start(lst[:], offs)
         nc.sync.dma_start(x_pl[0][:], x_rows[0])
         nc.sync.dma_start(lst2[:], offs2)
-        nc.sync.dma_start(x_pl[1][:], x_rows[1])
-        load_scale_rows(1, 3, wb_scales)
-        nc.sync.dma_start(x_pl[2][:], x_rows[2])
-        load_scale_rows(0, 1, wa_scales)
-        nc.sync.dma_start(x_pl[3][:], x_rows[3])
         nc.sync.dma_start(w_raw[:, 0, :].bitcast(I32), wa_words[0].bitcast(I32))
         nc.sync.dma_start(w_raw[:, 1:3, :].bitcast(I32), wb_words.rearrange("a p c -> p a c").bitcast(I32))
+        nc.sync.dma_start(x_pl[1][:], x_rows[1])
+        nc.vector.tensor_copy(got_s[:], tab_s[:].indirect(lst[:]))
+        load_scale_rows(wbs_raw, wb_scales)
+        move_scale_rows(0, 2)
+        nc.sync.dma_start(x_pl[2][:], x_rows[2])
+        load_scale_rows(was_raw, wa_scales)
+        move_scale_rows(2, 4)
+        nc.sync.dma_start(x_pl[3][:], x_rows[3])
         nc.sync.dma_start(tab_w[:], tab_words[0].rearrange("p t b -> p (t b)").bitcast(I32))
         for t in range(PACK):
             nc.sync.dma_start(wd_raw[:, t, :], wd_rows[t])
 
-        x_bf = [keep.tile([P, XC * PACK], BF16, name="x_bf%d" % c, tag="x_bf%d" % c, align_bytes=64) for c in range(J // XC)]
-        x_cod, x_scl, h_bf = {}, {}, {}
-        gate = [keep.tile([P, PACK * XC], F32, name="gate%d" % c, align_bytes=64)[:] for c in range(J // XC)]
         out_rows = out.rearrange("(m p) j -> p m j", p=P)
+        x_bf, x_cod, x_scl, gate, got_w, v_cod, yb, h_bf, h_cod, h_scl = {}, {}, {}, {}, {}, {}, {}, {}, {}, {}
 
-        def order_columns():
-            nc.vector.tensor_copy(
-                w_cod[:].bitcast(I32).rearrange("p a (t b w) -> p t a b w", t=PACK, w=4),
-                w_raw[:].bitcast(I32).rearrange("p a (b t w) -> p t a b w", t=PACK, w=4),
-            )
-            nc.vector.tensor_copy(
-                w_scl[:].bitcast(I32).rearrange("p a (t b w) -> p t a b w", t=PACK, w=2),
-                ws_raw[:].bitcast(I32).rearrange("p a (b t w) -> p t a b w", t=PACK, w=2),
+        step_gate = {}
+
+        def order_columns(ordered, raw, words):
+            nc.scalar.copy(
+                ordered[:].bitcast(U32).rearrange("p a (t b w) -> p a t b w", t=PACK, w=words),
+                raw[:].bitcast(U32).rearrange("p a (b t w) -> p a t b w", t=PACK, w=words),
             )
 
         def gather_x(i, j0, j1):
             entries = lst2[:, j0 // GROUP : j1 // GROUP]
             nc.vector.tensor_tensor(got_x[:, i, j0:j1], x_pl[i][:].indirect(entries), wgt[:, j0:j1], MULT)
 
-        def round_x(c):
+        def round_x(c, t0):
             nc.scalar.copy(
-                x_bf[c][:].rearrange("p (c i t) -> p c t i", i=2, t=PACK),
-                got_x[:, :, c * XC : (c + 1) * XC].rearrange("p t (c i) -> p c t i", i=2),
+                x_bf[c][:].rearrange("p (c i t) -> p c t i", i=2, t=PACK)[:, :, t0 : t0 + 2, :],
+                got_x[:, t0 : t0 + 2, c * CHUNK : (c + 1) * CHUNK].rearrange("p t (c i) -> p c t i", i=2),
             )
 
         def quantize_x(c):
-            x_cod[c] = keep.tile([P, XC], U32, name="x_cod%d" % c, align_bytes=64)
-            x_scl[c] = keep.tile([P, XC], U8, name="x_scl%d" % c, align_bytes=64)
+            x_cod[c] = sb("x_cod%d" % c, [P, CHUNK], U32)
+            x_scl[c] = sb("x_scl%d" % c, [P, CHUNK], U8)
             nc.vector.quantize_mx(out=x_cod[c][:].bitcast(FP8X4), scales=x_scl[c][:], in_=x_bf[c][:])
 
-        def gates(c):
-            for t0 in range(0, PACK, 2):
-                ya = psum_a.tile([P, 2, XC], F32, name="ya", tag="acc")
-                for t in range(t0, t0 + 2):
+        def gates(c, first_bank):
+            for u in range(2):
+                ya = bank(first_bank + u, "ya%d_%d" % (c, u), [P, 2, CHUNK])
+                for t in range(2 * u, 2 * u + 2):
                     nc.tensor.matmul_mx(
-                        out=ya[:, t - t0, :],
+                        out=ya[:, t - 2 * u, :],
                         lhsT=w_cod[:, 0, 2 * P * t : 2 * P * (t + 1)].bitcast(FP4X4),
-                        lhsT_scale=w_scl[:, 0, P * t : P * (t + 1)],
+                        lhsT_scale=wa_scl[:, 0, P * t : P * (t + 1)],
                         rhs=x_cod[c][:].bitcast(FP8X4),
                         rhs_scale=x_scl[c][:],
                         start=True,
                         stop=True,
                     )
-                nc.scalar.activation(gate[c][:, t0 * XC : (t0 + 2) * XC], ya[:].rearrange("p t j -> p (t j)"), SILU)
+                nc.scalar.activation(
+                    gate[c][:, 2 * u * CHUNK : (2 * u + 2) * CHUNK], ya[:].rearrange("p t j -> p (t j)"), SILU
+                )
+            pairs = gate[c][:].rearrange("p (t c i) -> p c t i", t=PACK, i=2)
+            for u in range(2):
+                step_gate[2 * c + u] = pairs[:, u * STEP // 2 : (u + 1) * STEP // 2, :, :]
 
-        def gather_words(c):
-            got_w[c] = keep.tile([P, TC], U32, name="got_w%d" % c, tag="got_w", align_bytes=64)
-            entries = lst[:, c * TC // GROUP : (c + 1) * TC // GROUP]
-            nc.vector.tensor_copy(got_w[c][:], tab_w[:].bitcast(U32).indirect(entries))
-
-        def round_wd(u):
-            nc.scalar.copy(
-                wd_bf[:, u * WC * PACK : (u + 1) * WC * PACK].rearrange("p (c i t) -> p c t i", i=2, t=PACK),
-                wd_raw[:, :, u * WC : (u + 1) * WC].rearrange("p t (c i) -> p c t i", i=2),
-            )
-
-        def part_words(c, tag):
-            v_cod[c] = keep.tile([P, 4 * TC], U8, name="v_cod%d" % c, tag=tag, align_bytes=64)
-            nc.vector.tensor_copy(
-                v_cod[c][:].bitcast(U16).rearrange("p (d j) -> p d j", d=2),
-                got_w[c][:].bitcast(U16).rearrange("p (j d) -> p d j", d=2),
-            )
-
-        def join(s):
-            group = [g for g in GROUPS if s in g][0]
-            if s == group[0]:
-                h_bf[group] = keep.tile([P, len(group) * HC * PACK], BF16, name="h_bf%d" % s, align_bytes=64)
-            h_cols = h_bf[group][:, (s - group[0]) * HC * PACK : (s - group[0] + 1) * HC * PACK]
-            j0 = s * HC
-            vc, vo = divmod(j0, TC)
-            gc, go = divmod(j0, XC)
-            yb = psum_b.tile([P, PACK, HC], F32, name="yb")
-            for t in range(PACK):
-                for a in range(2):
+        def gates_by_step(c, first_bank, tiles):
+            for u in range(2):
+                ya = bank(first_bank + u, "ya%d_%d" % (c, u), [P, PACK, STEP])
+                for t in range(PACK):
                     nc.tensor.matmul_mx(
-                        out=yb[:, t, :],
-                        lhsT=w_cod[:, 1 + a, 2 * P * t : 2 * P * (t + 1)].bitcast(FP4X4),
-                        lhsT_scale=w_scl[:, 1 + a, P * t : P * (t + 1)],
-                        rhs=v_cod[vc][:, 2 * (a * TC + vo) : 2 * (a * TC + vo + HC)].bitcast(FP4X4),
-                        rhs_scale=v_scl[a][:, j0 : j0 + HC],
-                        start=(a == 0),
-                        stop=(a == 1),
-                    )
-            nc.vector.tensor_tensor(
-                h_cols.rearrange("p (c i t) -> p c t i", i=2, t=PACK),
-                yb[:].rearrange("p t (c i) -> p c t i", i=2),
-                gate[gc].rearrange("p (t c i) -> p c t i", t=PACK, i=2)[:, go // 2 : (go + HC) // 2, :, :],
-                MULT,
-            )
-
-        def quantize_h(group):
-            width = len(group) * HC
-            h_cod = keep.tile([P, width], U32, name="h_cod%d" % group[0], align_bytes=64)
-            h_scl = keep.tile([P, width], U8, name="h_scl%d" % group[0], align_bytes=64)
-            nc.vector.quantize_mx(out=h_cod[:].bitcast(FP8X4), scales=h_scl[:], in_=h_bf[group][:])
-            return h_cod, h_scl
-
-        def second_layer(group, h_cod, h_scl):
-            width = len(group) * HC
-            j0 = group[0] * HC
-            per_bank = 2 if group == GROUPS[-1] else PACK * HC // width
-            for m0 in range(0, N // P, per_bank):
-                y = psum_a.tile([P, per_bank, width], F32, name="y", tag="acc")
-                for m in range(m0, m0 + per_bank):
-                    nc.tensor.matmul_mx(
-                        out=y[:, m - m0, :],
-                        lhsT=wd_cod[:, P * m : P * (m + 1)].bitcast(FP8X4),
-                        lhsT_scale=wd_scl[:, P * m : P * (m + 1)],
-                        rhs=h_cod[:].bitcast(FP8X4),
-                        rhs_scale=h_scl[:],
+                        out=ya[:, t, :],
+                        lhsT=w_cod[:, 0, 2 * P * t : 2 * P * (t + 1)].bitcast(FP4X4),
+                        lhsT_scale=wa_scl[:, 0, P * t : P * (t + 1)],
+                        rhs=x_cod[c][:, u * STEP : (u + 1) * STEP].bitcast(FP8X4),
+                        rhs_scale=x_scl[c][:, u * STEP : (u + 1) * STEP],
                         start=True,
                         stop=True,
                     )
-                y_sb = keep.tile([P, per_bank, width], F32, name="y_sb%d_%d" % (group[0], m0), align_bytes=64)
-                if group == GROUPS[-1] and m0 > 0:
-                    nc.vector.tensor_copy(y_sb[:], y[:])
-                else:
-                    nc.scalar.copy(y_sb[:], y[:])
-                nc.sync.dma_start(out_rows[:, m0 : m0 + per_bank, j0 : j0 + width], y_sb[:])
+                nc.scalar.activation(tiles[u][:], ya[:].rearrange("p t j -> p (t j)"), SILU)
+                step_gate[2 * c + u] = tiles[u][:].rearrange("p (t c i) -> p c t i", t=PACK, i=2)
 
-        turned = psum_a.tile([P, P], F32, name="turned", tag="acc")
+        def gather_words(half):
+            got_w[half] = sb("got_w%d" % half, [P, HALF], U32)
+            entries = lst[:, half * HALF // GROUP : (half + 1) * HALF // GROUP]
+            nc.vector.tensor_copy(got_w[half][:], tab_w[:].bitcast(U32).indirect(entries))
+
+        def part_words(half):
+            v_cod[half] = sb("v_cod%d" % half, [P, 4 * HALF], U8)
+            nc.vector.tensor_copy(
+                v_cod[half][:].bitcast(U16).rearrange("p (d j) -> p d j", d=2),
+                got_w[half][:].bitcast(U16).rearrange("p (j d) -> p d j", d=2),
+            )
+
+        def round_wd(u):
+            nc.scalar.copy(
+                wd_bf[:, u * CHUNK * PACK : (u + 1) * CHUNK * PACK].rearrange("p (c i t) -> p c t i", i=2, t=PACK),
+                wd_raw[:, :, u * CHUNK : (u + 1) * CHUNK].rearrange("p t (c i) -> p c t i", i=2),
+            )
+
+        def memory_sums(s):
+            half, first = divmod(s * STEP, HALF)
+            yb[s] = bank(4 + s % 4, "yb%d" % s, [P, PACK, STEP])
+            for t in range(PACK):
+                for a in range(2):
+                    nc.tensor.matmul_mx(
+                        out=yb[s][:, t, :],
+                        lhsT=w_cod[:, 1 + a, 2 * P * t : 2 * P * (t + 1)].bitcast(FP4X4),
+                        lhsT_scale=wb_scl[:, a, P * t : P * (t + 1)],
+                        rhs=v_cod[half][:, 2 * (a * HALF + first) : 2 * (a * HALF + first + STEP)].bitcast(FP4X4),
+                        rhs_scale=v_scl[:, a, s * STEP : (s + 1) * STEP],
+                        start=(a == 0),
+                        stop=(a == 1),
+                    )
+
+        def join(s):
+            c, u = divmod(s, 2)
+            if u == 0:
+                h_bf[c] = sb("h_bf%d" % c, [P, CHUNK * PACK], BF16)
+            nc.vector.tensor_tensor(
+                h_bf[c][:, u * STEP * PACK : (u + 1) * STEP * PACK].rearrange("p (c i t) -> p c t i", i=2, t=PACK),
+                yb[s][:].rearrange("p t (c i) -> p c t i", i=2),
+                step_gate[s],
+                MULT,
+            )
+
+        def quantize_h(c, j0, j1):
+            nc.vector.quantize_mx(
+                out=h_cod[c][:, j0:j1].bitcast(FP8X4),
+                scales=h_scl[c][:, j0:j1],
+                in_=h_bf[c][:, j0 * PACK : j1 * PACK],
+            )
+
+        def second_layer(c, first_bank, pieces, engines):
+            banks = [bank(first_bank + u, "y%d_%d" % (c, u), [P, 2, CHUNK]) for u in range(2)]
+            for j0, j1 in pieces:
+                for m in range(N // P):
+                    nc.tensor.matmul_mx(
+                        out=banks[m // 2][:, m % 2, j0:j1],
+                        lhsT=wd_cod[:, P * m : P * (m + 1)].bitcast(FP8X4),
+                        lhsT_scale=wd_scl[:, P * m : P * (m + 1)],
+                        rhs=h_cod[c][:, j0:j1].bitcast(FP8X4),
+                        rhs_scale=h_scl[c][:, j0:j1],
+                        start=True,
+                        stop=True,
+                    )
+            for u in range(2):
+                y_sb = sb("y_sb%d_%d" % (c, u), [P, 2, CHUNK], F32)
+                engines[u](y_sb[:], banks[u][:])
+                nc.sync.dma_start(out_rows[:, 2 * u : 2 * u + 2, c * CHUNK : (c + 1) * CHUNK], y_sb[:])
+
+        def last_outputs(c, bank_numbers):
+            banks = [bank(number, "y%d_%d" % (c, m), [P, CHUNK]) for m, number in enumerate(bank_numbers)]
+            for u in range(2):
+                for m in (0, 2, 1, 3):
+                    nc.tensor.matmul_mx(
+                        out=banks[m][:, u * STEP : (u + 1) * STEP],
+                        lhsT=wd_cod[:, P * m : P * (m + 1)].bitcast(FP8X4),
+                        lhsT_scale=wd_scl[:, P * m : P * (m + 1)],
+                        rhs=h_cod[c][:, u * STEP : (u + 1) * STEP].bitcast(FP8X4),
+                        rhs_scale=h_scl[c][:, u * STEP : (u + 1) * STEP],
+                        start=True,
+                        stop=True,
+                    )
+            for m in (0, 2, 1, 3):
+                y_sb = sb("y_sb%d_%d" % (c, m), [P, CHUNK], F32)
+                (nc.scalar.copy if m < 2 else nc.vector.tensor_copy)(y_sb[:], banks[m][:])
+                nc.sync.dma_start(out_rows[:, m, c * CHUNK : (c + 1) * CHUNK], y_sb[:])
+
+        turned = bank(6, "turned", [P, P])
         nc.tensor.transpose(turned[:], wgt_rows[:], ident[:])
-        for c0, c1 in ((0, 2), (2, 4), (4, 8)):
+        pieces = ((0, 2), (2, 4), (4, 8))
+        for c0, c1 in pieces:
             nc.scalar.copy(
                 wgt_cols[:, c0:c1, :].rearrange("p c (g r) -> p (c g) r", r=GROUP),
                 turned[:, 8 * c0 : 8 * c1].unsqueeze(2).to_broadcast([P, 8 * (c1 - c0), GROUP]),
             )
-        for c0, c1 in ((0, 2), (2, 4), (4, 8)):
-            spread = psum_a.tile([P, c1 - c0, P], F32, name="spread", tag="acc")
+        for number, (c0, c1) in enumerate(pieces):
+            spread = bank(number, "spread%d" % number, [P, c1 - c0, P])
             for c in range(c0, c1):
                 nc.tensor.transpose(spread[:, c - c0, :], wgt_cols[:, c, :], ident[:])
             nc.scalar.copy(wgt[:, c0 * P : c1 * P], spread[:].rearrange("p c j -> p (c j)"))
 
-        nc.vector.tensor_copy(got_s[:], tab_s[:].indirect(lst[:]))
-        move_scale_rows(range(8))
+        w_cod = sb_at("w_cod", [P, 3, 2 * R], U8, 11264)
+        wb_scl = sb_at("wb_scl", [P, 2, R], U8, 14336)
+        order_columns(w_cod, w_raw, 4)
+        order_columns(wb_scl, wbs_raw, 2)
         for half in range(2):
-            gather_x(0, half * TC, (half + 1) * TC)
-        for i in range(1, PACK - 1):
-            gather_x(i, 0, J)
-        for c in range(2):
-            gather_x(3, c * XC, (c + 1) * XC)
-            round_x(c)
-        gather_x(3, TC, J)
-        for c in range(2, 4):
-            round_x(c)
-        order_columns()
-        for c in range(2):
-            quantize_x(c)
-            gates(c)
+            gather_x(0, half * HALF, (half + 1) * HALF)
+        gather_x(1, 0, J)
+        x_bf[0] = sb_at("x_bf0", [P, CHUNK * PACK], BF16, 9216)
+        for c in range(1, 4):
+            x_bf[c] = sb("x_bf%d" % c, [P, CHUNK * PACK], BF16)
+        for c in range(4):
+            round_x(c, 0)
+        order_columns(wa_scl, was_raw, 2)
+        gather_x(2, 0, J)
+        for half in range(2):
+            gather_x(3, half * HALF, (half + 1) * HALF)
+            for c in range(2 * half, 2 * half + 2):
+                round_x(c, 2)
+
+        for c in range(4):
+            h_scl[c] = sb("h_scl%d" % c, [P, CHUNK], U8)
+        for c in range(1, 4):
+            h_cod[c] = sb("h_cod%d" % c, [P, CHUNK], U32)
+        first_gates = (sb_at("gate_step0", [P, PACK * STEP], F32, 15360), sb("gate_step1", [P, PACK * STEP], F32))
+        gate[3] = sb("gate3", [P, PACK * CHUNK], F32)
+        scalar_pair = (nc.scalar.copy, nc.scalar.copy)
+        whole = ((0, CHUNK),)
+
+        quantize_x(0)
+        gates_by_step(0, 0, first_gates)
+        quantize_x(1)
         gather_words(0)
-        for u in range(N // WC):
+        quantize_x(2)
+        part_words(0)
+        quantize_x(3)
+        for u in range(2):
             round_wd(u)
-        for c in range(2, 4):
-            quantize_x(c)
-            gates(c)
-        part_words(0, "v_cod0")
+        gate[1] = sb_at("gate1", [P, PACK * CHUNK], F32, 1024)
+        gate[2] = sb_at("gate2", [P, PACK * CHUNK], F32, 5120)
+        gates(1, 2)
+        for s in range(4):
+            memory_sums(s)
+        gates(2, 0)
         gather_words(1)
-        part_words(1, "v_cod1")
-        for s in GROUPS[0]:
-            join(s)
+        join(0)
+        part_words(1)
+        memory_sums(4)
+        join(1)
+        memory_sums(5)
+        wd_cod = sb_at("wd_cod", [P, N], U32, 15360)
         nc.vector.quantize_mx(out=wd_cod[:].bitcast(FP8X4), scales=wd_scl[:], in_=wd_bf[:])
-        second_layer(GROUPS[0], *quantize_h(GROUPS[0]))
-        for s in range(len(GROUPS[0]), J // HC):
-            join(s)
-            for group in GROUPS[1:]:
-                if group[-1] == s - 1:
-                    second_layer(group, *quantize_h(group))
-        second_layer(GROUPS[-1], *quantize_h(GROUPS[-1]))
+        h_cod[0] = sb_at("h_cod0", [P, CHUNK], U32, 0)
+        quantize_h(0, 0, CHUNK)
+        second_layer(0, 2, whole, scalar_pair)
+        gates(3, 0)
+        join(2)
+        memory_sums(6)
+        join(3)
+        memory_sums(7)
+        join(4)
+        quantize_h(1, 0, CHUNK)
+        second_layer(1, 2, whole, scalar_pair)
+        join(5)
+        join(6)
+        quantize_h(2, 0, CHUNK)
+        second_layer(2, 4, whole, scalar_pair)
+        join(7)
+        for u in range(2):
+            quantize_h(3, u * STEP, (u + 1) * STEP)
+        last_outputs(3, (0, 1, 6, 2))

@@ -51,7 +51,8 @@ def tile_list_htabg_glu_none_kernel(
         got_x = sb("got_x", [P, PACK, J], F32)
         x_pl = [sb("x_pl%d" % i, [P, T], F32) for i in range(PACK)]
         wd_raw = sb_at("wd_raw", [P, PACK, N], F32, 960)
-        w_raw = sb("w_raw", [P, 3, 2 * R], U8)
+        wa_raw = sb("wa_raw", [P, 1, 2 * R], U8)
+        wb_raw = sb_at("wb_raw", [P, 2, 2 * R], U8, 18432)
         was_raw = sb("was_raw", [P, 1, R], U8)
         wbs_raw = sb_at("wbs_raw", [P, 2, R], U8, 9216)
         wa_scl = sb("wa_scl", [P, 1, R], U8)
@@ -87,23 +88,22 @@ def tile_list_htabg_glu_none_kernel(
 
         def move_scale_rows(q0, q1):
             for q in range(q0, q1):
-                nc.sync.dma_start(v_scl[32 * q : 32 * q + 4, :, :].bitcast(I32), got_s[8 * q : 8 * q + 8, :].bitcast(I32))
+                nc.gpsimd.dma_start(v_scl[32 * q : 32 * q + 4, :, :].bitcast(I32), got_s[8 * q : 8 * q + 8, :].bitcast(I32))
 
         nc.sync.dma_start(wgt_rows[0:64, :], wgt2.rearrange("(g r) (c j) -> r c g j", r=GROUP, j=P)[0])
         nc.sync.dma_start(tab_s[0:32, :].bitcast(I32), tab_scales.rearrange("a q t -> q a t").bitcast(I32))
         nc.sync.dma_start(lst[:], offs)
         nc.sync.dma_start(x_pl[0][:], x_rows[0])
         nc.sync.dma_start(lst2[:], offs2)
-        nc.sync.dma_start(w_raw[:, 0, :].bitcast(I32), wa_words[0].bitcast(I32))
-        nc.sync.dma_start(w_raw[:, 1:3, :].bitcast(I32), wb_words.rearrange("a p c -> p a c").bitcast(I32))
         nc.sync.dma_start(x_pl[1][:], x_rows[1])
         nc.vector.tensor_copy(got_s[:], tab_s[:].indirect(lst[:]))
+        move_scale_rows(0, 4)
         load_scale_rows(wbs_raw, wb_scales)
-        move_scale_rows(0, 2)
         nc.sync.dma_start(x_pl[2][:], x_rows[2])
         load_scale_rows(was_raw, wa_scales)
-        move_scale_rows(2, 4)
         nc.sync.dma_start(x_pl[3][:], x_rows[3])
+        nc.sync.dma_start(wb_raw[:].bitcast(I32), wb_words.rearrange("a p c -> p a c").bitcast(I32))
+        nc.sync.dma_start(wa_raw[:].bitcast(I32), wa_words.rearrange("a p c -> p a c").bitcast(I32))
         nc.sync.dma_start(tab_w[:], tab_words[0].rearrange("p t b -> p (t b)").bitcast(I32))
         for t in range(PACK):
             nc.sync.dma_start(wd_raw[:, t, :], wd_rows[t])
@@ -123,10 +123,10 @@ def tile_list_htabg_glu_none_kernel(
             entries = lst2[:, j0 // GROUP : j1 // GROUP]
             nc.vector.tensor_tensor(got_x[:, i, j0:j1], x_pl[i][:].indirect(entries), wgt[:, j0:j1], MULT)
 
-        def round_x(c, t0):
+        def round_x(c, t0, t1):
             nc.scalar.copy(
-                x_bf[c][:].rearrange("p (c i t) -> p c t i", i=2, t=PACK)[:, :, t0 : t0 + 2, :],
-                got_x[:, t0 : t0 + 2, c * CHUNK : (c + 1) * CHUNK].rearrange("p t (c i) -> p c t i", i=2),
+                x_bf[c][:].rearrange("p (c i t) -> p c t i", i=2, t=PACK)[:, :, t0:t1, :],
+                got_x[:, t0:t1, c * CHUNK : (c + 1) * CHUNK].rearrange("p t (c i) -> p c t i", i=2),
             )
 
         def quantize_x(c):
@@ -140,7 +140,7 @@ def tile_list_htabg_glu_none_kernel(
                 for t in range(2 * u, 2 * u + 2):
                     nc.tensor.matmul_mx(
                         out=ya[:, t - 2 * u, :],
-                        lhsT=w_cod[:, 0, 2 * P * t : 2 * P * (t + 1)].bitcast(FP4X4),
+                        lhsT=wa_cod[:, 0, 2 * P * t : 2 * P * (t + 1)].bitcast(FP4X4),
                         lhsT_scale=wa_scl[:, 0, P * t : P * (t + 1)],
                         rhs=x_cod[c][:].bitcast(FP8X4),
                         rhs_scale=x_scl[c][:],
@@ -160,7 +160,7 @@ def tile_list_htabg_glu_none_kernel(
                 for t in range(PACK):
                     nc.tensor.matmul_mx(
                         out=ya[:, t, :],
-                        lhsT=w_cod[:, 0, 2 * P * t : 2 * P * (t + 1)].bitcast(FP4X4),
+                        lhsT=wa_cod[:, 0, 2 * P * t : 2 * P * (t + 1)].bitcast(FP4X4),
                         lhsT_scale=wa_scl[:, 0, P * t : P * (t + 1)],
                         rhs=x_cod[c][:, u * STEP : (u + 1) * STEP].bitcast(FP8X4),
                         rhs_scale=x_scl[c][:, u * STEP : (u + 1) * STEP],
@@ -195,7 +195,7 @@ def tile_list_htabg_glu_none_kernel(
                 for a in range(2):
                     nc.tensor.matmul_mx(
                         out=yb[s][:, t, :],
-                        lhsT=w_cod[:, 1 + a, 2 * P * t : 2 * P * (t + 1)].bitcast(FP4X4),
+                        lhsT=wb_cod[:, a, 2 * P * t : 2 * P * (t + 1)].bitcast(FP4X4),
                         lhsT_scale=wb_scl[:, a, P * t : P * (t + 1)],
                         rhs=v_cod[half][:, 2 * (a * HALF + first) : 2 * (a * HALF + first + STEP)].bitcast(FP4X4),
                         rhs_scale=v_scl[:, a, s * STEP : (s + 1) * STEP],
@@ -271,24 +271,27 @@ def tile_list_htabg_glu_none_kernel(
                 nc.tensor.transpose(spread[:, c - c0, :], wgt_cols[:, c, :], ident[:])
             nc.scalar.copy(wgt[:, c0 * P : c1 * P], spread[:].rearrange("p c j -> p (c j)"))
 
-        w_cod = sb_at("w_cod", [P, 3, 2 * R], U8, 11264)
+        wa_cod = sb("wa_cod", [P, 1, 2 * R], U8)
+        wb_cod = sb("wb_cod", [P, 2, 2 * R], U8)
         wb_scl = sb_at("wb_scl", [P, 2, R], U8, 14336)
-        order_columns(w_cod, w_raw, 4)
         order_columns(wb_scl, wbs_raw, 2)
         for half in range(2):
             gather_x(0, half * HALF, (half + 1) * HALF)
         gather_x(1, 0, J)
-        x_bf[0] = sb_at("x_bf0", [P, CHUNK * PACK], BF16, 9216)
-        for c in range(1, 4):
+        for c in range(2, 4):
             x_bf[c] = sb("x_bf%d" % c, [P, CHUNK * PACK], BF16)
-        for c in range(4):
-            round_x(c, 0)
+            round_x(c, 0, 2)
         order_columns(wa_scl, was_raw, 2)
+        order_columns(wb_cod, wb_raw, 4)
+        order_columns(wa_cod, wa_raw, 4)
         gather_x(2, 0, J)
-        for half in range(2):
-            gather_x(3, half * HALF, (half + 1) * HALF)
-            for c in range(2 * half, 2 * half + 2):
-                round_x(c, 2)
+        for c in range(2):
+            x_bf[c] = sb_at("x_bf%d" % c, [P, CHUNK * PACK], BF16, 17408 + 2048 * c)
+            gather_x(3, c * CHUNK, (c + 1) * CHUNK)
+            round_x(c, 0, PACK)
+        gather_x(3, HALF, J)
+        for c in range(2, 4):
+            round_x(c, 2, PACK)
 
         for c in range(4):
             h_scl[c] = sb("h_scl%d" % c, [P, CHUNK], U8)

@@ -51,11 +51,10 @@ def tile_list_htabg_glu_none_kernel(
         got_x = sb("got_x", [P, PACK, J], F32)
         x_pl = [sb("x_pl%d" % i, [P, T], F32) for i in range(PACK)]
         wd_raw = sb_at("wd_raw", [P, PACK, N], F32, 960)
-        wa_raw = sb("wa_raw", [P, 1, 2 * R], U8)
-        wb_raw = sb_at("wb_raw", [P, 2, 2 * R], U8, 18432)
-        was_raw = sb("was_raw", [P, 1, R], U8)
-        wbs_raw = sb_at("wbs_raw", [P, 2, R], U8, 9216)
-        wa_scl = sb("wa_scl", [P, 1, R], U8)
+        w_raw = sb("w_raw", [P, 3, 2 * R], U8)
+        ws_raw = sb("ws_raw", [P, 3, R], U8)
+        w_scl = sb("w_scl", [P, 3, R], U8)
+        w_cod = sb("w_cod", [P, 3, 2 * R], U8)
         wd_bf = sb("wd_bf", [P, N * PACK], BF16)
         wd_scl = sb("wd_scl", [P, N], U8)
         got_s = sb("got_s", [P, J], U8)
@@ -68,8 +67,7 @@ def tile_list_htabg_glu_none_kernel(
 
         make_identity(nc, ident[:])
         nc.vector.memset(wgt_rows[64:128, :], 0.0)
-        nc.vector.memset(wbs_raw[:].rearrange("p a r -> p (a r)").bitcast(I32), 0)
-        nc.vector.memset(was_raw[:].rearrange("p a r -> p (a r)").bitcast(I32), 0)
+        nc.vector.memset(ws_raw[:].rearrange("p a r -> p (a r)").bitcast(I32), 0)
         nc.vector.memset(warm[:], 0.0)
         nc.vector.memset(tab_s[32:64, :].bitcast(I32), 0)
         nc.vector.memset(tab_s[64:128, :].bitcast(I32), 0)
@@ -79,10 +77,10 @@ def tile_list_htabg_glu_none_kernel(
         x_rows = xT.rearrange("(p i) t -> i p t", i=PACK)
         wd_rows = wd.rearrange("(b t q) n -> t b q n", t=PACK, q=8)
 
-        def load_scale_rows(tile, scales):
+        def load_scale_rows(a0, a1, scales):
             for q in range(4):
                 nc.sync.dma_start(
-                    tile[32 * q : 32 * q + 4, :, :].bitcast(I32),
+                    ws_raw[32 * q : 32 * q + 4, a0:a1, :].bitcast(I32),
                     scales[:, 4 * q : 4 * q + 4, :].rearrange("a q r -> q a r").bitcast(I32),
                 )
 
@@ -98,12 +96,12 @@ def tile_list_htabg_glu_none_kernel(
         nc.sync.dma_start(x_pl[1][:], x_rows[1])
         nc.vector.tensor_copy(got_s[:], tab_s[:].indirect(lst[:]))
         move_scale_rows(0, 4)
-        load_scale_rows(wbs_raw, wb_scales)
+        load_scale_rows(1, 3, wb_scales)
         nc.sync.dma_start(x_pl[2][:], x_rows[2])
-        load_scale_rows(was_raw, wa_scales)
+        load_scale_rows(0, 1, wa_scales)
         nc.sync.dma_start(x_pl[3][:], x_rows[3])
-        nc.sync.dma_start(wb_raw[:].bitcast(I32), wb_words.rearrange("a p c -> p a c").bitcast(I32))
-        nc.sync.dma_start(wa_raw[:].bitcast(I32), wa_words.rearrange("a p c -> p a c").bitcast(I32))
+        nc.sync.dma_start(w_raw[:, 0, :].bitcast(I32), wa_words[0].bitcast(I32))
+        nc.sync.dma_start(w_raw[:, 1:3, :].bitcast(I32), wb_words.rearrange("a p c -> p a c").bitcast(I32))
         nc.sync.dma_start(tab_w[:], tab_words[0].rearrange("p t b -> p (t b)").bitcast(I32))
         for t in range(PACK):
             nc.sync.dma_start(wd_raw[:, t, :], wd_rows[t])
@@ -114,9 +112,9 @@ def tile_list_htabg_glu_none_kernel(
         step_gate = {}
 
         def order_columns(ordered, raw, words):
-            nc.scalar.copy(
-                ordered[:].bitcast(U32).rearrange("p a (t b w) -> p a t b w", t=PACK, w=words),
-                raw[:].bitcast(U32).rearrange("p a (b t w) -> p a t b w", t=PACK, w=words),
+            nc.vector.tensor_copy(
+                ordered[:].bitcast(I32).rearrange("p a (t b w) -> p t a b w", t=PACK, w=words),
+                raw[:].bitcast(I32).rearrange("p a (b t w) -> p t a b w", t=PACK, w=words),
             )
 
         def gather_x(i, j0, j1):
@@ -140,8 +138,8 @@ def tile_list_htabg_glu_none_kernel(
                 for t in range(2 * u, 2 * u + 2):
                     nc.tensor.matmul_mx(
                         out=ya[:, t - 2 * u, :],
-                        lhsT=wa_cod[:, 0, 2 * P * t : 2 * P * (t + 1)].bitcast(FP4X4),
-                        lhsT_scale=wa_scl[:, 0, P * t : P * (t + 1)],
+                        lhsT=w_cod[:, 0, 2 * P * t : 2 * P * (t + 1)].bitcast(FP4X4),
+                        lhsT_scale=w_scl[:, 0, P * t : P * (t + 1)],
                         rhs=x_cod[c][:].bitcast(FP8X4),
                         rhs_scale=x_scl[c][:],
                         start=True,
@@ -160,8 +158,8 @@ def tile_list_htabg_glu_none_kernel(
                 for t in range(PACK):
                     nc.tensor.matmul_mx(
                         out=ya[:, t, :],
-                        lhsT=wa_cod[:, 0, 2 * P * t : 2 * P * (t + 1)].bitcast(FP4X4),
-                        lhsT_scale=wa_scl[:, 0, P * t : P * (t + 1)],
+                        lhsT=w_cod[:, 0, 2 * P * t : 2 * P * (t + 1)].bitcast(FP4X4),
+                        lhsT_scale=w_scl[:, 0, P * t : P * (t + 1)],
                         rhs=x_cod[c][:, u * STEP : (u + 1) * STEP].bitcast(FP8X4),
                         rhs_scale=x_scl[c][:, u * STEP : (u + 1) * STEP],
                         start=True,
@@ -195,8 +193,8 @@ def tile_list_htabg_glu_none_kernel(
                 for a in range(2):
                     nc.tensor.matmul_mx(
                         out=yb[s][:, t, :],
-                        lhsT=wb_cod[:, a, 2 * P * t : 2 * P * (t + 1)].bitcast(FP4X4),
-                        lhsT_scale=wb_scl[:, a, P * t : P * (t + 1)],
+                        lhsT=w_cod[:, 1 + a, 2 * P * t : 2 * P * (t + 1)].bitcast(FP4X4),
+                        lhsT_scale=w_scl[:, 1 + a, P * t : P * (t + 1)],
                         rhs=v_cod[half][:, 2 * (a * HALF + first) : 2 * (a * HALF + first + STEP)].bitcast(FP4X4),
                         rhs_scale=v_scl[:, a, s * STEP : (s + 1) * STEP],
                         start=(a == 0),
@@ -271,22 +269,15 @@ def tile_list_htabg_glu_none_kernel(
                 nc.tensor.transpose(spread[:, c - c0, :], wgt_cols[:, c, :], ident[:])
             nc.scalar.copy(wgt[:, c0 * P : c1 * P], spread[:].rearrange("p c j -> p (c j)"))
 
-        wa_cod = sb("wa_cod", [P, 1, 2 * R], U8)
-        wb_cod = sb("wb_cod", [P, 2, 2 * R], U8)
-        wb_scl = sb_at("wb_scl", [P, 2, R], U8, 14336)
-        order_columns(wb_scl, wbs_raw, 2)
         for half in range(2):
             gather_x(0, half * HALF, (half + 1) * HALF)
         gather_x(1, 0, J)
         for c in range(2, 4):
             x_bf[c] = sb("x_bf%d" % c, [P, CHUNK * PACK], BF16)
             round_x(c, 0, 2)
-        order_columns(wa_scl, was_raw, 2)
-        order_columns(wb_cod, wb_raw, 4)
-        order_columns(wa_cod, wa_raw, 4)
         gather_x(2, 0, J)
         for c in range(2):
-            x_bf[c] = sb_at("x_bf%d" % c, [P, CHUNK * PACK], BF16, 17408 + 2048 * c)
+            x_bf[c] = sb("x_bf%d" % c, [P, CHUNK * PACK], BF16)
             gather_x(3, c * CHUNK, (c + 1) * CHUNK)
             round_x(c, 0, PACK)
         gather_x(3, HALF, J)
@@ -302,6 +293,8 @@ def tile_list_htabg_glu_none_kernel(
         scalar_pair = (nc.scalar.copy, nc.scalar.copy)
         whole = ((0, CHUNK),)
 
+        order_columns(w_cod, w_raw, 4)
+        order_columns(w_scl, ws_raw, 2)
         quantize_x(0)
         gates_by_step(0, 0, first_gates)
         quantize_x(1)

@@ -52,8 +52,10 @@ def tile_list_htabg_glu_none_kernel(
         x_pl = [sb("x_pl%d" % i, [P, T], F32) for i in range(PACK)]
         wd_raw = sb_at("wd_raw", [P, PACK, N], F32, 960)
         w_raw = sb("w_raw", [P, 3, 2 * R], U8)
-        ws_raw = sb("ws_raw", [P, 3, R], U8)
-        w_scl = sb("w_scl", [P, 3, R], U8)
+        was_raw = sb("was_raw", [P, 1, R], U8)
+        wbs_raw = sb("wbs_raw", [P, 2, R], U8)
+        wa_scl = sb("wa_scl", [P, 1, R], U8)
+        wb_scl = sb("wb_scl", [P, 2, R], U8)
         w_cod = sb("w_cod", [P, 3, 2 * R], U8)
         wd_bf = sb("wd_bf", [P, N * PACK], BF16)
         wd_scl = sb("wd_scl", [P, N], U8)
@@ -67,7 +69,8 @@ def tile_list_htabg_glu_none_kernel(
 
         make_identity(nc, ident[:])
         nc.vector.memset(wgt_rows[64:128, :], 0.0)
-        nc.vector.memset(ws_raw[:].rearrange("p a r -> p (a r)").bitcast(I32), 0)
+        nc.vector.memset(was_raw[:].rearrange("p a r -> p (a r)").bitcast(I32), 0)
+        nc.vector.memset(wbs_raw[:].rearrange("p a r -> p (a r)").bitcast(I32), 0)
         nc.vector.memset(warm[:], 0.0)
         nc.vector.memset(tab_s[32:64, :].bitcast(I32), 0)
         nc.vector.memset(tab_s[64:128, :].bitcast(I32), 0)
@@ -77,17 +80,19 @@ def tile_list_htabg_glu_none_kernel(
         x_rows = xT.rearrange("(p i) t -> i p t", i=PACK)
         wd_rows = wd.rearrange("(b t q) n -> t b q n", t=PACK, q=8)
 
-        def load_scale_rows(a0, a1, scales):
+        def load_scale_rows(tile, scales):
             for q in range(4):
-                nc.sync.dma_start(
-                    ws_raw[32 * q : 32 * q + 4, a0:a1, :].bitcast(I32),
+                nc.gpsimd.dma_start(
+                    tile[32 * q : 32 * q + 4, :, :].bitcast(I32),
                     scales[:, 4 * q : 4 * q + 4, :].rearrange("a q r -> q a r").bitcast(I32),
                 )
 
         def move_scale_rows(q0, q1):
             for q in range(q0, q1):
-                nc.gpsimd.dma_start(v_scl[32 * q : 32 * q + 4, :, :].bitcast(I32), got_s[8 * q : 8 * q + 8, :].bitcast(I32))
+                nc.sync.dma_start(v_scl[32 * q : 32 * q + 4, :, :].bitcast(I32), got_s[8 * q : 8 * q + 8, :].bitcast(I32))
 
+        load_scale_rows(was_raw, wa_scales)
+        load_scale_rows(wbs_raw, wb_scales)
         nc.sync.dma_start(wgt_rows[0:64, :], wgt2.rearrange("(g r) (c j) -> r c g j", r=GROUP, j=P)[0])
         nc.sync.dma_start(tab_s[0:32, :].bitcast(I32), tab_scales.rearrange("a q t -> q a t").bitcast(I32))
         nc.sync.dma_start(lst[:], offs)
@@ -95,16 +100,14 @@ def tile_list_htabg_glu_none_kernel(
         nc.sync.dma_start(lst2[:], offs2)
         nc.sync.dma_start(x_pl[1][:], x_rows[1])
         nc.vector.tensor_copy(got_s[:], tab_s[:].indirect(lst[:]))
-        move_scale_rows(0, 4)
-        load_scale_rows(1, 3, wb_scales)
         nc.sync.dma_start(x_pl[2][:], x_rows[2])
-        load_scale_rows(0, 1, wa_scales)
         nc.sync.dma_start(x_pl[3][:], x_rows[3])
         nc.sync.dma_start(w_raw[:, 0, :].bitcast(I32), wa_words[0].bitcast(I32))
         nc.sync.dma_start(w_raw[:, 1:3, :].bitcast(I32), wb_words.rearrange("a p c -> p a c").bitcast(I32))
         nc.sync.dma_start(tab_w[:], tab_words[0].rearrange("p t b -> p (t b)").bitcast(I32))
         for t in range(PACK):
             nc.sync.dma_start(wd_raw[:, t, :], wd_rows[t])
+        move_scale_rows(0, 4)
 
         out_rows = out.rearrange("(m p) j -> p m j", p=P)
         x_bf, x_cod, x_scl, gate, got_w, v_cod, yb, h_bf, h_cod, h_scl = {}, {}, {}, {}, {}, {}, {}, {}, {}, {}
@@ -139,7 +142,7 @@ def tile_list_htabg_glu_none_kernel(
                     nc.tensor.matmul_mx(
                         out=ya[:, t - 2 * u, :],
                         lhsT=w_cod[:, 0, 2 * P * t : 2 * P * (t + 1)].bitcast(FP4X4),
-                        lhsT_scale=w_scl[:, 0, P * t : P * (t + 1)],
+                        lhsT_scale=wa_scl[:, 0, P * t : P * (t + 1)],
                         rhs=x_cod[c][:].bitcast(FP8X4),
                         rhs_scale=x_scl[c][:],
                         start=True,
@@ -159,7 +162,7 @@ def tile_list_htabg_glu_none_kernel(
                     nc.tensor.matmul_mx(
                         out=ya[:, t, :],
                         lhsT=w_cod[:, 0, 2 * P * t : 2 * P * (t + 1)].bitcast(FP4X4),
-                        lhsT_scale=w_scl[:, 0, P * t : P * (t + 1)],
+                        lhsT_scale=wa_scl[:, 0, P * t : P * (t + 1)],
                         rhs=x_cod[c][:, u * STEP : (u + 1) * STEP].bitcast(FP8X4),
                         rhs_scale=x_scl[c][:, u * STEP : (u + 1) * STEP],
                         start=True,
@@ -194,7 +197,7 @@ def tile_list_htabg_glu_none_kernel(
                     nc.tensor.matmul_mx(
                         out=yb[s][:, t, :],
                         lhsT=w_cod[:, 1 + a, 2 * P * t : 2 * P * (t + 1)].bitcast(FP4X4),
-                        lhsT_scale=w_scl[:, 1 + a, P * t : P * (t + 1)],
+                        lhsT_scale=wb_scl[:, a, P * t : P * (t + 1)],
                         rhs=v_cod[half][:, 2 * (a * HALF + first) : 2 * (a * HALF + first + STEP)].bitcast(FP4X4),
                         rhs_scale=v_scl[:, a, s * STEP : (s + 1) * STEP],
                         start=(a == 0),
@@ -294,14 +297,14 @@ def tile_list_htabg_glu_none_kernel(
         whole = ((0, CHUNK),)
 
         order_columns(w_cod, w_raw, 4)
-        order_columns(w_scl, ws_raw, 2)
+        order_columns(wa_scl, was_raw, 2)
         quantize_x(0)
         gates_by_step(0, 0, first_gates)
         quantize_x(1)
         gather_words(0)
         quantize_x(2)
+        order_columns(wb_scl, wbs_raw, 2)
         part_words(0)
-        quantize_x(3)
         for u in range(2):
             round_wd(u)
         gate[1] = sb_at("gate1", [P, PACK * CHUNK], F32, 1024)
@@ -311,8 +314,9 @@ def tile_list_htabg_glu_none_kernel(
             memory_sums(s)
         gates(2, 0)
         gather_words(1)
-        join(0)
+        quantize_x(3)
         part_words(1)
+        join(0)
         memory_sums(4)
         join(1)
         memory_sums(5)

@@ -51,12 +51,11 @@ def tile_list_htabg_glu_none_kernel(
         got_x = sb("got_x", [P, PACK, J], F32)
         x_pl = [sb("x_pl%d" % i, [P, T], F32) for i in range(PACK)]
         wd_raw = sb_at("wd_raw", [P, PACK, N], F32, 960)
-        w_raw = sb("w_raw", [P, 3, 2 * R], U8)
+        wa_raw = sb("wa_raw", [P, 1, 2 * R], U8)
+        wb_raw = sb_at("wb_raw", [P, 2, 2 * R], U8, 18432)
         was_raw = sb("was_raw", [P, 1, R], U8)
-        wbs_raw = sb("wbs_raw", [P, 2, R], U8)
+        wbs_raw = sb_at("wbs_raw", [P, 2, R], U8, 9216)
         wa_scl = sb("wa_scl", [P, 1, R], U8)
-        wb_scl = sb("wb_scl", [P, 2, R], U8)
-        w_cod = sb("w_cod", [P, 3, 2 * R], U8)
         wd_bf = sb("wd_bf", [P, N * PACK], BF16)
         wd_scl = sb("wd_scl", [P, N], U8)
         got_s = sb("got_s", [P, J], U8)
@@ -69,8 +68,8 @@ def tile_list_htabg_glu_none_kernel(
 
         make_identity(nc, ident[:])
         nc.vector.memset(wgt_rows[64:128, :], 0.0)
-        nc.vector.memset(was_raw[:].rearrange("p a r -> p (a r)").bitcast(I32), 0)
         nc.vector.memset(wbs_raw[:].rearrange("p a r -> p (a r)").bitcast(I32), 0)
+        nc.vector.memset(was_raw[:].rearrange("p a r -> p (a r)").bitcast(I32), 0)
         nc.vector.memset(warm[:], 0.0)
         nc.vector.memset(tab_s[32:64, :].bitcast(I32), 0)
         nc.vector.memset(tab_s[64:128, :].bitcast(I32), 0)
@@ -91,8 +90,8 @@ def tile_list_htabg_glu_none_kernel(
             for q in range(q0, q1):
                 nc.sync.dma_start(v_scl[32 * q : 32 * q + 4, :, :].bitcast(I32), got_s[8 * q : 8 * q + 8, :].bitcast(I32))
 
-        load_scale_rows(was_raw, wa_scales)
         load_scale_rows(wbs_raw, wb_scales)
+        load_scale_rows(was_raw, wa_scales)
         nc.sync.dma_start(wgt_rows[0:64, :], wgt2.rearrange("(g r) (c j) -> r c g j", r=GROUP, j=P)[0])
         nc.sync.dma_start(tab_s[0:32, :].bitcast(I32), tab_scales.rearrange("a q t -> q a t").bitcast(I32))
         nc.sync.dma_start(lst[:], offs)
@@ -102,8 +101,8 @@ def tile_list_htabg_glu_none_kernel(
         nc.vector.tensor_copy(got_s[:], tab_s[:].indirect(lst[:]))
         nc.sync.dma_start(x_pl[2][:], x_rows[2])
         nc.sync.dma_start(x_pl[3][:], x_rows[3])
-        nc.sync.dma_start(w_raw[:, 0, :].bitcast(I32), wa_words[0].bitcast(I32))
-        nc.sync.dma_start(w_raw[:, 1:3, :].bitcast(I32), wb_words.rearrange("a p c -> p a c").bitcast(I32))
+        nc.sync.dma_start(wb_raw[:].bitcast(I32), wb_words.rearrange("a p c -> p a c").bitcast(I32))
+        nc.sync.dma_start(wa_raw[:].bitcast(I32), wa_words.rearrange("a p c -> p a c").bitcast(I32))
         nc.sync.dma_start(tab_w[:], tab_words[0].rearrange("p t b -> p (t b)").bitcast(I32))
         for t in range(PACK):
             nc.sync.dma_start(wd_raw[:, t, :], wd_rows[t])
@@ -115,9 +114,9 @@ def tile_list_htabg_glu_none_kernel(
         step_gate = {}
 
         def order_columns(ordered, raw, words):
-            nc.vector.tensor_copy(
-                ordered[:].bitcast(I32).rearrange("p a (t b w) -> p t a b w", t=PACK, w=words),
-                raw[:].bitcast(I32).rearrange("p a (b t w) -> p t a b w", t=PACK, w=words),
+            nc.scalar.copy(
+                ordered[:].bitcast(U32).rearrange("p a (t b w) -> p a t b w", t=PACK, w=words),
+                raw[:].bitcast(U32).rearrange("p a (b t w) -> p a t b w", t=PACK, w=words),
             )
 
         def gather_x(i, j0, j1):
@@ -141,7 +140,7 @@ def tile_list_htabg_glu_none_kernel(
                 for t in range(2 * u, 2 * u + 2):
                     nc.tensor.matmul_mx(
                         out=ya[:, t - 2 * u, :],
-                        lhsT=w_cod[:, 0, 2 * P * t : 2 * P * (t + 1)].bitcast(FP4X4),
+                        lhsT=wa_cod[:, 0, 2 * P * t : 2 * P * (t + 1)].bitcast(FP4X4),
                         lhsT_scale=wa_scl[:, 0, P * t : P * (t + 1)],
                         rhs=x_cod[c][:].bitcast(FP8X4),
                         rhs_scale=x_scl[c][:],
@@ -161,7 +160,7 @@ def tile_list_htabg_glu_none_kernel(
                 for t in range(PACK):
                     nc.tensor.matmul_mx(
                         out=ya[:, t, :],
-                        lhsT=w_cod[:, 0, 2 * P * t : 2 * P * (t + 1)].bitcast(FP4X4),
+                        lhsT=wa_cod[:, 0, 2 * P * t : 2 * P * (t + 1)].bitcast(FP4X4),
                         lhsT_scale=wa_scl[:, 0, P * t : P * (t + 1)],
                         rhs=x_cod[c][:, u * STEP : (u + 1) * STEP].bitcast(FP8X4),
                         rhs_scale=x_scl[c][:, u * STEP : (u + 1) * STEP],
@@ -196,7 +195,7 @@ def tile_list_htabg_glu_none_kernel(
                 for a in range(2):
                     nc.tensor.matmul_mx(
                         out=yb[s][:, t, :],
-                        lhsT=w_cod[:, 1 + a, 2 * P * t : 2 * P * (t + 1)].bitcast(FP4X4),
+                        lhsT=wb_cod[:, a, 2 * P * t : 2 * P * (t + 1)].bitcast(FP4X4),
                         lhsT_scale=wb_scl[:, a, P * t : P * (t + 1)],
                         rhs=v_cod[half][:, 2 * (a * HALF + first) : 2 * (a * HALF + first + STEP)].bitcast(FP4X4),
                         rhs_scale=v_scl[:, a, s * STEP : (s + 1) * STEP],
@@ -272,15 +271,22 @@ def tile_list_htabg_glu_none_kernel(
                 nc.tensor.transpose(spread[:, c - c0, :], wgt_cols[:, c, :], ident[:])
             nc.scalar.copy(wgt[:, c0 * P : c1 * P], spread[:].rearrange("p c j -> p (c j)"))
 
+        wa_cod = sb("wa_cod", [P, 1, 2 * R], U8)
+        wb_cod = sb("wb_cod", [P, 2, 2 * R], U8)
+        wb_scl = sb_at("wb_scl", [P, 2, R], U8, 14336)
+        order_columns(wb_scl, wbs_raw, 2)
         for half in range(2):
             gather_x(0, half * HALF, (half + 1) * HALF)
         gather_x(1, 0, J)
         for c in range(2, 4):
             x_bf[c] = sb("x_bf%d" % c, [P, CHUNK * PACK], BF16)
             round_x(c, 0, 2)
+        order_columns(wa_scl, was_raw, 2)
+        order_columns(wb_cod, wb_raw, 4)
+        order_columns(wa_cod, wa_raw, 4)
         gather_x(2, 0, J)
         for c in range(2):
-            x_bf[c] = sb("x_bf%d" % c, [P, CHUNK * PACK], BF16)
+            x_bf[c] = sb_at("x_bf%d" % c, [P, CHUNK * PACK], BF16, 17408 + 2048 * c)
             gather_x(3, c * CHUNK, (c + 1) * CHUNK)
             round_x(c, 0, PACK)
         gather_x(3, HALF, J)
@@ -296,14 +302,11 @@ def tile_list_htabg_glu_none_kernel(
         scalar_pair = (nc.scalar.copy, nc.scalar.copy)
         whole = ((0, CHUNK),)
 
-        order_columns(w_cod, w_raw, 4)
-        order_columns(wa_scl, was_raw, 2)
         quantize_x(0)
         gates_by_step(0, 0, first_gates)
         quantize_x(1)
         gather_words(0)
         quantize_x(2)
-        order_columns(wb_scl, wbs_raw, 2)
         part_words(0)
         for u in range(2):
             round_wd(u)

@@ -49,10 +49,9 @@ def tile_list_htabg_glu_none_kernel(
         tab_w = sb("tab_w", [P, T], I32)
         wgt = sb("wgt", [P, J], F32)
         got_x = sb("got_x", [P, PACK, J], F32)
-        x_pl = [sb("x_pl%d" % i, [P, T], F32) for i in range(PACK)]
+        x_pl = [sb_at("x_pl%d" % i, [P, T], F32, 24576 + 8192 * i) for i in range(PACK)]
         wd_raw = sb_at("wd_raw", [P, PACK, N], F32, 960)
-        wa_raw = sb("wa_raw", [P, 1, 2 * R], U8)
-        wb_raw = sb_at("wb_raw", [P, 2, 2 * R], U8, 18432)
+        w_raw = sb("w_raw", [P, 3, 2 * R], U8)
         was_raw = sb("was_raw", [P, 1, R], U8)
         wbs_raw = sb_at("wbs_raw", [P, 2, R], U8, 9216)
         wa_scl = sb("wa_scl", [P, 1, R], U8)
@@ -90,8 +89,8 @@ def tile_list_htabg_glu_none_kernel(
             for q in range(q0, q1):
                 nc.sync.dma_start(v_scl[32 * q : 32 * q + 4, :, :].bitcast(I32), got_s[8 * q : 8 * q + 8, :].bitcast(I32))
 
-        load_scale_rows(wbs_raw, wb_scales)
         load_scale_rows(was_raw, wa_scales)
+        load_scale_rows(wbs_raw, wb_scales)
         nc.sync.dma_start(wgt_rows[0:64, :], wgt2.rearrange("(g r) (c j) -> r c g j", r=GROUP, j=P)[0])
         nc.sync.dma_start(tab_s[0:32, :].bitcast(I32), tab_scales.rearrange("a q t -> q a t").bitcast(I32))
         nc.sync.dma_start(lst[:], offs)
@@ -100,9 +99,9 @@ def tile_list_htabg_glu_none_kernel(
         nc.sync.dma_start(x_pl[1][:], x_rows[1])
         nc.vector.tensor_copy(got_s[:], tab_s[:].indirect(lst[:]))
         nc.sync.dma_start(x_pl[2][:], x_rows[2])
+        nc.sync.dma_start(w_raw[:, 1:3, :].bitcast(I32), wb_words.rearrange("a p c -> p a c").bitcast(I32))
+        nc.sync.dma_start(w_raw[:, 0, :].bitcast(I32), wa_words[0].bitcast(I32))
         nc.sync.dma_start(x_pl[3][:], x_rows[3])
-        nc.sync.dma_start(wb_raw[:].bitcast(I32), wb_words.rearrange("a p c -> p a c").bitcast(I32))
-        nc.sync.dma_start(wa_raw[:].bitcast(I32), wa_words.rearrange("a p c -> p a c").bitcast(I32))
         nc.sync.dma_start(tab_w[:], tab_words[0].rearrange("p t b -> p (t b)").bitcast(I32))
         for t in range(PACK):
             nc.sync.dma_start(wd_raw[:, t, :], wd_rows[t])
@@ -117,6 +116,12 @@ def tile_list_htabg_glu_none_kernel(
             nc.scalar.copy(
                 ordered[:].bitcast(U32).rearrange("p a (t b w) -> p a t b w", t=PACK, w=words),
                 raw[:].bitcast(U32).rearrange("p a (b t w) -> p a t b w", t=PACK, w=words),
+            )
+
+        def order_scales(ordered, raw):
+            nc.vector.tensor_copy(
+                ordered[:].bitcast(I32).rearrange("p a (t b w) -> p t a b w", t=PACK, w=2),
+                raw[:].bitcast(I32).rearrange("p a (b t w) -> p t a b w", t=PACK, w=2),
             )
 
         def gather_x(i, j0, j1):
@@ -140,7 +145,7 @@ def tile_list_htabg_glu_none_kernel(
                 for t in range(2 * u, 2 * u + 2):
                     nc.tensor.matmul_mx(
                         out=ya[:, t - 2 * u, :],
-                        lhsT=wa_cod[:, 0, 2 * P * t : 2 * P * (t + 1)].bitcast(FP4X4),
+                        lhsT=w_cod[:, 0, 2 * P * t : 2 * P * (t + 1)].bitcast(FP4X4),
                         lhsT_scale=wa_scl[:, 0, P * t : P * (t + 1)],
                         rhs=x_cod[c][:].bitcast(FP8X4),
                         rhs_scale=x_scl[c][:],
@@ -160,7 +165,7 @@ def tile_list_htabg_glu_none_kernel(
                 for t in range(PACK):
                     nc.tensor.matmul_mx(
                         out=ya[:, t, :],
-                        lhsT=wa_cod[:, 0, 2 * P * t : 2 * P * (t + 1)].bitcast(FP4X4),
+                        lhsT=w_cod[:, 0, 2 * P * t : 2 * P * (t + 1)].bitcast(FP4X4),
                         lhsT_scale=wa_scl[:, 0, P * t : P * (t + 1)],
                         rhs=x_cod[c][:, u * STEP : (u + 1) * STEP].bitcast(FP8X4),
                         rhs_scale=x_scl[c][:, u * STEP : (u + 1) * STEP],
@@ -195,7 +200,7 @@ def tile_list_htabg_glu_none_kernel(
                 for a in range(2):
                     nc.tensor.matmul_mx(
                         out=yb[s][:, t, :],
-                        lhsT=wb_cod[:, a, 2 * P * t : 2 * P * (t + 1)].bitcast(FP4X4),
+                        lhsT=w_cod[:, 1 + a, 2 * P * t : 2 * P * (t + 1)].bitcast(FP4X4),
                         lhsT_scale=wb_scl[:, a, P * t : P * (t + 1)],
                         rhs=v_cod[half][:, 2 * (a * HALF + first) : 2 * (a * HALF + first + STEP)].bitcast(FP4X4),
                         rhs_scale=v_scl[:, a, s * STEP : (s + 1) * STEP],
@@ -271,19 +276,15 @@ def tile_list_htabg_glu_none_kernel(
                 nc.tensor.transpose(spread[:, c - c0, :], wgt_cols[:, c, :], ident[:])
             nc.scalar.copy(wgt[:, c0 * P : c1 * P], spread[:].rearrange("p c j -> p (c j)"))
 
-        wa_cod = sb("wa_cod", [P, 1, 2 * R], U8)
-        wb_cod = sb("wb_cod", [P, 2, 2 * R], U8)
-        wb_scl = sb_at("wb_scl", [P, 2, R], U8, 14336)
-        order_columns(wb_scl, wbs_raw, 2)
         for half in range(2):
             gather_x(0, half * HALF, (half + 1) * HALF)
+        w_cod = sb_at("w_cod", [P, 3, 2 * R], U8, 24576)
+        order_columns(w_cod, w_raw, 4)
         gather_x(1, 0, J)
         for c in range(2, 4):
             x_bf[c] = sb("x_bf%d" % c, [P, CHUNK * PACK], BF16)
             round_x(c, 0, 2)
         order_columns(wa_scl, was_raw, 2)
-        order_columns(wb_cod, wb_raw, 4)
-        order_columns(wa_cod, wa_raw, 4)
         gather_x(2, 0, J)
         for c in range(2):
             x_bf[c] = sb_at("x_bf%d" % c, [P, CHUNK * PACK], BF16, 17408 + 2048 * c)
@@ -306,8 +307,10 @@ def tile_list_htabg_glu_none_kernel(
         gates_by_step(0, 0, first_gates)
         quantize_x(1)
         gather_words(0)
-        quantize_x(2)
         part_words(0)
+        wb_scl = sb_at("wb_scl", [P, 2, R], U8, 17408 + 2048)
+        order_scales(wb_scl, wbs_raw)
+        quantize_x(2)
         for u in range(2):
             round_wd(u)
         gate[1] = sb_at("gate1", [P, PACK * CHUNK], F32, 1024)

@@ -51,10 +51,12 @@ def tile_list_htabg_glu_none_kernel(
         got_x = sb("got_x", [P, PACK, J], F32)
         x_pl = [sb_at("x_pl%d" % i, [P, T], F32, 24576 + 8192 * i) for i in range(PACK)]
         wd_raw = sb_at("wd_raw", [P, PACK, N], F32, 960)
-        w_raw = sb("w_raw", [P, 3, 2 * R], U8)
+        wa_raw = sb("wa_raw", [P, 1, 2 * R], U8)
+        wb_raw = sb_at("wb_raw", [P, 2, 2 * R], U8, 18432)
+        wa_cod = sb("wa_cod", [P, 1, 2 * R], U8)
+        wb_cod = sb("wb_cod", [P, 2, 2 * R], U8)
         was_raw = sb("was_raw", [P, 1, R], U8)
         wbs_raw = sb_at("wbs_raw", [P, 2, R], U8, 9216)
-        wa_scl = sb("wa_scl", [P, 1, R], U8)
         wd_bf = sb("wd_bf", [P, N * PACK], BF16)
         wd_scl = sb("wd_scl", [P, N], U8)
         got_s = sb("got_s", [P, J], U8)
@@ -99,9 +101,9 @@ def tile_list_htabg_glu_none_kernel(
         nc.sync.dma_start(x_pl[1][:], x_rows[1])
         nc.vector.tensor_copy(got_s[:], tab_s[:].indirect(lst[:]))
         nc.sync.dma_start(x_pl[2][:], x_rows[2])
-        nc.sync.dma_start(w_raw[:, 1:3, :].bitcast(I32), wb_words.rearrange("a p c -> p a c").bitcast(I32))
-        nc.sync.dma_start(w_raw[:, 0, :].bitcast(I32), wa_words[0].bitcast(I32))
         nc.sync.dma_start(x_pl[3][:], x_rows[3])
+        nc.sync.dma_start(wb_raw[:].bitcast(I32), wb_words.rearrange("a p c -> p a c").bitcast(I32))
+        nc.sync.dma_start(wa_raw[:].bitcast(I32), wa_words.rearrange("a p c -> p a c").bitcast(I32))
         nc.sync.dma_start(tab_w[:], tab_words[0].rearrange("p t b -> p (t b)").bitcast(I32))
         for t in range(PACK):
             nc.sync.dma_start(wd_raw[:, t, :], wd_rows[t])
@@ -145,7 +147,7 @@ def tile_list_htabg_glu_none_kernel(
                 for t in range(2 * u, 2 * u + 2):
                     nc.tensor.matmul_mx(
                         out=ya[:, t - 2 * u, :],
-                        lhsT=w_cod[:, 0, 2 * P * t : 2 * P * (t + 1)].bitcast(FP4X4),
+                        lhsT=wa_cod[:, 0, 2 * P * t : 2 * P * (t + 1)].bitcast(FP4X4),
                         lhsT_scale=wa_scl[:, 0, P * t : P * (t + 1)],
                         rhs=x_cod[c][:].bitcast(FP8X4),
                         rhs_scale=x_scl[c][:],
@@ -165,7 +167,7 @@ def tile_list_htabg_glu_none_kernel(
                 for t in range(PACK):
                     nc.tensor.matmul_mx(
                         out=ya[:, t, :],
-                        lhsT=w_cod[:, 0, 2 * P * t : 2 * P * (t + 1)].bitcast(FP4X4),
+                        lhsT=wa_cod[:, 0, 2 * P * t : 2 * P * (t + 1)].bitcast(FP4X4),
                         lhsT_scale=wa_scl[:, 0, P * t : P * (t + 1)],
                         rhs=x_cod[c][:, u * STEP : (u + 1) * STEP].bitcast(FP8X4),
                         rhs_scale=x_scl[c][:, u * STEP : (u + 1) * STEP],
@@ -200,7 +202,7 @@ def tile_list_htabg_glu_none_kernel(
                 for a in range(2):
                     nc.tensor.matmul_mx(
                         out=yb[s][:, t, :],
-                        lhsT=w_cod[:, 1 + a, 2 * P * t : 2 * P * (t + 1)].bitcast(FP4X4),
+                        lhsT=wb_cod[:, a, 2 * P * t : 2 * P * (t + 1)].bitcast(FP4X4),
                         lhsT_scale=wb_scl[:, a, P * t : P * (t + 1)],
                         rhs=v_cod[half][:, 2 * (a * HALF + first) : 2 * (a * HALF + first + STEP)].bitcast(FP4X4),
                         rhs_scale=v_scl[:, a, s * STEP : (s + 1) * STEP],
@@ -278,14 +280,15 @@ def tile_list_htabg_glu_none_kernel(
 
         for half in range(2):
             gather_x(0, half * HALF, (half + 1) * HALF)
-        w_cod = sb_at("w_cod", [P, 3, 2 * R], U8, 24576)
-        order_columns(w_cod, w_raw, 4)
         gather_x(1, 0, J)
         for c in range(2, 4):
             x_bf[c] = sb("x_bf%d" % c, [P, CHUNK * PACK], BF16)
             round_x(c, 0, 2)
-        order_columns(wa_scl, was_raw, 2)
         gather_x(2, 0, J)
+        order_columns(wb_cod, wb_raw, 4)
+        order_columns(wa_cod, wa_raw, 4)
+        wa_scl = sb_at("wa_scl", [P, 1, R], U8, 24576 + 2 * 8192)
+        order_columns(wa_scl, was_raw, 2)
         for c in range(2):
             x_bf[c] = sb_at("x_bf%d" % c, [P, CHUNK * PACK], BF16, 17408 + 2048 * c)
             gather_x(3, c * CHUNK, (c + 1) * CHUNK)

@@ -56,7 +56,8 @@ def tile_list_htabg_glu_none_kernel(
         wa_cod = sb("wa_cod", [P, 1, 2 * R], U8)
         wb_cod = sb("wb_cod", [P, 2, 2 * R], U8)
         was_raw = sb("was_raw", [P, 1, R], U8)
-        wbs_raw = sb_at("wbs_raw", [P, 2, R], U8, 9216)
+        wbs_raw = sb("wbs_raw", [P, R], U8)
+        wb_scl = sb("wb_scl", [P, 2, R], U8)
         wd_bf = sb("wd_bf", [P, N * PACK], BF16)
         wd_scl = sb("wd_scl", [P, N], U8)
         got_s = sb("got_s", [P, J], U8)
@@ -69,11 +70,11 @@ def tile_list_htabg_glu_none_kernel(
 
         make_identity(nc, ident[:])
         nc.vector.memset(wgt_rows[64:128, :], 0.0)
-        nc.vector.memset(wbs_raw[:].rearrange("p a r -> p (a r)").bitcast(I32), 0)
         nc.vector.memset(was_raw[:].rearrange("p a r -> p (a r)").bitcast(I32), 0)
         nc.vector.memset(warm[:], 0.0)
         nc.vector.memset(tab_s[32:64, :].bitcast(I32), 0)
         nc.vector.memset(tab_s[64:128, :].bitcast(I32), 0)
+        nc.vector.memset(wb_scl[:].rearrange("p a r -> p (a r)").bitcast(I32), 0)
         nc.vector.memset(v_scl[:].rearrange("p a j -> p (a j)").bitcast(I32), 0)
         nc.scalar.activation(warm_out[:], warm[:], SILU)
 
@@ -92,12 +93,12 @@ def tile_list_htabg_glu_none_kernel(
                 nc.sync.dma_start(v_scl[32 * q : 32 * q + 4, :, :].bitcast(I32), got_s[8 * q : 8 * q + 8, :].bitcast(I32))
 
         load_scale_rows(was_raw, wa_scales)
-        load_scale_rows(wbs_raw, wb_scales)
         nc.sync.dma_start(wgt_rows[0:64, :], wgt2.rearrange("(g r) (c j) -> r c g j", r=GROUP, j=P)[0])
         nc.sync.dma_start(tab_s[0:32, :].bitcast(I32), tab_scales.rearrange("a q t -> q a t").bitcast(I32))
         nc.sync.dma_start(lst[:], offs)
         nc.sync.dma_start(x_pl[0][:], x_rows[0])
         nc.sync.dma_start(lst2[:], offs2)
+        nc.sync.dma_start(wbs_raw[0:32, :].bitcast(I32), wb_scales.rearrange("a q r -> q a r").bitcast(I32))
         nc.sync.dma_start(x_pl[1][:], x_rows[1])
         nc.vector.tensor_copy(got_s[:], tab_s[:].indirect(lst[:]))
         nc.sync.dma_start(x_pl[2][:], x_rows[2])
@@ -118,12 +119,6 @@ def tile_list_htabg_glu_none_kernel(
             nc.scalar.copy(
                 ordered[:].bitcast(U32).rearrange("p a (t b w) -> p a t b w", t=PACK, w=words),
                 raw[:].bitcast(U32).rearrange("p a (b t w) -> p a t b w", t=PACK, w=words),
-            )
-
-        def order_scales(ordered, raw):
-            nc.vector.tensor_copy(
-                ordered[:].bitcast(I32).rearrange("p a (t b w) -> p t a b w", t=PACK, w=2),
-                raw[:].bitcast(I32).rearrange("p a (b t w) -> p t a b w", t=PACK, w=2),
             )
 
         def gather_x(i, j0, j1):
@@ -280,15 +275,22 @@ def tile_list_htabg_glu_none_kernel(
 
         for half in range(2):
             gather_x(0, half * HALF, (half + 1) * HALF)
+        wbs_rows = sb_at("wbs_rows", [P, R], U8, 24576)
+        nc.scalar.copy(
+            wbs_rows[0:32, :].bitcast(U32).rearrange("p (t b w) -> p t b w", t=PACK, w=2),
+            wbs_raw[0:32, :].bitcast(U32).rearrange("p (b t w) -> p t b w", t=PACK, w=2),
+        )
+        for q in range(4):
+            nc.gpsimd.dma_start(wb_scl[32 * q : 32 * q + 4, :, :].bitcast(I32), wbs_rows[8 * q : 8 * q + 8, :].bitcast(I32))
         gather_x(1, 0, J)
         for c in range(2, 4):
             x_bf[c] = sb("x_bf%d" % c, [P, CHUNK * PACK], BF16)
             round_x(c, 0, 2)
+        wa_scl = sb_at("wa_scl", [P, 1, R], U8, 24576 + 8192)
+        order_columns(wa_scl, was_raw, 2)
         gather_x(2, 0, J)
         order_columns(wb_cod, wb_raw, 4)
         order_columns(wa_cod, wa_raw, 4)
-        wa_scl = sb_at("wa_scl", [P, 1, R], U8, 24576 + 2 * 8192)
-        order_columns(wa_scl, was_raw, 2)
         for c in range(2):
             x_bf[c] = sb_at("x_bf%d" % c, [P, CHUNK * PACK], BF16, 17408 + 2048 * c)
             gather_x(3, c * CHUNK, (c + 1) * CHUNK)
@@ -310,10 +312,8 @@ def tile_list_htabg_glu_none_kernel(
         gates_by_step(0, 0, first_gates)
         quantize_x(1)
         gather_words(0)
-        part_words(0)
-        wb_scl = sb_at("wb_scl", [P, 2, R], U8, 17408 + 2048)
-        order_scales(wb_scl, wbs_raw)
         quantize_x(2)
+        part_words(0)
         for u in range(2):
             round_wd(u)
         gate[1] = sb_at("gate1", [P, PACK * CHUNK], F32, 1024)

@@ -23,6 +23,10 @@ GROUP = 16
 CHUNK = 256
 HALF = 512
 STEP = 128
+SPLIT = 640
+AT_SCALES = 32768
+AT_GATE0 = 34816
+AT_WD = 40960
 
 
 def tile_list_htabg_glu_none_kernel(
@@ -49,29 +53,34 @@ def tile_list_htabg_glu_none_kernel(
         tab_w = sb("tab_w", [P, T], I32)
         wgt = sb("wgt", [P, J], F32)
         got_x = sb("got_x", [P, PACK, J], F32)
-        x_pl = [sb_at("x_pl%d" % i, [P, T], F32, 24576 + 8192 * i) for i in range(PACK)]
-        wd_raw = sb_at("wd_raw", [P, PACK, N], F32, 960)
+        x_pl = [sb_at("x_pl%d" % i, [P, T], F32, 8192 * i) for i in range(PACK)]
+        got_s = sb_at("got_s", [P, J], U8, AT_SCALES)
+        wd_raw = sb_at("wd_raw", [P, PACK, N], F32, AT_WD)
         wa_raw = sb("wa_raw", [P, 1, 2 * R], U8)
-        wb_raw = sb_at("wb_raw", [P, 2, 2 * R], U8, 18432)
+        wb_raw = sb("wb_raw", [P, 2, 2 * R], U8)
         wa_cod = sb("wa_cod", [P, 1, 2 * R], U8)
         wb_cod = sb("wb_cod", [P, 2, 2 * R], U8)
         was_raw = sb("was_raw", [P, 1, R], U8)
         wbs_raw = sb("wbs_raw", [P, R], U8)
         wb_scl = sb("wb_scl", [P, 2, R], U8)
-        wd_bf = sb("wd_bf", [P, N * PACK], BF16)
+        wd_bf = [sb("wd_bf%d" % u, [P, CHUNK * PACK], BF16) for u in range(2)]
+        wd_cod = sb("wd_cod", [P, N], U32)
         wd_scl = sb("wd_scl", [P, N], U8)
-        got_s = sb("got_s", [P, J], U8)
         v_scl = sb("v_scl", [P, 2, J], U8)
         warm = sb("warm", [P, 8], F32)
         warm_out = sb("warm_out", [P, 8], F32)
         ident = sb("ident", [P, P], F32)
         wgt_rows = sb("wgt_rows", [P, P], F32)
-        wgt_cols = sb_at("wgt_cols", [P, J // P, P], F32, 11264)
+        wgt_cols = sb("wgt_cols", [P, J // P, P], F32)
+        x_bf = [sb("x_bf%d" % c, [P, CHUNK * PACK], BF16) for c in range(4)]
+        h_bf = [sb("h_bf%d" % c, [P, CHUNK * PACK], BF16) for c in range(4)]
+        h_cod = [sb("h_cod%d" % c, [P, CHUNK], U32) for c in range(4)]
+        h_scl = [sb("h_scl%d" % c, [P, CHUNK], U8) for c in range(4)]
 
         make_identity(nc, ident[:])
+        nc.vector.memset(warm[:], 0.0)
         nc.vector.memset(wgt_rows[64:128, :], 0.0)
         nc.vector.memset(was_raw[:].rearrange("p a r -> p (a r)").bitcast(I32), 0)
-        nc.vector.memset(warm[:], 0.0)
         nc.vector.memset(tab_s[32:64, :].bitcast(I32), 0)
         nc.vector.memset(tab_s[64:128, :].bitcast(I32), 0)
         nc.vector.memset(wb_scl[:].rearrange("p a r -> p (a r)").bitcast(I32), 0)
@@ -80,19 +89,11 @@ def tile_list_htabg_glu_none_kernel(
 
         x_rows = xT.rearrange("(p i) t -> i p t", i=PACK)
         wd_rows = wd.rearrange("(b t q) n -> t b q n", t=PACK, q=8)
-
-        def load_scale_rows(tile, scales):
-            for q in range(4):
-                nc.gpsimd.dma_start(
-                    tile[32 * q : 32 * q + 4, :, :].bitcast(I32),
-                    scales[:, 4 * q : 4 * q + 4, :].rearrange("a q r -> q a r").bitcast(I32),
-                )
-
-        def move_scale_rows(q0, q1):
-            for q in range(q0, q1):
-                nc.sync.dma_start(v_scl[32 * q : 32 * q + 4, :, :].bitcast(I32), got_s[8 * q : 8 * q + 8, :].bitcast(I32))
-
-        load_scale_rows(was_raw, wa_scales)
+        for q in range(4):
+            nc.scalar.dma_start(
+                was_raw[32 * q : 32 * q + 4, :, :].bitcast(I32),
+                wa_scales[:, 4 * q : 4 * q + 4, :].rearrange("a q r -> q a r").bitcast(I32),
+            )
         nc.sync.dma_start(wgt_rows[0:64, :], wgt2.rearrange("(g r) (c j) -> r c g j", r=GROUP, j=P)[0])
         nc.sync.dma_start(tab_s[0:32, :].bitcast(I32), tab_scales.rearrange("a q t -> q a t").bitcast(I32))
         nc.sync.dma_start(lst[:], offs)
@@ -103,17 +104,19 @@ def tile_list_htabg_glu_none_kernel(
         nc.vector.tensor_copy(got_s[:], tab_s[:].indirect(lst[:]))
         nc.sync.dma_start(x_pl[2][:], x_rows[2])
         nc.sync.dma_start(x_pl[3][:], x_rows[3])
-        nc.sync.dma_start(wb_raw[:].bitcast(I32), wb_words.rearrange("a p c -> p a c").bitcast(I32))
         nc.sync.dma_start(wa_raw[:].bitcast(I32), wa_words.rearrange("a p c -> p a c").bitcast(I32))
+        nc.sync.dma_start(wb_raw[:].bitcast(I32), wb_words.rearrange("a p c -> p a c").bitcast(I32))
         nc.sync.dma_start(tab_w[:], tab_words[0].rearrange("p t b -> p (t b)").bitcast(I32))
+        for q in range(4):
+            nc.sync.dma_start(v_scl[32 * q : 32 * q + 4, :, :].bitcast(I32), got_s[8 * q : 8 * q + 8, :].bitcast(I32))
         for t in range(PACK):
             nc.sync.dma_start(wd_raw[:, t, :], wd_rows[t])
-        move_scale_rows(0, 4)
 
         out_rows = out.rearrange("(m p) j -> p m j", p=P)
-        x_bf, x_cod, x_scl, gate, got_w, v_cod, yb, h_bf, h_cod, h_scl = {}, {}, {}, {}, {}, {}, {}, {}, {}, {}
+        x_cod, x_scl, gate, got_w, v_cod, ya, yb, y = {}, {}, {}, {}, {}, {}, {}, {}
 
-        step_gate = {}
+        def place(name, shape, dtype, offset):
+            return sb(name, shape, dtype) if offset is None else sb_at(name, shape, dtype, offset)
 
         def order_columns(ordered, raw, words):
             nc.scalar.copy(
@@ -131,75 +134,65 @@ def tile_list_htabg_glu_none_kernel(
                 got_x[:, t0:t1, c * CHUNK : (c + 1) * CHUNK].rearrange("p t (c i) -> p c t i", i=2),
             )
 
-        def quantize_x(c):
+        def quantize_x(c, scales_at=None):
             x_cod[c] = sb("x_cod%d" % c, [P, CHUNK], U32)
-            x_scl[c] = sb("x_scl%d" % c, [P, CHUNK], U8)
+            x_scl[c] = place("x_scl%d" % c, [P, CHUNK], U8, scales_at)
             nc.vector.quantize_mx(out=x_cod[c][:].bitcast(FP8X4), scales=x_scl[c][:], in_=x_bf[c][:])
 
-        def gates(c, first_bank):
-            for u in range(2):
-                ya = bank(first_bank + u, "ya%d_%d" % (c, u), [P, 2, CHUNK])
-                for t in range(2 * u, 2 * u + 2):
-                    nc.tensor.matmul_mx(
-                        out=ya[:, t - 2 * u, :],
-                        lhsT=wa_cod[:, 0, 2 * P * t : 2 * P * (t + 1)].bitcast(FP4X4),
-                        lhsT_scale=wa_scl[:, 0, P * t : P * (t + 1)],
-                        rhs=x_cod[c][:].bitcast(FP8X4),
-                        rhs_scale=x_scl[c][:],
-                        start=True,
-                        stop=True,
-                    )
-                nc.scalar.activation(
-                    gate[c][:, 2 * u * CHUNK : (2 * u + 2) * CHUNK], ya[:].rearrange("p t j -> p (t j)"), SILU
+        def gate_sums(s, number):
+            c, u = divmod(s, 2)
+            ya[s] = bank(number, "ya%d" % s, [P, PACK, STEP])
+            for t in range(PACK):
+                nc.tensor.matmul_mx(
+                    out=ya[s][:, t, :],
+                    lhsT=wa_cod[:, 0, 2 * P * t : 2 * P * (t + 1)].bitcast(FP4X4),
+                    lhsT_scale=wa_scl[:, 0, P * t : P * (t + 1)],
+                    rhs=x_cod[c][:, u * STEP : (u + 1) * STEP].bitcast(FP8X4),
+                    rhs_scale=x_scl[c][:, u * STEP : (u + 1) * STEP],
+                    start=True,
+                    stop=True,
                 )
-            pairs = gate[c][:].rearrange("p (t c i) -> p c t i", t=PACK, i=2)
-            for u in range(2):
-                step_gate[2 * c + u] = pairs[:, u * STEP // 2 : (u + 1) * STEP // 2, :, :]
 
-        def gates_by_step(c, first_bank, tiles):
-            for u in range(2):
-                ya = bank(first_bank + u, "ya%d_%d" % (c, u), [P, PACK, STEP])
-                for t in range(PACK):
-                    nc.tensor.matmul_mx(
-                        out=ya[:, t, :],
-                        lhsT=wa_cod[:, 0, 2 * P * t : 2 * P * (t + 1)].bitcast(FP4X4),
-                        lhsT_scale=wa_scl[:, 0, P * t : P * (t + 1)],
-                        rhs=x_cod[c][:, u * STEP : (u + 1) * STEP].bitcast(FP8X4),
-                        rhs_scale=x_scl[c][:, u * STEP : (u + 1) * STEP],
-                        start=True,
-                        stop=True,
-                    )
-                nc.scalar.activation(tiles[u][:], ya[:].rearrange("p t j -> p (t j)"), SILU)
-                step_gate[2 * c + u] = tiles[u][:].rearrange("p (t c i) -> p c t i", t=PACK, i=2)
+        def make_gate(s, at=None):
+            gate[s] = place("gate%d" % s, [P, PACK * STEP], F32, at)
+            nc.scalar.activation(gate[s][:], ya[s][:].rearrange("p t j -> p (t j)"), SILU)
 
-        def gather_words(half):
-            got_w[half] = sb("got_w%d" % half, [P, HALF], U32)
-            entries = lst[:, half * HALF // GROUP : (half + 1) * HALF // GROUP]
-            nc.vector.tensor_copy(got_w[half][:], tab_w[:].bitcast(U32).indirect(entries))
+        def gather_words(c, at=None):
+            got_w[c] = place("got_w%d" % c, [P, CHUNK], U32, at)
+            entries = lst[:, c * CHUNK // GROUP : (c + 1) * CHUNK // GROUP]
+            nc.vector.tensor_copy(got_w[c][:], tab_w[:].bitcast(U32).indirect(entries))
 
-        def part_words(half):
-            v_cod[half] = sb("v_cod%d" % half, [P, 4 * HALF], U8)
+        def part_words(c, at=None):
+            v_cod[c] = place("v_cod%d" % c, [P, 4 * CHUNK], U8, at)
             nc.vector.tensor_copy(
-                v_cod[half][:].bitcast(U16).rearrange("p (d j) -> p d j", d=2),
-                got_w[half][:].bitcast(U16).rearrange("p (j d) -> p d j", d=2),
+                v_cod[c][:].bitcast(U16).rearrange("p (d j) -> p d j", d=2),
+                got_w[c][:].bitcast(U16).rearrange("p (j d) -> p d j", d=2),
             )
 
         def round_wd(u):
             nc.scalar.copy(
-                wd_bf[:, u * CHUNK * PACK : (u + 1) * CHUNK * PACK].rearrange("p (c i t) -> p c t i", i=2, t=PACK),
+                wd_bf[u][:].rearrange("p (c i t) -> p c t i", i=2, t=PACK),
                 wd_raw[:, :, u * CHUNK : (u + 1) * CHUNK].rearrange("p t (c i) -> p c t i", i=2),
             )
 
-        def memory_sums(s):
-            half, first = divmod(s * STEP, HALF)
-            yb[s] = bank(4 + s % 4, "yb%d" % s, [P, PACK, STEP])
+        def quantize_wd(u):
+            nc.vector.quantize_mx(
+                out=wd_cod[:, u * CHUNK : (u + 1) * CHUNK].bitcast(FP8X4),
+                scales=wd_scl[:, u * CHUNK : (u + 1) * CHUNK],
+                in_=wd_bf[u][:],
+            )
+
+        def memory_sums(s, number):
+            c, u = divmod(s, 2)
+            yb[s] = bank(number, "yb%d" % s, [P, PACK, STEP])
             for t in range(PACK):
                 for a in range(2):
+                    first = a * CHUNK + u * STEP
                     nc.tensor.matmul_mx(
                         out=yb[s][:, t, :],
                         lhsT=wb_cod[:, a, 2 * P * t : 2 * P * (t + 1)].bitcast(FP4X4),
                         lhsT_scale=wb_scl[:, a, P * t : P * (t + 1)],
-                        rhs=v_cod[half][:, 2 * (a * HALF + first) : 2 * (a * HALF + first + STEP)].bitcast(FP4X4),
+                        rhs=v_cod[c][:, 2 * first : 2 * (first + STEP)].bitcast(FP4X4),
                         rhs_scale=v_scl[:, a, s * STEP : (s + 1) * STEP],
                         start=(a == 0),
                         stop=(a == 1),
@@ -207,12 +200,10 @@ def tile_list_htabg_glu_none_kernel(
 
         def join(s):
             c, u = divmod(s, 2)
-            if u == 0:
-                h_bf[c] = sb("h_bf%d" % c, [P, CHUNK * PACK], BF16)
             nc.vector.tensor_tensor(
                 h_bf[c][:, u * STEP * PACK : (u + 1) * STEP * PACK].rearrange("p (c i t) -> p c t i", i=2, t=PACK),
                 yb[s][:].rearrange("p t (c i) -> p c t i", i=2),
-                step_gate[s],
+                gate[s][:].rearrange("p (t c i) -> p c t i", t=PACK, i=2),
                 MULT,
             )
 
@@ -223,41 +214,26 @@ def tile_list_htabg_glu_none_kernel(
                 in_=h_bf[c][:, j0 * PACK : j1 * PACK],
             )
 
-        def second_layer(c, first_bank, pieces, engines):
-            banks = [bank(first_bank + u, "y%d_%d" % (c, u), [P, 2, CHUNK]) for u in range(2)]
-            for j0, j1 in pieces:
-                for m in range(N // P):
-                    nc.tensor.matmul_mx(
-                        out=banks[m // 2][:, m % 2, j0:j1],
-                        lhsT=wd_cod[:, P * m : P * (m + 1)].bitcast(FP8X4),
-                        lhsT_scale=wd_scl[:, P * m : P * (m + 1)],
-                        rhs=h_cod[c][:, j0:j1].bitcast(FP8X4),
-                        rhs_scale=h_scl[c][:, j0:j1],
-                        start=True,
-                        stop=True,
-                    )
-            for u in range(2):
-                y_sb = sb("y_sb%d_%d" % (c, u), [P, 2, CHUNK], F32)
-                engines[u](y_sb[:], banks[u][:])
-                nc.sync.dma_start(out_rows[:, 2 * u : 2 * u + 2, c * CHUNK : (c + 1) * CHUNK], y_sb[:])
+        def output_pass(target, c, m, j0, j1):
+            nc.tensor.matmul_mx(
+                out=target,
+                lhsT=wd_cod[:, P * m : P * (m + 1)].bitcast(FP8X4),
+                lhsT_scale=wd_scl[:, P * m : P * (m + 1)],
+                rhs=h_cod[c][:, j0:j1].bitcast(FP8X4),
+                rhs_scale=h_scl[c][:, j0:j1],
+                start=True,
+                stop=True,
+            )
 
-        def last_outputs(c, bank_numbers):
-            banks = [bank(number, "y%d_%d" % (c, m), [P, CHUNK]) for m, number in enumerate(bank_numbers)]
-            for u in range(2):
-                for m in (0, 2, 1, 3):
-                    nc.tensor.matmul_mx(
-                        out=banks[m][:, u * STEP : (u + 1) * STEP],
-                        lhsT=wd_cod[:, P * m : P * (m + 1)].bitcast(FP8X4),
-                        lhsT_scale=wd_scl[:, P * m : P * (m + 1)],
-                        rhs=h_cod[c][:, u * STEP : (u + 1) * STEP].bitcast(FP8X4),
-                        rhs_scale=h_scl[c][:, u * STEP : (u + 1) * STEP],
-                        start=True,
-                        stop=True,
-                    )
-            for m in (0, 2, 1, 3):
-                y_sb = sb("y_sb%d_%d" % (c, m), [P, CHUNK], F32)
-                (nc.scalar.copy if m < 2 else nc.vector.tensor_copy)(y_sb[:], banks[m][:])
-                nc.sync.dma_start(out_rows[:, m, c * CHUNK : (c + 1) * CHUNK], y_sb[:])
+        def output_sums(c, u, number):
+            y[c, u] = bank(number, "y%d_%d" % (c, u), [P, 2, CHUNK])
+            for m in range(2):
+                output_pass(y[c, u][:, m, :], c, 2 * u + m, 0, CHUNK)
+
+        def store(c, u, copy, at=None):
+            y_sb = place("y_sb%d_%d" % (c, u), [P, 2, CHUNK], F32, at)
+            copy(y_sb[:], y[c, u][:])
+            nc.sync.dma_start(out_rows[:, 2 * u : 2 * u + 2, c * CHUNK : (c + 1) * CHUNK], y_sb[:])
 
         turned = bank(6, "turned", [P, P])
         nc.tensor.transpose(turned[:], wgt_rows[:], ident[:])
@@ -275,78 +251,93 @@ def tile_list_htabg_glu_none_kernel(
 
         for half in range(2):
             gather_x(0, half * HALF, (half + 1) * HALF)
-        wbs_rows = sb_at("wbs_rows", [P, R], U8, 24576)
+        wbs_rows = sb_at("wbs_rows", [P, R], U8, 0)
         nc.scalar.copy(
             wbs_rows[0:32, :].bitcast(U32).rearrange("p (t b w) -> p t b w", t=PACK, w=2),
             wbs_raw[0:32, :].bitcast(U32).rearrange("p (b t w) -> p t b w", t=PACK, w=2),
         )
         for q in range(4):
-            nc.gpsimd.dma_start(wb_scl[32 * q : 32 * q + 4, :, :].bitcast(I32), wbs_rows[8 * q : 8 * q + 8, :].bitcast(I32))
-        gather_x(1, 0, J)
-        for c in range(2, 4):
-            x_bf[c] = sb("x_bf%d" % c, [P, CHUNK * PACK], BF16)
-            round_x(c, 0, 2)
-        wa_scl = sb_at("wa_scl", [P, 1, R], U8, 24576 + 8192)
+            nc.scalar.dma_start(wb_scl[32 * q : 32 * q + 4, :, :].bitcast(I32), wbs_rows[8 * q : 8 * q + 8, :].bitcast(I32))
+        wa_scl = sb_at("wa_scl", [P, 1, R], U8, R)
         order_columns(wa_scl, was_raw, 2)
-        gather_x(2, 0, J)
-        order_columns(wb_cod, wb_raw, 4)
-        order_columns(wa_cod, wa_raw, 4)
-        for c in range(2):
-            x_bf[c] = sb_at("x_bf%d" % c, [P, CHUNK * PACK], BF16, 17408 + 2048 * c)
-            gather_x(3, c * CHUNK, (c + 1) * CHUNK)
-            round_x(c, 0, PACK)
-        gather_x(3, HALF, J)
-        for c in range(2, 4):
-            round_x(c, 2, PACK)
-
+        gather_x(1, 0, SPLIT)
+        gather_x(1, SPLIT, J)
         for c in range(4):
-            h_scl[c] = sb("h_scl%d" % c, [P, CHUNK], U8)
-        for c in range(1, 4):
-            h_cod[c] = sb("h_cod%d" % c, [P, CHUNK], U32)
-        first_gates = (sb_at("gate_step0", [P, PACK * STEP], F32, 15360), sb("gate_step1", [P, PACK * STEP], F32))
-        gate[3] = sb("gate3", [P, PACK * CHUNK], F32)
-        scalar_pair = (nc.scalar.copy, nc.scalar.copy)
-        whole = ((0, CHUNK),)
+            round_x(c, 0, 2)
+        gather_x(2, 0, J)
+        for c in range(4):
+            gather_x(3, c * CHUNK, (c + 1) * CHUNK)
+        order_columns(wa_cod, wa_raw, 4)
+        round_x(0, 2, PACK)
+        round_x(1, 2, PACK)
+        order_columns(wb_cod, wb_raw, 4)
+        round_x(2, 2, PACK)
+        round_x(3, 2, PACK)
 
         quantize_x(0)
-        gates_by_step(0, 0, first_gates)
         quantize_x(1)
+        for s in range(4):
+            gate_sums(s, s)
+        make_gate(0, AT_GATE0)
+        make_gate(1, AT_GATE0 + 2048)
+        make_gate(2)
         gather_words(0)
-        quantize_x(2)
+        gather_words(1)
         part_words(0)
+        part_words(1)
+        gather_words(2)
+        quantize_x(2, AT_SCALES)
+        quantize_x(3, AT_SCALES + CHUNK)
+        for s, number in enumerate((4, 5, 0, 1)):
+            memory_sums(s, number)
+        gate_sums(4, 6)
+        gate_sums(5, 7)
+        gate_sums(6, 2)
+        join(0)
+        join(1)
+        part_words(2, AT_GATE0)
+        gather_words(3, AT_GATE0 + 2048)
+        quantize_h(0, 0, CHUNK)
+        join(2)
+        part_words(3)
+        memory_sums(4, 4)
+        memory_sums(5, 5)
         for u in range(2):
             round_wd(u)
-        gate[1] = sb_at("gate1", [P, PACK * CHUNK], F32, 1024)
-        gate[2] = sb_at("gate2", [P, PACK * CHUNK], F32, 5120)
-        gates(1, 2)
-        for s in range(4):
-            memory_sums(s)
-        gates(2, 0)
-        gather_words(1)
-        quantize_x(3)
-        part_words(1)
-        join(0)
-        memory_sums(4)
-        join(1)
-        memory_sums(5)
-        wd_cod = sb_at("wd_cod", [P, N], U32, 15360)
-        nc.vector.quantize_mx(out=wd_cod[:].bitcast(FP8X4), scales=wd_scl[:], in_=wd_bf[:])
-        h_cod[0] = sb_at("h_cod0", [P, CHUNK], U32, 0)
-        quantize_h(0, 0, CHUNK)
-        second_layer(0, 2, whole, scalar_pair)
-        gates(3, 0)
-        join(2)
-        memory_sums(6)
+        for u in range(2):
+            quantize_wd(u)
+        output_sums(0, 0, 0)
+        for s in range(3, 7):
+            make_gate(s, AT_WD - 1024 + 2048 * (s - 3))
+        gate_sums(7, 3)
+        output_sums(0, 1, 6)
         join(3)
-        memory_sums(7)
+        memory_sums(6, 1)
+        memory_sums(7, 7)
         join(4)
         quantize_h(1, 0, CHUNK)
-        second_layer(1, 2, whole, scalar_pair)
+        store(0, 0, nc.scalar.copy, AT_WD - 2048)
+        store(0, 1, nc.scalar.copy)
+        make_gate(7, AT_WD - 1024 + 2048 * 4)
+        output_sums(1, 0, 4)
+        output_sums(1, 1, 0)
         join(5)
         join(6)
         quantize_h(2, 0, CHUNK)
-        second_layer(2, 4, whole, scalar_pair)
+        store(1, 0, nc.scalar.copy)
+        store(1, 1, nc.scalar.copy)
+        output_sums(2, 0, 5)
+        output_sums(2, 1, 6)
         join(7)
         for u in range(2):
             quantize_h(3, u * STEP, (u + 1) * STEP)
-        last_outputs(3, (0, 1, 6, 2))
+        store(2, 0, nc.scalar.copy)
+        store(2, 1, nc.vector.tensor_copy)
+        last = [bank(number, "y3_%d" % m, [P, CHUNK]) for m, number in enumerate((2, 3, 1, 4))]
+        for u in range(2):
+            for m in (0, 2, 1, 3):
+                output_pass(last[m][:, u * STEP : (u + 1) * STEP], 3, m, u * STEP, (u + 1) * STEP)
+        for m in (0, 2, 1, 3):
+            y_sb = sb("y_last%d" % m, [P, CHUNK], F32)
+            (nc.scalar.copy if m < 2 else nc.vector.tensor_copy)(y_sb[:], last[m][:])
+            nc.sync.dma_start(out_rows[:, m, 3 * CHUNK : 4 * CHUNK], y_sb[:])

@@ -15,6 +15,7 @@ U8 = mybir.dt.uint8
 FP8X4 = mybir.dt.float8_e4m3fn_x4
 FP4X4 = mybir.dt.float4_e2m1fn_x4
 MULT = mybir.AluOpType.mult
+ADD = mybir.AluOpType.add
 SILU = mybir.ActivationFunctionType.Silu
 
 P = 128
@@ -26,7 +27,9 @@ STEP = 128
 SPLIT = 640
 AT_SCALES = 32768
 AT_GATE0 = 34816
-AT_WD = 40960
+AT_WD = 43008
+AT_X3 = 53248
+AT_WORDS = 55296
 
 
 def tile_list_htabg_glu_none_kernel(
@@ -63,7 +66,6 @@ def tile_list_htabg_glu_none_kernel(
         was_raw = sb("was_raw", [P, 1, R], U8)
         wbs_raw = sb("wbs_raw", [P, R], U8)
         wb_scl = sb("wb_scl", [P, 2, R], U8)
-        wd_bf = [sb("wd_bf%d" % u, [P, CHUNK * PACK], BF16) for u in range(2)]
         wd_cod = sb("wd_cod", [P, N], U32)
         wd_scl = sb("wd_scl", [P, N], U8)
         v_scl = sb("v_scl", [P, 2, J], U8)
@@ -72,7 +74,8 @@ def tile_list_htabg_glu_none_kernel(
         ident = sb("ident", [P, P], F32)
         wgt_rows = sb("wgt_rows", [P, P], F32)
         wgt_cols = sb("wgt_cols", [P, J // P, P], F32)
-        x_bf = [sb("x_bf%d" % c, [P, CHUNK * PACK], BF16) for c in range(4)]
+        x_bf = [sb("x_bf%d" % c, [P, CHUNK * PACK], BF16) for c in range(3)]
+        x_bf.append(sb_at("x_bf3", [P, CHUNK * PACK], BF16, AT_X3))
         h_bf = [sb("h_bf%d" % c, [P, CHUNK * PACK], BF16) for c in range(4)]
         h_cod = [sb("h_cod%d" % c, [P, CHUNK], U32) for c in range(4)]
         h_scl = [sb("h_scl%d" % c, [P, CHUNK], U8) for c in range(4)]
@@ -139,23 +142,24 @@ def tile_list_htabg_glu_none_kernel(
             x_scl[c] = place("x_scl%d" % c, [P, CHUNK], U8, scales_at)
             nc.vector.quantize_mx(out=x_cod[c][:].bitcast(FP8X4), scales=x_scl[c][:], in_=x_bf[c][:])
 
-        def gate_sums(s, number):
-            c, u = divmod(s, 2)
-            ya[s] = bank(number, "ya%d" % s, [P, PACK, STEP])
-            for t in range(PACK):
-                nc.tensor.matmul_mx(
-                    out=ya[s][:, t, :],
-                    lhsT=wa_cod[:, 0, 2 * P * t : 2 * P * (t + 1)].bitcast(FP4X4),
-                    lhsT_scale=wa_scl[:, 0, P * t : P * (t + 1)],
-                    rhs=x_cod[c][:, u * STEP : (u + 1) * STEP].bitcast(FP8X4),
-                    rhs_scale=x_scl[c][:, u * STEP : (u + 1) * STEP],
-                    start=True,
-                    stop=True,
-                )
+        def gate_sums(c, first_bank):
+            for u in range(2):
+                ya[c, u] = bank(first_bank + u, "ya%d_%d" % (c, u), [P, 2, CHUNK])
+                for t in range(2 * u, 2 * u + 2):
+                    nc.tensor.matmul_mx(
+                        out=ya[c, u][:, t - 2 * u, :],
+                        lhsT=wa_cod[:, 0, 2 * P * t : 2 * P * (t + 1)].bitcast(FP4X4),
+                        lhsT_scale=wa_scl[:, 0, P * t : P * (t + 1)],
+                        rhs=x_cod[c][:].bitcast(FP8X4),
+                        rhs_scale=x_scl[c][:],
+                        start=True,
+                        stop=True,
+                    )
 
-        def make_gate(s, at=None):
-            gate[s] = place("gate%d" % s, [P, PACK * STEP], F32, at)
-            nc.scalar.activation(gate[s][:], ya[s][:].rearrange("p t j -> p (t j)"), SILU)
+        def make_gates(c, at=None):
+            gate[c] = place("gate%d" % c, [P, PACK, CHUNK], F32, at)
+            for u in range(2):
+                nc.scalar.activation(gate[c][:, 2 * u : 2 * u + 2, :], ya[c, u][:], SILU)
 
         def gather_words(c, at=None):
             got_w[c] = place("got_w%d" % c, [P, CHUNK], U32, at)
@@ -169,10 +173,10 @@ def tile_list_htabg_glu_none_kernel(
                 got_w[c][:].bitcast(U16).rearrange("p (j d) -> p d j", d=2),
             )
 
-        def round_wd(u):
-            nc.scalar.copy(
-                wd_bf[u][:].rearrange("p (c i t) -> p c t i", i=2, t=PACK),
-                wd_raw[:, :, u * CHUNK : (u + 1) * CHUNK].rearrange("p t (c i) -> p c t i", i=2),
+        def wd_views(u, n0, n1):
+            return (
+                wd_bf[u][:, n0 * PACK : n1 * PACK].rearrange("p (c i t) -> p c t i", i=2, t=PACK),
+                wd_raw[:, :, u * CHUNK + n0 : u * CHUNK + n1].rearrange("p t (c i) -> p c t i", i=2),
             )
 
         def quantize_wd(u):
@@ -203,7 +207,7 @@ def tile_list_htabg_glu_none_kernel(
             nc.vector.tensor_tensor(
                 h_bf[c][:, u * STEP * PACK : (u + 1) * STEP * PACK].rearrange("p (c i t) -> p c t i", i=2, t=PACK),
                 yb[s][:].rearrange("p t (c i) -> p c t i", i=2),
-                gate[s][:].rearrange("p (t c i) -> p c t i", t=PACK, i=2),
+                gate[c][:, :, u * STEP : (u + 1) * STEP].rearrange("p t (c i) -> p c t i", i=2),
                 MULT,
             )
 
@@ -276,64 +280,67 @@ def tile_list_htabg_glu_none_kernel(
 
         quantize_x(0)
         quantize_x(1)
-        for s in range(4):
-            gate_sums(s, s)
-        make_gate(0, AT_GATE0)
-        make_gate(1, AT_GATE0 + 2048)
-        make_gate(2)
-        gather_words(0)
+        gate_sums(0, 0)
+        gate_sums(1, 2)
+        make_gates(0, AT_GATE0)
+        make_gates(1)
+        gather_words(0, AT_WORDS)
         gather_words(1)
         part_words(0)
         part_words(1)
-        gather_words(2)
+        gather_words(2, AT_WORDS)
         quantize_x(2, AT_SCALES)
         quantize_x(3, AT_SCALES + CHUNK)
         for s, number in enumerate((4, 5, 0, 1)):
             memory_sums(s, number)
-        gate_sums(4, 6)
-        gate_sums(5, 7)
-        gate_sums(6, 2)
-        join(0)
-        join(1)
+        gate_sums(2, 6)
+        gate_sums(3, 2)
+        wd_bf = [sb("wd_bf0", [P, CHUNK * PACK], BF16), sb_at("wd_bf1", [P, CHUNK * PACK], BF16, AT_X3)]
+        nc.scalar.copy(*wd_views(0, 0, CHUNK))
+        for n0 in range(0, CHUNK, STEP):
+            nc.gpsimd.tensor_scalar(
+                wd_bf[1][:, n0 * PACK : (n0 + STEP) * PACK].rearrange("p (n t) -> p n t", t=PACK),
+                wd_raw[:, :, CHUNK + n0 : CHUNK + n0 + STEP].rearrange("p t n -> p n t"),
+                1.0,
+                0.0,
+                MULT,
+                ADD,
+            )
+        for s in range(3):
+            join(s)
         part_words(2, AT_GATE0)
-        gather_words(3, AT_GATE0 + 2048)
         quantize_h(0, 0, CHUNK)
-        join(2)
-        part_words(3)
-        memory_sums(4, 4)
-        memory_sums(5, 5)
-        for u in range(2):
-            round_wd(u)
-        for u in range(2):
-            quantize_wd(u)
-        output_sums(0, 0, 0)
-        for s in range(3, 7):
-            make_gate(s, AT_WD - 1024 + 2048 * (s - 3))
-        gate_sums(7, 3)
-        output_sums(0, 1, 6)
         join(3)
-        memory_sums(6, 1)
-        memory_sums(7, 7)
-        join(4)
+        memory_sums(4, 4)
+        quantize_wd(0)
         quantize_h(1, 0, CHUNK)
-        store(0, 0, nc.scalar.copy, AT_WD - 2048)
-        store(0, 1, nc.scalar.copy)
-        make_gate(7, AT_WD - 1024 + 2048 * 4)
-        output_sums(1, 0, 4)
-        output_sums(1, 1, 0)
+        gather_words(3, AT_WD - 960)
+        quantize_wd(1)
+        part_words(3)
+        output_sums(0, 0, 5)
+        output_sums(1, 0, 0)
+        make_gates(2, AT_WD + 64)
+        make_gates(3, AT_WD + 64 + 4096)
+        memory_sums(5, 6)
+        output_sums(0, 1, 1)
+        output_sums(1, 1, 7)
+        memory_sums(6, 2)
+        memory_sums(7, 3)
+        for c, u in ((0, 0), (1, 0), (0, 1), (1, 1)):
+            store(c, u, nc.scalar.copy)
+        join(4)
         join(5)
-        join(6)
-        quantize_h(2, 0, CHUNK)
-        store(1, 0, nc.scalar.copy)
-        store(1, 1, nc.scalar.copy)
-        output_sums(2, 0, 5)
+        for u in range(2):
+            quantize_h(2, u * STEP, (u + 1) * STEP)
+        output_sums(2, 0, 4)
         output_sums(2, 1, 6)
+        join(6)
         join(7)
         for u in range(2):
             quantize_h(3, u * STEP, (u + 1) * STEP)
         store(2, 0, nc.scalar.copy)
-        store(2, 1, nc.vector.tensor_copy)
-        last = [bank(number, "y3_%d" % m, [P, CHUNK]) for m, number in enumerate((2, 3, 1, 4))]
+        store(2, 1, nc.scalar.copy)
+        last = [bank(number, "y3_%d" % m, [P, CHUNK]) for m, number in enumerate((5, 0, 1, 7))]
         for u in range(2):
             for m in (0, 2, 1, 3):
                 output_pass(last[m][:, u * STEP : (u + 1) * STEP], 3, m, u * STEP, (u + 1) * STEP)

@@ -15,7 +15,6 @@ U8 = mybir.dt.uint8
 FP8X4 = mybir.dt.float8_e4m3fn_x4
 FP4X4 = mybir.dt.float4_e2m1fn_x4
 MULT = mybir.AluOpType.mult
-ADD = mybir.AluOpType.add
 SILU = mybir.ActivationFunctionType.Silu
 
 P = 128
@@ -77,7 +76,6 @@ def tile_list_htabg_glu_none_kernel(
         x_bf = [sb("x_bf%d" % c, [P, CHUNK * PACK], BF16) for c in range(3)]
         x_bf.append(sb_at("x_bf3", [P, CHUNK * PACK], BF16, AT_X3))
         h_bf = [sb("h_bf%d" % c, [P, CHUNK * PACK], BF16) for c in range(4)]
-        h_cod = [sb("h_cod%d" % c, [P, CHUNK], U32) for c in range(4)]
         h_scl = [sb("h_scl%d" % c, [P, CHUNK], U8) for c in range(4)]
 
         make_identity(nc, ident[:])
@@ -282,47 +280,36 @@ def tile_list_htabg_glu_none_kernel(
         quantize_x(1)
         gate_sums(0, 0)
         gate_sums(1, 2)
-        make_gates(0, AT_GATE0)
+        make_gates(0)
         make_gates(1)
-        gather_words(0, AT_WORDS)
-        gather_words(1)
-        part_words(0)
-        part_words(1)
-        gather_words(2, AT_WORDS)
+        for c in range(0, 4, 2):
+            gather_words(c, AT_WORDS + 1024)
+            gather_words(c + 1, AT_WORDS)
+            part_words(c)
+            part_words(c + 1)
         quantize_x(2, AT_SCALES)
         quantize_x(3, AT_SCALES + CHUNK)
         for s, number in enumerate((4, 5, 0, 1)):
             memory_sums(s, number)
         gate_sums(2, 6)
         gate_sums(3, 2)
-        wd_bf = [sb("wd_bf0", [P, CHUNK * PACK], BF16), sb_at("wd_bf1", [P, CHUNK * PACK], BF16, AT_X3)]
+        wd_bf = [sb("wd_bf0", [P, CHUNK * PACK], BF16), sb("wd_bf1", [P, CHUNK * PACK], BF16)]
         nc.scalar.copy(*wd_views(0, 0, CHUNK))
-        for n0 in range(0, CHUNK, STEP):
-            nc.gpsimd.tensor_scalar(
-                wd_bf[1][:, n0 * PACK : (n0 + STEP) * PACK].rearrange("p (n t) -> p n t", t=PACK),
-                wd_raw[:, :, CHUNK + n0 : CHUNK + n0 + STEP].rearrange("p t n -> p n t"),
-                1.0,
-                0.0,
-                MULT,
-                ADD,
-            )
-        for s in range(3):
+        nc.scalar.copy(*wd_views(1, 0, CHUNK))
+        for s in range(4):
             join(s)
-        part_words(2, AT_GATE0)
-        quantize_h(0, 0, CHUNK)
-        join(3)
         memory_sums(4, 4)
+        memory_sums(5, 5)
+        h_cod = [sb_at("h_cod%d" % c, [P, CHUNK], U32, AT_WD + 1024 * c) for c in range(4)]
         quantize_wd(0)
+        quantize_h(0, 0, CHUNK)
         quantize_h(1, 0, CHUNK)
-        gather_words(3, AT_WD - 960)
         quantize_wd(1)
-        part_words(3)
-        output_sums(0, 0, 5)
-        output_sums(1, 0, 0)
-        make_gates(2, AT_WD + 64)
-        make_gates(3, AT_WD + 64 + 4096)
-        memory_sums(5, 6)
-        output_sums(0, 1, 1)
+        output_sums(0, 0, 0)
+        output_sums(1, 0, 1)
+        make_gates(2)
+        make_gates(3)
+        output_sums(0, 1, 6)
         output_sums(1, 1, 7)
         memory_sums(6, 2)
         memory_sums(7, 3)
@@ -333,14 +320,14 @@ def tile_list_htabg_glu_none_kernel(
         for u in range(2):
             quantize_h(2, u * STEP, (u + 1) * STEP)
         output_sums(2, 0, 4)
-        output_sums(2, 1, 6)
+        output_sums(2, 1, 5)
         join(6)
         join(7)
         for u in range(2):
             quantize_h(3, u * STEP, (u + 1) * STEP)
         store(2, 0, nc.scalar.copy)
         store(2, 1, nc.scalar.copy)
-        last = [bank(number, "y3_%d" % m, [P, CHUNK]) for m, number in enumerate((5, 0, 1, 7))]
+        last = [bank(number, "y3_%d" % m, [P, CHUNK]) for m, number in enumerate((0, 1, 6, 7))]
         for u in range(2):
             for m in (0, 2, 1, 3):
                 output_pass(last[m][:, u * STEP : (u + 1) * STEP], 3, m, u * STEP, (u + 1) * STEP)

@@ -29,6 +29,7 @@ AT_GATE0 = 34816
 AT_WD = 43008
 AT_X3 = 53248
 AT_WORDS = 55296
+AT_FIRST = 57344
 
 
 def tile_list_htabg_glu_none_kernel(
@@ -125,14 +126,16 @@ def tile_list_htabg_glu_none_kernel(
                 raw[:].bitcast(U32).rearrange("p a (b t w) -> p a t b w", t=PACK, w=words),
             )
 
-        def gather_x(i, j0, j1):
+        def gather_x(i, j0, j1, target=None):
             entries = lst2[:, j0 // GROUP : j1 // GROUP]
-            nc.vector.tensor_tensor(got_x[:, i, j0:j1], x_pl[i][:].indirect(entries), wgt[:, j0:j1], MULT)
+            target = got_x[:, i, j0:j1] if target is None else target
+            nc.vector.tensor_tensor(target, x_pl[i][:].indirect(entries), wgt[:, j0:j1], MULT)
 
-        def round_x(c, t0, t1):
+        def round_x(c, t0, t1, source=None):
+            source = got_x[:, t0:t1, c * CHUNK : (c + 1) * CHUNK] if source is None else source
             nc.scalar.copy(
                 x_bf[c][:].rearrange("p (c i t) -> p c t i", i=2, t=PACK)[:, :, t0:t1, :],
-                got_x[:, t0:t1, c * CHUNK : (c + 1) * CHUNK].rearrange("p t (c i) -> p c t i", i=2),
+                source.rearrange("p t (c i) -> p c t i", i=2),
             )
 
         def quantize_x(c, scales_at=None):
@@ -264,19 +267,28 @@ def tile_list_htabg_glu_none_kernel(
         order_columns(wa_scl, was_raw, 2)
         gather_x(1, 0, SPLIT)
         gather_x(1, SPLIT, J)
-        for c in range(4):
+        for c in range(3):
             round_x(c, 0, 2)
-        gather_x(2, 0, J)
-        for c in range(4):
-            gather_x(3, c * CHUNK, (c + 1) * CHUNK)
+        got_first = sb_at("got_first", [P, 2, CHUNK], F32, AT_FIRST)
+        gather_x(2, 3 * CHUNK, J)
+        round_x(3, 0, 3)
+        gather_x(2, 0, CHUNK, got_first[:, 0, :])
+        got_second = sb_at("got_second", [P, 2, CHUNK], F32, AT_WORDS)
+        gather_x(2, CHUNK, 2 * CHUNK, got_second[:, 0, :])
+        gather_x(2, 2 * CHUNK, 3 * CHUNK)
+        gather_x(3, 0, CHUNK, got_first[:, 1, :])
+        gather_x(3, CHUNK, 2 * CHUNK, got_second[:, 1, :])
+        gather_x(3, 2 * CHUNK, 3 * CHUNK)
         order_columns(wa_cod, wa_raw, 4)
-        round_x(0, 2, PACK)
-        round_x(1, 2, PACK)
+        round_x(0, 2, PACK, got_first[:])
+        quantize_x(0)
+        got_last = sb_at("got_last", [P, 1, CHUNK], F32, AT_FIRST)
+        gather_x(3, 3 * CHUNK, J, got_last[:, 0, :])
+        round_x(1, 2, PACK, got_second[:])
         order_columns(wb_cod, wb_raw, 4)
         round_x(2, 2, PACK)
-        round_x(3, 2, PACK)
+        round_x(3, 3, PACK, got_last[:])
 
-        quantize_x(0)
         quantize_x(1)
         gate_sums(0, 0)
         gate_sums(1, 2)

@@ -107,8 +107,8 @@ def tile_list_htabg_glu_none_kernel(
         nc.sync.dma_start(x_pl[2][:], x_rows[2])
         nc.sync.dma_start(x_pl[3][:], x_rows[3])
         nc.sync.dma_start(wa_raw[:].bitcast(I32), wa_words.rearrange("a p c -> p a c").bitcast(I32))
-        nc.sync.dma_start(wb_raw[:].bitcast(I32), wb_words.rearrange("a p c -> p a c").bitcast(I32))
         nc.sync.dma_start(tab_w[:], tab_words[0].rearrange("p t b -> p (t b)").bitcast(I32))
+        nc.sync.dma_start(wb_raw[:].bitcast(I32), wb_words.rearrange("a p c -> p a c").bitcast(I32))
         for q in range(4):
             nc.sync.dma_start(v_scl[32 * q : 32 * q + 4, :, :].bitcast(I32), got_s[8 * q : 8 * q + 8, :].bitcast(I32))
         for t in range(PACK):
@@ -285,8 +285,8 @@ def tile_list_htabg_glu_none_kernel(
         got_last = sb_at("got_last", [P, 1, CHUNK], F32, AT_FIRST)
         gather_x(3, 3 * CHUNK, J, got_last[:, 0, :])
         round_x(1, 2, PACK, got_second[:])
-        order_columns(wb_cod, wb_raw, 4)
         round_x(2, 2, PACK)
+        order_columns(wb_cod, wb_raw, 4)
         round_x(3, 3, PACK, got_last[:])
 
         quantize_x(1)

@@ -15,6 +15,7 @@ U8 = mybir.dt.uint8
 FP8X4 = mybir.dt.float8_e4m3fn_x4
 FP4X4 = mybir.dt.float4_e2m1fn_x4
 MULT = mybir.AluOpType.mult
+ADD = mybir.AluOpType.add
 SILU = mybir.ActivationFunctionType.Silu
 
 P = 128
@@ -76,8 +77,8 @@ def tile_list_htabg_glu_none_kernel(
         wgt_cols = sb("wgt_cols", [P, J // P, P], F32)
         x_bf = [sb("x_bf%d" % c, [P, CHUNK * PACK], BF16) for c in range(3)]
         x_bf.append(sb_at("x_bf3", [P, CHUNK * PACK], BF16, AT_X3))
-        h_bf = [sb("h_bf%d" % c, [P, CHUNK * PACK], BF16) for c in range(4)]
-        h_scl = [sb("h_scl%d" % c, [P, CHUNK], U8) for c in range(4)]
+        h_bf = sb("h_bf", [P, J * PACK], BF16)
+        h_scl = sb("h_scl", [P, J], U8)
 
         make_identity(nc, ident[:])
         nc.vector.memset(warm[:], 0.0)
@@ -115,7 +116,7 @@ def tile_list_htabg_glu_none_kernel(
             nc.sync.dma_start(wd_raw[:, t, :], wd_rows[t])
 
         out_rows = out.rearrange("(m p) j -> p m j", p=P)
-        x_cod, x_scl, gate, got_w, v_cod, ya, yb, y = {}, {}, {}, {}, {}, {}, {}, {}
+        x_cod, x_scl, gate, got_w, v_cod, ya, yb = {}, {}, {}, {}, {}, {}, {}
 
         def place(name, shape, dtype, offset):
             return sb(name, shape, dtype) if offset is None else sb_at(name, shape, dtype, offset)
@@ -206,39 +207,32 @@ def tile_list_htabg_glu_none_kernel(
         def join(s):
             c, u = divmod(s, 2)
             nc.vector.tensor_tensor(
-                h_bf[c][:, u * STEP * PACK : (u + 1) * STEP * PACK].rearrange("p (c i t) -> p c t i", i=2, t=PACK),
+                h_bf[:, s * STEP * PACK : (s + 1) * STEP * PACK].rearrange("p (c i t) -> p c t i", i=2, t=PACK),
                 yb[s][:].rearrange("p t (c i) -> p c t i", i=2),
                 gate[c][:, :, u * STEP : (u + 1) * STEP].rearrange("p t (c i) -> p c t i", i=2),
                 MULT,
             )
 
-        def quantize_h(c, j0, j1):
+        def quantize_h(j0, j1):
             nc.vector.quantize_mx(
-                out=h_cod[c][:, j0:j1].bitcast(FP8X4),
-                scales=h_scl[c][:, j0:j1],
-                in_=h_bf[c][:, j0 * PACK : j1 * PACK],
+                out=h_cod[:, j0:j1].bitcast(FP8X4), scales=h_scl[:, j0:j1], in_=h_bf[:, j0 * PACK : j1 * PACK]
             )
 
-        def output_pass(target, c, m, j0, j1):
+        def output_pass(target, m, j0, j1):
             nc.tensor.matmul_mx(
                 out=target,
                 lhsT=wd_cod[:, P * m : P * (m + 1)].bitcast(FP8X4),
                 lhsT_scale=wd_scl[:, P * m : P * (m + 1)],
-                rhs=h_cod[c][:, j0:j1].bitcast(FP8X4),
-                rhs_scale=h_scl[c][:, j0:j1],
+                rhs=h_cod[:, j0:j1].bitcast(FP8X4),
+                rhs_scale=h_scl[:, j0:j1],
                 start=True,
                 stop=True,
             )
 
-        def output_sums(c, u, number):
-            y[c, u] = bank(number, "y%d_%d" % (c, u), [P, 2, CHUNK])
-            for m in range(2):
-                output_pass(y[c, u][:, m, :], c, 2 * u + m, 0, CHUNK)
-
-        def store(c, u, copy, at=None):
-            y_sb = place("y_sb%d_%d" % (c, u), [P, 2, CHUNK], F32, at)
-            copy(y_sb[:], y[c, u][:])
-            nc.sync.dma_start(out_rows[:, 2 * u : 2 * u + 2, c * CHUNK : (c + 1) * CHUNK], y_sb[:])
+        def store(name, sums, rows, copy):
+            y_sb = sb(name, sums.shape, F32)
+            copy(y_sb[:], sums)
+            nc.sync.dma_start(rows, y_sb[:])
 
         turned = bank(6, "turned", [P, P])
         nc.tensor.transpose(turned[:], wgt_rows[:], ident[:])
@@ -305,45 +299,58 @@ def tile_list_htabg_glu_none_kernel(
             memory_sums(s, number)
         gate_sums(2, 6)
         gate_sums(3, 2)
-        wd_bf = [sb("wd_bf0", [P, CHUNK * PACK], BF16), sb("wd_bf1", [P, CHUNK * PACK], BF16)]
+        wd_bf = [sb("wd_bf0", [P, CHUNK * PACK], BF16), sb_at("wd_bf1", [P, CHUNK * PACK], BF16, AT_X3 + 1024)]
         nc.scalar.copy(*wd_views(0, 0, CHUNK))
-        nc.scalar.copy(*wd_views(1, 0, CHUNK))
+        nc.scalar.copy(*wd_views(1, 0, STEP))
+        nc.gpsimd.tensor_scalar(
+            wd_bf[1][:, STEP * PACK :].rearrange("p (n t) -> p n t", t=PACK),
+            wd_raw[:, :, N - STEP :].rearrange("p t n -> p n t"),
+            1.0,
+            0.0,
+            MULT,
+            ADD,
+        )
         for s in range(4):
             join(s)
         memory_sums(4, 4)
         memory_sums(5, 5)
-        h_cod = [sb_at("h_cod%d" % c, [P, CHUNK], U32, AT_WD + 1024 * c) for c in range(4)]
+        h_cod = sb_at("h_cod", [P, J], U32, AT_WD)
         quantize_wd(0)
-        quantize_h(0, 0, CHUNK)
-        quantize_h(1, 0, CHUNK)
+        quantize_h(0, CHUNK)
+        quantize_h(CHUNK, HALF)
         quantize_wd(1)
-        output_sums(0, 0, 0)
-        output_sums(1, 0, 1)
+        upper = [bank(c, "y_upper%d" % c, [P, 2, CHUNK]) for c in range(2)]
+        for c in range(2):
+            for m in range(2):
+                output_pass(upper[c][:, m, :], m, c * CHUNK, (c + 1) * CHUNK)
         make_gates(2)
         make_gates(3)
-        output_sums(0, 1, 6)
-        output_sums(1, 1, 7)
+        lower = [bank(6 + u, "y_lower%d" % u, [P, HALF]) for u in range(2)]
+        for u in range(2):
+            output_pass(lower[u][:], 2 + u, 0, HALF)
         memory_sums(6, 2)
         memory_sums(7, 3)
-        for c, u in ((0, 0), (1, 0), (0, 1), (1, 1)):
-            store(c, u, nc.scalar.copy)
+        for c in range(2):
+            store("upper_sb%d" % c, upper[c][:], out_rows[:, 0:2, c * CHUNK : (c + 1) * CHUNK], nc.scalar.copy)
+        for u in range(2):
+            store("lower_sb%d" % u, lower[u][:], out_rows[:, 2 + u, 0:HALF], nc.scalar.copy)
         join(4)
         join(5)
-        for u in range(2):
-            quantize_h(2, u * STEP, (u + 1) * STEP)
-        output_sums(2, 0, 4)
-        output_sums(2, 1, 5)
+        for s in range(4, 6):
+            quantize_h(s * STEP, (s + 1) * STEP)
+        third = [bank(4 + u, "y_third%d" % u, [P, 2, CHUNK]) for u in range(2)]
+        for m in range(N // P):
+            output_pass(third[m // 2][:, m % 2, :], m, HALF, 3 * CHUNK)
         join(6)
         join(7)
+        for s in range(6, 8):
+            quantize_h(s * STEP, (s + 1) * STEP)
         for u in range(2):
-            quantize_h(3, u * STEP, (u + 1) * STEP)
-        store(2, 0, nc.scalar.copy)
-        store(2, 1, nc.scalar.copy)
-        last = [bank(number, "y3_%d" % m, [P, CHUNK]) for m, number in enumerate((0, 1, 6, 7))]
+            store("third_sb%d" % u, third[u][:], out_rows[:, 2 * u : 2 * u + 2, HALF : 3 * CHUNK], nc.scalar.copy)
+        last = [bank(number, "y_last%d" % m, [P, CHUNK]) for m, number in enumerate((0, 1, 6, 7))]
         for u in range(2):
             for m in (0, 2, 1, 3):
-                output_pass(last[m][:, u * STEP : (u + 1) * STEP], 3, m, u * STEP, (u + 1) * STEP)
+                output_pass(last[m][:, u * STEP : (u + 1) * STEP], m, (6 + u) * STEP, (7 + u) * STEP)
         for m in (0, 2, 1, 3):
-            y_sb = sb("y_last%d" % m, [P, CHUNK], F32)
-            (nc.scalar.copy if m < 2 else nc.vector.tensor_copy)(y_sb[:], last[m][:])
-            nc.sync.dma_start(out_rows[:, m, 3 * CHUNK : 4 * CHUNK], y_sb[:])
+            copy = nc.scalar.copy if m < 2 else nc.vector.tensor_copy
+            store("last_sb%d" % m, last[m][:], out_rows[:, m, 3 * CHUNK : J], copy)

@@ -43,10 +43,10 @@ def tile_list_htabg_glu_none_kernel(
         psum = ctx.enter_context(tc.psum_pool(name="psum", bufs=1))
 
         def sb(name, shape, dtype):
-            return keep.tile(shape, dtype, name=name, tag=name, align_bytes=64)
+            return keep.tile(shape, dtype, name=name, tag=name, align_bytes=256)
 
         def sb_at(name, shape, dtype, offset):
-            return reuse.tile(shape, dtype, name=name, tag=name, align_bytes=64, offset=offset)
+            return reuse.tile(shape, dtype, name=name, tag=name, align_bytes=256, offset=offset)
 
         def bank(number, name, shape):
             return psum.tile(shape, F32, name=name, tag="bank%d" % number)

@@ -24,12 +24,13 @@ GROUP = 16
 CHUNK = 256
 HALF = 512
 STEP = 128
-SPLIT = 640
+SPLIT = 544
+WARM_PASSES = 6
 AT_SCALES = 32768
 AT_GATE0 = 34816
 AT_WD = 43008
 AT_X3 = 53248
-AT_WORDS = 55296
+AT_WORDS = 61440
 AT_FIRST = 57344
 
 
@@ -274,25 +275,41 @@ def tile_list_htabg_glu_none_kernel(
         gather_x(3, CHUNK, 2 * CHUNK, got_second[:, 1, :])
         gather_x(3, 2 * CHUNK, 3 * CHUNK)
         order_columns(wa_cod, wa_raw, 4)
+        idle = bank(4, "idle", [P, CHUNK])
+        for t in range(WARM_PASSES):
+            nc.tensor.matmul_mx(
+                out=idle[:],
+                lhsT=wa_cod[:, 0, 0 : 2 * P].bitcast(FP4X4),
+                lhsT_scale=wa_scl[:, 0, 0:P],
+                rhs=wa_cod[:, 0, 0 : 2 * CHUNK].bitcast(FP4X4),
+                rhs_scale=wa_scl[:, 0, 0:CHUNK],
+                start=True,
+                stop=True,
+            )
         round_x(0, 2, PACK, got_first[:])
         quantize_x(0)
-        got_last = sb_at("got_last", [P, 1, CHUNK], F32, AT_FIRST)
-        gather_x(3, 3 * CHUNK, J, got_last[:, 0, :])
         round_x(1, 2, PACK, got_second[:])
         round_x(2, 2, PACK)
         order_columns(wb_cod, wb_raw, 4)
-        round_x(3, 3, PACK, got_last[:])
 
         quantize_x(1)
         gate_sums(0, 0)
         gate_sums(1, 2)
         make_gates(0)
         make_gates(1)
-        for c in range(0, 4, 2):
-            gather_words(c, AT_WORDS + 1024)
-            gather_words(c + 1, AT_WORDS)
-            part_words(c)
-            part_words(c + 1)
+        gather_words(0, AT_WORDS + 1024)
+        gather_words(1, AT_WORDS)
+        part_words(0)
+        part_words(1)
+        got_last = sb_at("got_last", [P, CHUNK], F32, AT_WORDS + 1536)
+        gather_x(3, 3 * CHUNK, J, got_last[:])
+        nc.gpsimd.tensor_scalar(
+            x_bf[3][:].rearrange("p (n t) -> p n t", t=PACK)[:, :, PACK - 1], got_last[:], 1.0, 0.0, MULT, ADD
+        )
+        gather_words(2, AT_WORDS - 512)
+        gather_words(3, AT_WORDS + 512)
+        part_words(2)
+        part_words(3)
         quantize_x(2, AT_SCALES)
         quantize_x(3, AT_SCALES + CHUNK)
         for s, number in enumerate((4, 5, 0, 1)):

@@ -24,14 +24,16 @@ GROUP = 16
 CHUNK = 256
 HALF = 512
 STEP = 128
-SPLIT = 544
-WARM_PASSES = 6
+SPLIT = 640
+SHARE = 192
 AT_SCALES = 32768
 AT_GATE0 = 34816
 AT_WD = 43008
 AT_X3 = 53248
 AT_WORDS = 61440
 AT_FIRST = 57344
+AT_H = 65536
+AT_STAGED = 67584
 
 
 def tile_list_htabg_glu_none_kernel(
@@ -78,8 +80,6 @@ def tile_list_htabg_glu_none_kernel(
         wgt_cols = sb("wgt_cols", [P, J // P, P], F32)
         x_bf = [sb("x_bf%d" % c, [P, CHUNK * PACK], BF16) for c in range(3)]
         x_bf.append(sb_at("x_bf3", [P, CHUNK * PACK], BF16, AT_X3))
-        h_bf = sb("h_bf", [P, J * PACK], BF16)
-        h_scl = sb("h_scl", [P, J], U8)
 
         make_identity(nc, ident[:])
         nc.vector.memset(warm[:], 0.0)
@@ -111,13 +111,15 @@ def tile_list_htabg_glu_none_kernel(
         nc.sync.dma_start(wa_raw[:].bitcast(I32), wa_words.rearrange("a p c -> p a c").bitcast(I32))
         nc.sync.dma_start(tab_w[:], tab_words[0].rearrange("p t b -> p (t b)").bitcast(I32))
         nc.sync.dma_start(wb_raw[:].bitcast(I32), wb_words.rearrange("a p c -> p a c").bitcast(I32))
+        for t in range(2):
+            nc.sync.dma_start(wd_raw[:, t, :], wd_rows[t])
         for q in range(4):
             nc.sync.dma_start(v_scl[32 * q : 32 * q + 4, :, :].bitcast(I32), got_s[8 * q : 8 * q + 8, :].bitcast(I32))
-        for t in range(PACK):
+        for t in range(2, PACK):
             nc.sync.dma_start(wd_raw[:, t, :], wd_rows[t])
 
         out_rows = out.rearrange("(m p) j -> p m j", p=P)
-        x_cod, x_scl, gate, got_w, v_cod, ya, yb = {}, {}, {}, {}, {}, {}, {}
+        x_cod, x_scl, gate, got_w, v_cod, ya, yb, h_bf, y = {}, {}, {}, {}, {}, {}, {}, {}, {}
 
         def place(name, shape, dtype, offset):
             return sb(name, shape, dtype) if offset is None else sb_at(name, shape, dtype, offset)
@@ -145,9 +147,9 @@ def tile_list_htabg_glu_none_kernel(
             x_scl[c] = place("x_scl%d" % c, [P, CHUNK], U8, scales_at)
             nc.vector.quantize_mx(out=x_cod[c][:].bitcast(FP8X4), scales=x_scl[c][:], in_=x_bf[c][:])
 
-        def gate_sums(c, first_bank):
+        def gate_sums(c, numbers):
             for u in range(2):
-                ya[c, u] = bank(first_bank + u, "ya%d_%d" % (c, u), [P, 2, CHUNK])
+                ya[c, u] = bank(numbers[u], "ya%d_%d" % (c, u), [P, 2, CHUNK])
                 for t in range(2 * u, 2 * u + 2):
                     nc.tensor.matmul_mx(
                         out=ya[c, u][:, t - 2 * u, :],
@@ -208,30 +210,43 @@ def tile_list_htabg_glu_none_kernel(
         def join(s):
             c, u = divmod(s, 2)
             nc.vector.tensor_tensor(
-                h_bf[:, s * STEP * PACK : (s + 1) * STEP * PACK].rearrange("p (c i t) -> p c t i", i=2, t=PACK),
+                h_bf[s].rearrange("p (c i t) -> p c t i", i=2, t=PACK),
                 yb[s][:].rearrange("p t (c i) -> p c t i", i=2),
                 gate[c][:, :, u * STEP : (u + 1) * STEP].rearrange("p t (c i) -> p c t i", i=2),
                 MULT,
             )
 
-        def quantize_h(j0, j1):
-            nc.vector.quantize_mx(
-                out=h_cod[:, j0:j1].bitcast(FP8X4), scales=h_scl[:, j0:j1], in_=h_bf[:, j0 * PACK : j1 * PACK]
-            )
+        def h_tile(s, steps, at=None):
+            whole = place("h_bf%d" % s, [P, steps * STEP * PACK], BF16, at)
+            for u in range(steps):
+                h_bf[s + u] = whole[:, u * STEP * PACK : (u + 1) * STEP * PACK]
+            return whole[:]
 
-        def output_pass(target, m, j0, j1):
+        def quantize_h(j0, j1, source, scales):
+            nc.vector.quantize_mx(out=h_cod[:, j0:j1].bitcast(FP8X4), scales=scales, in_=source)
+
+        def output_pass(target, m, j0, j1, scales):
             nc.tensor.matmul_mx(
                 out=target,
                 lhsT=wd_cod[:, P * m : P * (m + 1)].bitcast(FP8X4),
                 lhsT_scale=wd_scl[:, P * m : P * (m + 1)],
                 rhs=h_cod[:, j0:j1].bitcast(FP8X4),
-                rhs_scale=h_scl[:, j0:j1],
+                rhs_scale=scales,
                 start=True,
                 stop=True,
             )
 
-        def store(name, sums, rows, copy):
-            y_sb = sb(name, sums.shape, F32)
+        def output_sums(c, numbers, scales):
+            for u in range(2):
+                y[c, u] = bank(numbers[u], "y%d_%d" % (c, u), [P, 2, CHUNK])
+                for m in range(2):
+                    output_pass(y[c, u][:, m, :], 2 * u + m, c * CHUNK, (c + 1) * CHUNK, scales)
+
+        def store_half(c, u, copy=nc.scalar.copy, at=None):
+            store("y_sb%d_%d" % (c, u), y[c, u][:], out_rows[:, 2 * u : 2 * u + 2, c * CHUNK : (c + 1) * CHUNK], copy, at)
+
+        def store(name, sums, rows, copy, at=None):
+            y_sb = place(name, sums.shape, F32, at)
             copy(y_sb[:], sums)
             nc.sync.dma_start(rows, y_sb[:])
 
@@ -275,99 +290,96 @@ def tile_list_htabg_glu_none_kernel(
         gather_x(3, CHUNK, 2 * CHUNK, got_second[:, 1, :])
         gather_x(3, 2 * CHUNK, 3 * CHUNK)
         order_columns(wa_cod, wa_raw, 4)
-        idle = bank(4, "idle", [P, CHUNK])
-        for t in range(WARM_PASSES):
-            nc.tensor.matmul_mx(
-                out=idle[:],
-                lhsT=wa_cod[:, 0, 0 : 2 * P].bitcast(FP4X4),
-                lhsT_scale=wa_scl[:, 0, 0:P],
-                rhs=wa_cod[:, 0, 0 : 2 * CHUNK].bitcast(FP4X4),
-                rhs_scale=wa_scl[:, 0, 0:CHUNK],
-                start=True,
-                stop=True,
-            )
         round_x(0, 2, PACK, got_first[:])
         quantize_x(0)
+        got_last = sb_at("got_last", [P, CHUNK], F32, AT_FIRST)
+        gather_x(3, 3 * CHUNK, J, got_last[:])
         round_x(1, 2, PACK, got_second[:])
         round_x(2, 2, PACK)
         order_columns(wb_cod, wb_raw, 4)
-
-        quantize_x(1)
-        gate_sums(0, 0)
-        gate_sums(1, 2)
-        make_gates(0)
-        make_gates(1)
-        gather_words(0, AT_WORDS + 1024)
-        gather_words(1, AT_WORDS)
-        part_words(0)
-        part_words(1)
-        got_last = sb_at("got_last", [P, CHUNK], F32, AT_WORDS + 1536)
-        gather_x(3, 3 * CHUNK, J, got_last[:])
         nc.gpsimd.tensor_scalar(
             x_bf[3][:].rearrange("p (n t) -> p n t", t=PACK)[:, :, PACK - 1], got_last[:], 1.0, 0.0, MULT, ADD
         )
+
+        quantize_x(1)
+        gate_sums(0, (0, 1))
+        gate_sums(1, (2, 3))
+        make_gates(0)
+        make_gates(1)
+        gather_words(0, AT_WORDS)
+        gather_words(1, AT_WORDS + 1024)
+        part_words(0)
+        part_words(1)
         gather_words(2, AT_WORDS - 512)
         gather_words(3, AT_WORDS + 512)
         part_words(2)
         part_words(3)
         quantize_x(2, AT_SCALES)
         quantize_x(3, AT_SCALES + CHUNK)
-        for s, number in enumerate((4, 5, 0, 1)):
+        for s, number in ((0, 4), (3, 1), (1, 5), (2, 0)):
             memory_sums(s, number)
-        gate_sums(2, 6)
-        gate_sums(3, 2)
-        wd_bf = [sb("wd_bf0", [P, CHUNK * PACK], BF16), sb_at("wd_bf1", [P, CHUNK * PACK], BF16, AT_X3 + 1024)]
+        gate_sums(2, (6, 7))
+        gate_sums(3, (2, 3))
+        wd_bf = [sb("wd_bf0", [P, CHUNK * PACK], BF16), sb_at("wd_bf1", [P, CHUNK * PACK], BF16, AT_WORDS + 1536)]
         nc.scalar.copy(*wd_views(0, 0, CHUNK))
-        nc.scalar.copy(*wd_views(1, 0, STEP))
         nc.gpsimd.tensor_scalar(
-            wd_bf[1][:, STEP * PACK :].rearrange("p (n t) -> p n t", t=PACK),
-            wd_raw[:, :, N - STEP :].rearrange("p t n -> p n t"),
+            wd_bf[1][:, (CHUNK - SHARE) * PACK :].rearrange("p (n t) -> p n t", t=PACK),
+            wd_raw[:, :, N - SHARE :].rearrange("p t n -> p n t"),
             1.0,
             0.0,
             MULT,
             ADD,
         )
-        for s in range(4):
+        staged = sb("staged", [P, STEP, PACK], F32)
+        nc.scalar.copy(staged[:], yb[3][:].rearrange("p t n -> p n t"))
+        nc.scalar.copy(*wd_views(1, 0, CHUNK - SHARE))
+        h_first = h_tile(0, 2)
+        h_second = h_tile(2, 2, AT_X3)
+        nc.gpsimd.tensor_tensor(
+            h_bf[3].rearrange("p (n t) -> p n t", t=PACK), staged[:], gate[1][:, :, STEP:].rearrange("p t n -> p n t"), MULT
+        )
+        for s in range(3):
             join(s)
-        memory_sums(4, 4)
-        memory_sums(5, 5)
-        h_cod = sb_at("h_cod", [P, J], U32, AT_WD)
-        quantize_wd(0)
-        quantize_h(0, CHUNK)
-        quantize_h(CHUNK, HALF)
-        quantize_wd(1)
-        upper = [bank(c, "y_upper%d" % c, [P, 2, CHUNK]) for c in range(2)]
-        for c in range(2):
-            for m in range(2):
-                output_pass(upper[c][:, m, :], m, c * CHUNK, (c + 1) * CHUNK)
+        memory_sums(4, 1)
+        memory_sums(5, 4)
         make_gates(2)
         make_gates(3)
-        lower = [bank(6 + u, "y_lower%d" % u, [P, HALF]) for u in range(2)]
-        for u in range(2):
-            output_pass(lower[u][:], 2 + u, 0, HALF)
+        h_cod = sb_at("h_cod", [P, J], U32, AT_WD)
+        first_scl = sb("first_scl", [P, CHUNK], U8)
+        second_scl = sb("second_scl", [P, CHUNK], U8)
+        quantize_wd(0)
+        quantize_h(0, CHUNK, h_first, first_scl[:])
+        quantize_wd(1)
+        output_sums(0, (5, 0), first_scl[:])
+        store_half(0, 0)
+        store_half(0, 1)
+        h_tile(4, 1, AT_WD + 4096)
+        join(4)
+        quantize_h(CHUNK, HALF, h_second, second_scl[:])
+        output_sums(1, (6, 7), second_scl[:])
         memory_sums(6, 2)
         memory_sums(7, 3)
-        for c in range(2):
-            store("upper_sb%d" % c, upper[c][:], out_rows[:, 0:2, c * CHUNK : (c + 1) * CHUNK], nc.scalar.copy)
-        for u in range(2):
-            store("lower_sb%d" % u, lower[u][:], out_rows[:, 2 + u, 0:HALF], nc.scalar.copy)
-        join(4)
+        store_half(1, 0)
+        store_half(1, 1)
+        third_scl = sb("third_scl", [P, CHUNK], U8)
+        quantize_h(4 * STEP, 5 * STEP, h_bf[4], third_scl[:, 0:STEP])
+        h_tile(5, 1, AT_X3)
         join(5)
-        for s in range(4, 6):
-            quantize_h(s * STEP, (s + 1) * STEP)
-        third = [bank(4 + u, "y_third%d" % u, [P, 2, CHUNK]) for u in range(2)]
-        for m in range(N // P):
-            output_pass(third[m // 2][:, m % 2, :], m, HALF, 3 * CHUNK)
+        h_tile(6, 2)
         join(6)
+        quantize_h(5 * STEP, 6 * STEP, h_bf[5], third_scl[:, STEP:])
+        output_sums(2, (1, 4), third_scl[:])
+        store_half(2, 0)
+        store_half(2, 1)
         join(7)
+        last_scl = sb("last_scl", [P, CHUNK], U8)
         for s in range(6, 8):
-            quantize_h(s * STEP, (s + 1) * STEP)
-        for u in range(2):
-            store("third_sb%d" % u, third[u][:], out_rows[:, 2 * u : 2 * u + 2, HALF : 3 * CHUNK], nc.scalar.copy)
-        last = [bank(number, "y_last%d" % m, [P, CHUNK]) for m, number in enumerate((0, 1, 6, 7))]
+            quantize_h(s * STEP, (s + 1) * STEP, h_bf[s], last_scl[:, (s - 6) * STEP : (s - 5) * STEP])
+        last = [bank(number, "y_last%d" % m, [P, CHUNK]) for m, number in enumerate((5, 0, 6, 7))]
         for u in range(2):
             for m in (0, 2, 1, 3):
-                output_pass(last[m][:, u * STEP : (u + 1) * STEP], m, (6 + u) * STEP, (7 + u) * STEP)
+                scales = last_scl[:, u * STEP : (u + 1) * STEP]
+                output_pass(last[m][:, u * STEP : (u + 1) * STEP], m, (6 + u) * STEP, (7 + u) * STEP, scales)
         for m in (0, 2, 1, 3):
             copy = nc.scalar.copy if m < 2 else nc.vector.tensor_copy
             store("last_sb%d" % m, last[m][:], out_rows[:, m, 3 * CHUNK : J], copy)

from contextlib import ExitStack

import concourse.mybir as mybir
from concourse.masks import make_identity

K, L, R, N, T, J = 512, 1024, 512, 512, 2048, 1024
FLOPS = 2 * J * (K * R + L * R + R * N)

F32 = mybir.dt.float32
BF16 = mybir.dt.bfloat16
I32 = mybir.dt.int32
U32 = mybir.dt.uint32
U16 = mybir.dt.uint16
U8 = mybir.dt.uint8
FP8X4 = mybir.dt.float8_e4m3fn_x4
FP4X4 = mybir.dt.float4_e2m1fn_x4
MULT = mybir.AluOpType.mult
ADD = mybir.AluOpType.add
SILU = mybir.ActivationFunctionType.Silu

P = 128
PACK = 4
GROUP = 16
CHUNK = 256
HALF = 512
STEP = 128
SPLIT = 640
SHARE = 192
AT_SCALES = 32768
AT_GATE0 = 34816
AT_WD = 43008
AT_X3 = 53248
AT_WORDS = 61440
AT_FIRST = 57344
AT_H = 65536
AT_STAGED = 67584


def tile_list_htabg_glu_none_kernel(
    tc, tab_words, tab_scales, xT, wgt2, wa_words, wa_scales, wb_words, wb_scales, wd, offs, offs2, out
):
    nc = tc.nc
    with ExitStack() as ctx:
        keep = ctx.enter_context(tc.tile_pool(name="keep", bufs=1))
        reuse = ctx.enter_context(tc.tile_pool(name="reuse", bufs=1))
        psum = ctx.enter_context(tc.psum_pool(name="psum", bufs=1))

        def sb(name, shape, dtype):
            return keep.tile(shape, dtype, name=name, tag=name, align_bytes=256)

        def sb_at(name, shape, dtype, offset):
            return reuse.tile(shape, dtype, name=name, tag=name, align_bytes=256, offset=offset)

        def bank(number, name, shape):
            return psum.tile(shape, F32, name=name, tag="bank%d" % number)

        lst = keep.tile([P, J // GROUP], U16, name="lst")
        lst2 = keep.tile([P, J // GROUP], U16, name="lst2")
        tab_s = sb("tab_s", [P, T], U8)
        tab_w = sb("tab_w", [P, T], I32)
        wgt = sb("wgt", [P, J], F32)
        got_x = sb("got_x", [P, PACK, J], F32)
        x_pl = [sb_at("x_pl%d" % i, [P, T], F32, 8192 * i) for i in range(PACK)]
        got_s = sb_at("got_s", [P, J], U8, AT_SCALES)
        wd_raw = sb_at("wd_raw", [P, PACK, N], F32, AT_WD)
        wa_raw = sb("wa_raw", [P, 1, 2 * R], U8)
        wb_raw = sb("wb_raw", [P, 2, 2 * R], U8)
        wa_cod = sb("wa_cod", [P, 1, 2 * R], U8)
        wb_cod = sb("wb_cod", [P, 2, 2 * R], U8)
        was_raw = sb("was_raw", [P, 1, R], U8)
        wbs_raw = sb("wbs_raw", [P, R], U8)
        wb_scl = sb("wb_scl", [P, 2, R], U8)
        wd_cod = sb("wd_cod", [P, N], U32)
        wd_scl = sb("wd_scl", [P, N], U8)
        v_scl = sb("v_scl", [P, 2, J], U8)
        warm = sb("warm", [P, 8], F32)
        warm_out = sb("warm_out", [P, 8], F32)
        ident = sb("ident", [P, P], F32)
        wgt_rows = sb("wgt_rows", [P, P], F32)
        wgt_cols = sb("wgt_cols", [P, J // P, P], F32)
        x_bf = [sb("x_bf%d" % c, [P, CHUNK * PACK], BF16) for c in range(3)]
        x_bf.append(sb_at("x_bf3", [P, CHUNK * PACK], BF16, AT_X3))

        make_identity(nc, ident[:])
        nc.vector.memset(warm[:], 0.0)
        nc.vector.memset(wgt_rows[64:128, :], 0.0)
        nc.vector.memset(was_raw[:].rearrange("p a r -> p (a r)").bitcast(I32), 0)
        nc.vector.memset(tab_s[32:64, :].bitcast(I32), 0)
        nc.vector.memset(tab_s[64:128, :].bitcast(I32), 0)
        nc.vector.memset(wb_scl[:].rearrange("p a r -> p (a r)").bitcast(I32), 0)
        nc.vector.memset(v_scl[:].rearrange("p a j -> p (a j)").bitcast(I32), 0)
        nc.scalar.activation(warm_out[:], warm[:], SILU)

        x_rows = xT.rearrange("(p i) t -> i p t", i=PACK)
        wd_rows = wd.rearrange("(b t q) n -> t b q n", t=PACK, q=8)
        for q in range(4):
            nc.scalar.dma_start(
                was_raw[32 * q : 32 * q + 4, :, :].bitcast(I32),
                wa_scales[:, 4 * q : 4 * q + 4, :].rearrange("a q r -> q a r").bitcast(I32),
            )
        nc.sync.dma_start(wgt_rows[0:64, :], wgt2.rearrange("(g r) (c j) -> r c g j", r=GROUP, j=P)[0])
        nc.sync.dma_start(tab_s[0:32, :].bitcast(I32), tab_scales.rearrange("a q t -> q a t").bitcast(I32))
        nc.sync.dma_start(lst[:], offs)
        nc.sync.dma_start(x_pl[0][:], x_rows[0])
        nc.sync.dma_start(lst2[:], offs2)
        nc.sync.dma_start(wbs_raw[0:32, :].bitcast(I32), wb_scales.rearrange("a q r -> q a r").bitcast(I32))
        nc.sync.dma_start(x_pl[1][:], x_rows[1])
        nc.vector.tensor_copy(got_s[:], tab_s[:].indirect(lst[:]))
        nc.sync.dma_start(x_pl[2][:], x_rows[2])
        nc.sync.dma_start(x_pl[3][:], x_rows[3])
        nc.sync.dma_start(wa_raw[:].bitcast(I32), wa_words.rearrange("a p c -> p a c").bitcast(I32))
        nc.sync.dma_start(tab_w[:], tab_words[0].rearrange("p t b -> p (t b)").bitcast(I32))
        nc.sync.dma_start(wb_raw[:].bitcast(I32), wb_words.rearrange("a p c -> p a c").bitcast(I32))
        for t in range(2):
            nc.sync.dma_start(wd_raw[:, t, :], wd_rows[t])
        for q in range(4):
            nc.sync.dma_start(v_scl[32 * q : 32 * q + 4, :, :].bitcast(I32), got_s[8 * q : 8 * q + 8, :].bitcast(I32))
        for t in range(2, PACK):
            nc.sync.dma_start(wd_raw[:, t, :], wd_rows[t])

        out_rows = out.rearrange("(m p) j -> p m j", p=P)
        x_cod, x_scl, gate, got_w, v_cod, ya, yb, h_bf, y = {}, {}, {}, {}, {}, {}, {}, {}, {}

        def place(name, shape, dtype, offset):
            return sb(name, shape, dtype) if offset is None else sb_at(name, shape, dtype, offset)

        def order_columns(ordered, raw, words):
            nc.scalar.copy(
                ordered[:].bitcast(U32).rearrange("p a (t b w) -> p a t b w", t=PACK, w=words),
                raw[:].bitcast(U32).rearrange("p a (b t w) -> p a t b w", t=PACK, w=words),
            )

        def gather_x(i, j0, j1, target=None):
            entries = lst2[:, j0 // GROUP : j1 // GROUP]
            target = got_x[:, i, j0:j1] if target is None else target
            nc.vector.tensor_tensor(target, x_pl[i][:].indirect(entries), wgt[:, j0:j1], MULT)

        def round_x(c, t0, t1, source=None):
            source = got_x[:, t0:t1, c * CHUNK : (c + 1) * CHUNK] if source is None else source
            nc.scalar.copy(
                x_bf[c][:].rearrange("p (c i t) -> p c t i", i=2, t=PACK)[:, :, t0:t1, :],
                source.rearrange("p t (c i) -> p c t i", i=2),
            )

        def quantize_x(c, scales_at=None):
            x_cod[c] = sb("x_cod%d" % c, [P, CHUNK], U32)
            x_scl[c] = place("x_scl%d" % c, [P, CHUNK], U8, scales_at)
            nc.vector.quantize_mx(out=x_cod[c][:].bitcast(FP8X4), scales=x_scl[c][:], in_=x_bf[c][:])

        def gate_sums(c, numbers):
            for u in range(2):
                ya[c, u] = bank(numbers[u], "ya%d_%d" % (c, u), [P, 2, CHUNK])
                for t in range(2 * u, 2 * u + 2):
                    nc.tensor.matmul_mx(
                        out=ya[c, u][:, t - 2 * u, :],
                        lhsT=wa_cod[:, 0, 2 * P * t : 2 * P * (t + 1)].bitcast(FP4X4),
                        lhsT_scale=wa_scl[:, 0, P * t : P * (t + 1)],
                        rhs=x_cod[c][:].bitcast(FP8X4),
                        rhs_scale=x_scl[c][:],
                        start=True,
                        stop=True,
                    )

        def make_gates(c, at=None):
            gate[c] = place("gate%d" % c, [P, PACK, CHUNK], F32, at)
            for u in range(2):
                nc.scalar.activation(gate[c][:, 2 * u : 2 * u + 2, :], ya[c, u][:], SILU)

        def gather_words(c, at=None):
            got_w[c] = place("got_w%d" % c, [P, CHUNK], U32, at)
            entries = lst[:, c * CHUNK // GROUP : (c + 1) * CHUNK // GROUP]
            nc.vector.tensor_copy(got_w[c][:], tab_w[:].bitcast(U32).indirect(entries))

        def part_words(c, at=None):
            v_cod[c] = place("v_cod%d" % c, [P, 4 * CHUNK], U8, at)
            nc.vector.tensor_copy(
                v_cod[c][:].bitcast(U16).rearrange("p (d j) -> p d j", d=2),
                got_w[c][:].bitcast(U16).rearrange("p (j d) -> p d j", d=2),
            )

        def wd_views(u, n0, n1):
            return (
                wd_bf[u][:, n0 * PACK : n1 * PACK].rearrange("p (c i t) -> p c t i", i=2, t=PACK),
                wd_raw[:, :, u * CHUNK + n0 : u * CHUNK + n1].rearrange("p t (c i) -> p c t i", i=2),
            )

        def quantize_wd(u):
            nc.vector.quantize_mx(
                out=wd_cod[:, u * CHUNK : (u + 1) * CHUNK].bitcast(FP8X4),
                scales=wd_scl[:, u * CHUNK : (u + 1) * CHUNK],
                in_=wd_bf[u][:],
            )

        def memory_sums(s, number):
            c, u = divmod(s, 2)
            yb[s] = bank(number, "yb%d" % s, [P, PACK, STEP])
            for t in range(PACK):
                for a in range(2):
                    first = a * CHUNK + u * STEP
                    nc.tensor.matmul_mx(
                        out=yb[s][:, t, :],
                        lhsT=wb_cod[:, a, 2 * P * t : 2 * P * (t + 1)].bitcast(FP4X4),
                        lhsT_scale=wb_scl[:, a, P * t : P * (t + 1)],
                        rhs=v_cod[c][:, 2 * first : 2 * (first + STEP)].bitcast(FP4X4),
                        rhs_scale=v_scl[:, a, s * STEP : (s + 1) * STEP],
                        start=(a == 0),
                        stop=(a == 1),
                    )

        def join(s):
            c, u = divmod(s, 2)
            nc.vector.tensor_tensor(
                h_bf[s].rearrange("p (c i t) -> p c t i", i=2, t=PACK),
                yb[s][:].rearrange("p t (c i) -> p c t i", i=2),
                gate[c][:, :, u * STEP : (u + 1) * STEP].rearrange("p t (c i) -> p c t i", i=2),
                MULT,
            )

        def h_tile(s, steps, at=None):
            whole = place("h_bf%d" % s, [P, steps * STEP * PACK], BF16, at)
            for u in range(steps):
                h_bf[s + u] = whole[:, u * STEP * PACK : (u + 1) * STEP * PACK]
            return whole[:]

        def quantize_h(j0, j1, source, scales):
            nc.vector.quantize_mx(out=h_cod[:, j0:j1].bitcast(FP8X4), scales=scales, in_=source)

        def output_pass(target, m, j0, j1, scales):
            nc.tensor.matmul_mx(
                out=target,
                lhsT=wd_cod[:, P * m : P * (m + 1)].bitcast(FP8X4),
                lhsT_scale=wd_scl[:, P * m : P * (m + 1)],
                rhs=h_cod[:, j0:j1].bitcast(FP8X4),
                rhs_scale=scales,
                start=True,
                stop=True,
            )

        def output_sums(c, numbers, scales):
            for u in range(2):
                y[c, u] = bank(numbers[u], "y%d_%d" % (c, u), [P, 2, CHUNK])
                for m in range(2):
                    output_pass(y[c, u][:, m, :], 2 * u + m, c * CHUNK, (c + 1) * CHUNK, scales)

        def store_half(c, u, copy=nc.scalar.copy, at=None):
            store("y_sb%d_%d" % (c, u), y[c, u][:], out_rows[:, 2 * u : 2 * u + 2, c * CHUNK : (c + 1) * CHUNK], copy, at)

        def store(name, sums, rows, copy, at=None):
            y_sb = place(name, sums.shape, F32, at)
            copy(y_sb[:], sums)
            nc.sync.dma_start(rows, y_sb[:])

        turned = bank(6, "turned", [P, P])
        nc.tensor.transpose(turned[:], wgt_rows[:], ident[:])
        pieces = ((0, 2), (2, 4), (4, 8))
        for c0, c1 in pieces:
            nc.scalar.copy(
                wgt_cols[:, c0:c1, :].rearrange("p c (g r) -> p (c g) r", r=GROUP),
                turned[:, 8 * c0 : 8 * c1].unsqueeze(2).to_broadcast([P, 8 * (c1 - c0), GROUP]),
            )
        for number, (c0, c1) in enumerate(pieces):
            spread = bank(number, "spread%d" % number, [P, c1 - c0, P])
            for c in range(c0, c1):
                nc.tensor.transpose(spread[:, c - c0, :], wgt_cols[:, c, :], ident[:])
            nc.scalar.copy(wgt[:, c0 * P : c1 * P], spread[:].rearrange("p c j -> p (c j)"))

        for half in range(2):
            gather_x(0, half * HALF, (half + 1) * HALF)
        wbs_rows = sb_at("wbs_rows", [P, R], U8, 0)
        nc.scalar.copy(
            wbs_rows[0:32, :].bitcast(U32).rearrange("p (t b w) -> p t b w", t=PACK, w=2),
            wbs_raw[0:32, :].bitcast(U32).rearrange("p (b t w) -> p t b w", t=PACK, w=2),
        )
        for q in range(4):
            nc.scalar.dma_start(wb_scl[32 * q : 32 * q + 4, :, :].bitcast(I32), wbs_rows[8 * q : 8 * q + 8, :].bitcast(I32))
        wa_scl = sb_at("wa_scl", [P, 1, R], U8, R)
        order_columns(wa_scl, was_raw, 2)
        gather_x(1, 0, SPLIT)
        gather_x(1, SPLIT, J)
        for c in range(3):
            round_x(c, 0, 2)
        got_first = sb_at("got_first", [P, 2, CHUNK], F32, AT_FIRST)
        gather_x(2, 3 * CHUNK, J)
        round_x(3, 0, 3)
        gather_x(2, 0, CHUNK, got_first[:, 0, :])
        got_second = sb_at("got_second", [P, 2, CHUNK], F32, AT_WORDS)
        gather_x(2, CHUNK, 2 * CHUNK, got_second[:, 0, :])
        gather_x(2, 2 * CHUNK, 3 * CHUNK)
        gather_x(3, 0, CHUNK, got_first[:, 1, :])
        gather_x(3, CHUNK, 2 * CHUNK, got_second[:, 1, :])
        gather_x(3, 2 * CHUNK, 3 * CHUNK)
        order_columns(wa_cod, wa_raw, 4)
        round_x(0, 2, PACK, got_first[:])
        quantize_x(0)
        got_last = sb_at("got_last", [P, CHUNK], F32, AT_FIRST)
        gather_x(3, 3 * CHUNK, J, got_last[:])
        round_x(1, 2, PACK, got_second[:])
        round_x(2, 2, PACK)
        order_columns(wb_cod, wb_raw, 4)
        nc.gpsimd.tensor_scalar(
            x_bf[3][:].rearrange("p (n t) -> p n t", t=PACK)[:, :, PACK - 1], got_last[:], 1.0, 0.0, MULT, ADD
        )

        quantize_x(1)
        gate_sums(0, (0, 1))
        gate_sums(1, (2, 3))
        make_gates(0)
        make_gates(1)
        gather_words(0, AT_WORDS)
        gather_words(1, AT_WORDS + 1024)
        part_words(0)
        part_words(1)
        gather_words(2, AT_WORDS - 512)
        gather_words(3, AT_WORDS + 512)
        part_words(2)
        part_words(3)
        quantize_x(2, AT_SCALES)
        quantize_x(3, AT_SCALES + CHUNK)
        for s, number in ((0, 4), (3, 1), (1, 5), (2, 0)):
            memory_sums(s, number)
        gate_sums(2, (6, 7))
        gate_sums(3, (2, 3))
        wd_bf = [sb("wd_bf0", [P, CHUNK * PACK], BF16), sb_at("wd_bf1", [P, CHUNK * PACK], BF16, AT_WORDS + 1536)]
        nc.scalar.copy(*wd_views(0, 0, CHUNK))
        nc.gpsimd.tensor_scalar(
            wd_bf[1][:, (CHUNK - SHARE) * PACK :].rearrange("p (n t) -> p n t", t=PACK),
            wd_raw[:, :, N - SHARE :].rearrange("p t n -> p n t"),
            1.0,
            0.0,
            MULT,
            ADD,
        )
        staged = sb("staged", [P, STEP, PACK], F32)
        nc.scalar.copy(staged[:], yb[3][:].rearrange("p t n -> p n t"))
        nc.scalar.copy(*wd_views(1, 0, CHUNK - SHARE))
        h_first = h_tile(0, 2)
        h_second = h_tile(2, 2, AT_X3)
        nc.gpsimd.tensor_tensor(
            h_bf[3].rearrange("p (n t) -> p n t", t=PACK), staged[:], gate[1][:, :, STEP:].rearrange("p t n -> p n t"), MULT
        )
        for s in range(3):
            join(s)
        memory_sums(4, 1)
        memory_sums(5, 4)
        make_gates(2)
        make_gates(3)
        h_cod = sb_at("h_cod", [P, J], U32, AT_WD)
        first_scl = sb("first_scl", [P, CHUNK], U8)
        second_scl = sb("second_scl", [P, CHUNK], U8)
        quantize_wd(0)
        quantize_h(0, CHUNK, h_first, first_scl[:])
        quantize_wd(1)
        output_sums(0, (5, 0), first_scl[:])
        store_half(0, 0)
        store_half(0, 1)
        h_tile(4, 1, AT_WD + 4096)
        join(4)
        quantize_h(CHUNK, HALF, h_second, second_scl[:])
        output_sums(1, (6, 7), second_scl[:])
        memory_sums(6, 2)
        memory_sums(7, 3)
        store_half(1, 0)
        store_half(1, 1)
        third_scl = sb("third_scl", [P, CHUNK], U8)
        quantize_h(4 * STEP, 5 * STEP, h_bf[4], third_scl[:, 0:STEP])
        h_tile(5, 1, AT_X3)
        join(5)
        h_tile(6, 2)
        join(6)
        quantize_h(5 * STEP, 6 * STEP, h_bf[5], third_scl[:, STEP:])
        output_sums(2, (1, 4), third_scl[:])
        store_half(2, 0)
        store_half(2, 1)
        join(7)
        last_scl = sb("last_scl", [P, CHUNK], U8)
        for s in range(6, 8):
            quantize_h(s * STEP, (s + 1) * STEP, h_bf[s], last_scl[:, (s - 6) * STEP : (s - 5) * STEP])
        last = [bank(number, "y_last%d" % m, [P, CHUNK]) for m, number in enumerate((5, 0, 6, 7))]
        for u in range(2):
            for m in (0, 2, 1, 3):
                scales = last_scl[:, u * STEP : (u + 1) * STEP]
                output_pass(last[m][:, u * STEP : (u + 1) * STEP], m, (6 + u) * STEP, (7 + u) * STEP, scales)
        for m in (0, 2, 1, 3):
            copy = nc.scalar.copy if m < 2 else nc.vector.tensor_copy
            store("last_sb%d" % m, last[m][:], out_rows[:, m, 3 * CHUNK : J], copy)
